import numpy as np, ml_dtypes
CORES = [3,11,19,27,35,43,51,59]
N = 8
BF = ml_dtypes.bfloat16
W, P, L, SH, RO = 2048, 256, 32, 4, 3
def parts(rng):
    return (rng.integers(0, 256, (N, 8, 16, W)), rng.integers(0, W, (N, 8, 16, P)), rng.integers(0, W, (N, 8, 16, P)),
            rng.integers(500, 1300, (N, 8, 16)), rng.integers(30, 100, (N, 8, 16)))
def pack(x, r, m, t, e):
    return {"flood": np.ascontiguousarray(x.reshape(N, 128, W)).astype(np.float32).astype(BF), "riv": np.ascontiguousarray(r.reshape(N, 128, P)).astype(np.int32),
            "bord": np.ascontiguousarray(m.reshape(N, 128, P)).astype(np.int32), "th": t.reshape(N, 128, 1).astype(np.int32), "eps": e.reshape(N, 128, 1).astype(np.int32)}
def setup_inputs(rng):
    return pack(*parts(rng))
def setup_inputs_spread(rng):
    x = np.minimum((np.exp2(3 + 5.5 * rng.random((N, 8, 1, W))) * rng.random((N, 8, 16, W))).astype(np.int64), 255)
    r = (W * rng.random((N, 8, 16, P)) ** 3).astype(np.int64); m = W - 1 - (W * rng.random((N, 8, 16, P)) ** 3).astype(np.int64)
    t = np.minimum(np.exp2(7 + 5 * rng.random((N, 8, 16))).astype(np.int64), 4080); e = np.minimum(np.exp2(8 * rng.random((N, 8, 16))).astype(np.int64) - 1, 255)
    return pack(x, r, m, t, e)
def setup_inputs_ends(rng):
    x = 255 * rng.integers(0, 2, (N, 8, 16, W)); pure = 255 * rng.integers(0, 2, (N, 8, 1, W))
    kind = rng.random((N, 8)) < 0.4; kind[:, 7] = True
    x = np.where(kind[:, :, None, None], pure, x)
    k2 = (((W - 1) * (W - 1) >> SH) + 38 * (W - 1)) & (W - 1)
    x[:, 7, :, 0] = 0
    for c in (W - 1, W - 37, k2): x[:, 7, :, c] = 255
    r = (W - 1) * rng.integers(0, 2, (N, 8, 16, P)); m = (W - 1) * rng.integers(0, 2, (N, 8, 16, P))
    t = 4080 * rng.integers(0, 2, (N, 8, 16)); t[:, :, 2] = 0; t[:, :, 5] = 4080
    e = np.zeros((N, 8, 16), np.int64)
    for q in range(N):
        for g in range(8):
            n = int(rng.choice(np.array([0, 7, 8, 8, 9, 9, 16])))
            if g == 7: n = 8 + q % 2
            e[q, g, rng.permutation(16)[:n]] = 255
    for p in (1, 8, 15):
        r[:, 7, p] = np.where((np.arange(P) // L) % 2 == 0, W - 1, 0); m[:, 7, p] = W - 1; t[:, 7, p] = 4080
    for p in (0, 3, 14):
        r[:, 7, p] = W - 1; r[:, 7, p, P - 1] = 0; m[:, 7, p] = W - 1
    t[:, 7, 0] = 0; t[:, 7, 14] = 0
    r[:, 7, 10] = ((W - 1) * (np.arange(N) % 2))[:, None]; m[:, 7, 10] = W - 1; t[:, 7, 10] = 4080
    return pack(x, r, m, t, e)
def setup_inputs_corners(rng):
    x, r, m, t, e = parts(rng)
    r = np.argsort(rng.random((N, 8, 16, W)), axis=-1)[..., :P]; r = np.ascontiguousarray(r)
    kd = rng.integers(0, 7, (N, 8, 16)); kd[:, 0] = 6; kd[0::2, 3] = 0; kd[1::2, 3] = 6; kd[:, 7, 14] = 5; kd[:, 7, 15] = 2
    r[..., L] = np.where((kd == 1) | (kd == 3), r[..., 0], r[..., L])
    r[..., P - 1] = np.where((kd == 2) | (kd == 3), r[..., P - 1 - L], r[..., P - 1])
    m = np.where(rng.random((N, 8, 16, P)) < 0.3, r, m); e = np.zeros((N, 8, 16), np.int64)
    for q in range(N):
        for g in range(8):
            k = 8 if g in (0, 7) else int(rng.choice(np.array([7, 8, 8, 9]))); o = rng.permutation(16)
            x[q, g, o[:k]] = rng.integers(0, 256, (k, 1))
            n = max(0, 9 - k - int(rng.integers(0, 2))); e[q, g, o[k:k + n]] = 255
            v = x[q, g][:, r[q, g]]; s = np.min(np.add.reduce(np.abs(v[..., :P - L] - v[..., L:]), axis=0), axis=-1); c = kd[q, g]
            t[q, g] = np.where(c == 0, 0, np.where(c < 4, 1, np.where(c == 4, s, np.where(c == 5, np.minimum(s + 1, 4080), 4080))))
    return pack(x, r, m, t, e)
def setup_inputs_ties(rng):
    x = rng.integers(0, 4, (N, 8, 16, W)); r, m = rng.integers(0, W, (2, N, 8, 16, P))
    w = rng.integers(0, W, (N, 4, 1, 12)); w[..., 0] = 0; w[..., 11] = W - 1
    r[:, 1::2] = np.take_along_axis(np.broadcast_to(w, (N, 4, 16, 12)), rng.integers(0, 12, (N, 4, 16, P)), -1)
    m[:, ::2] = np.where(rng.random((N, 4, 16, P)) < 0.5, r[:, ::2], m[:, ::2])
    return pack(x, r, m, rng.integers(0, 18, (N, 8, 16)), rng.integers(0, 3, (N, 8, 16)))
def setup_inputs_far(rng):
    k = W // 16; n = W - 2 * k; pos = np.argsort(rng.random((N, 8, W)), axis=-1); o = np.argsort(pos, axis=-1)
    share = np.where(np.arange(8) % 2 == 0, 0.5, rng.choice(np.array([0.2, 0.8]), (N, 8)))
    hn = (share * n).astype(np.int64)[..., None]; high = (pos >= k) & (pos < 2 * k + hn)
    x = np.where((pos < 2 * k)[:, :, None], 0, rng.integers(0, 8, (N, 8, 16, W))); x = np.where(high[:, :, None], 255 - x, x)
    c = rng.integers(0, 2, (N, 8, 16, P)); c[:, :, ::2] = (np.arange(P) // L + rng.integers(0, 2, (N, 8, 8, 1))) % 2; c[:, :, 1::4, P - 1] = 0
    u = rng.random((N, 8, 16, P)); hn = hn[..., None]; odd = (np.arange(16) % 2 == 1)[:, None]
    mixed = np.where(c == 1, 2 * k + (u * hn).astype(np.int64), 2 * k + hn + (u * (n - hn)).astype(np.int64))
    i = np.where(odd, c * k + (u * k).astype(np.int64), mixed)
    r = np.take_along_axis(o, i.reshape(N, 8, -1), -1).reshape(N, 8, 16, P)
    i = (1 - c) * k + rng.integers(0, k, (N, 8, 16, P)); far = np.take_along_axis(o, i.reshape(N, 8, -1), -1).reshape(N, 8, 16, P)
    m = np.where(odd & (rng.random((N, 8, 16, P)) < 0.25), far, rng.integers(0, W, (N, 8, 16, P))); m[:, :, 1::4, P - 1] = far[:, :, 1::4, P - 1]
    t = rng.integers(3925, 3976, (N, 8, 16)); t[:, :, ::4] = 3929 + 4 * rng.integers(0, 12, (N, 8, 4)); t[:, :, 1::4] = 0; t[:, :, 3::4] = rng.integers(3900, 4080, (N, 8, 4))
    e = np.where(np.argsort(rng.random((N, 8, 16)), axis=-1) < 12, 254, rng.integers(247, 255, (N, 8, 16)))
    return pack(x, r, m, t, e)
def check_inputs(d):
    bad = []
    for k, lo, hi in (("flood", 0, 255), ("riv", 0, W - 1), ("bord", 0, W - 1), ("th", 0, 4080), ("eps", 0, 255)):
        v = np.asarray(d[k]).astype(np.float64)
        if not (np.all(v >= lo) and np.all(v <= hi)): bad.append("range of " + k)
        elif not np.all(v == np.floor(v)): bad.append("whole numbers in " + k)
    return bad
def columns(x, names):
    return np.take(x, names + W * np.arange(8)[:, None, None], axis=0)
def total(v):
    return np.add.reduce(v, axis=-1, dtype=np.int16)
def reference(flood, riv, bord, th, eps):
    R = riv.astype(np.int64).reshape(N, 8, 16, P); M = bord.astype(np.int64).reshape(N, 8, 16, P); A = np.zeros((N, 8, 16), np.int64)
    T = th.astype(np.int64).reshape(N, 8, 16); E = eps.astype(np.int16).reshape(N, 8, 1, 1, 16)
    X = [np.ascontiguousarray(a.astype(np.float32).astype(np.int16).reshape(8, 16, W).transpose(0, 2, 1)).reshape(8 * W, 16) for a in flood]
    place = np.arange(P)
    for t in range(RO):
        first = np.zeros((N, 8, 16), np.int64); loops = np.zeros((N, 8, 16, L), np.int64)
        for q in range(N):
            r, m = R[q], M[q]; h = r[..., :P - 1]; x = columns(X[q], r); nxt = x[:, :, 1:]; now = np.abs(x[:, :, :P - 1] - nxt)
            before = np.concatenate([r[..., :1], r[..., :P - 2]], axis=-1)
            cand = np.stack([((h * a >> SH) + 37 * h + a + 77 * t) & (W - 1) for a in (before, r[..., 1:], m[..., :P - 1], m[..., 1:])] + [m[..., :P - 1]])
            score = np.stack([total(np.abs(columns(X[q], c) - nxt)) for c in cand])
            best = np.take_along_axis(cand, np.argmin(score, axis=0)[None], 0)[0]
            near = total((np.abs(columns(X[q], best) - nxt) < now).astype(np.int16))
            R[q, :, :, :P - 1] = np.where(near >= 9, best, h)
            x = columns(X[q], R[q]); ok = total(np.abs(x[:, :, :P - L] - x[:, :, L:])) < (T[q] + 16 * A[q])[..., None]
            first[q] = np.where(np.any(ok, axis=-1), np.argmax(ok, axis=-1), P)
            loops[q] = np.take_along_axis(R[q], np.minimum(first[q] + 1, P - L)[..., None] + np.arange(L), -1)
        for q in range(N):
            src = (q - 1 - t % (N - 1)) % N
            lp = np.where((first[src] < P)[..., None], loops[src], loops[q])
            R[q] = np.take_along_axis(np.concatenate([R[q], lp], axis=-1), place + L * (place > first[q][..., None]), -1)
            A[q] = A[q] + (first[q] < P)
            near = total((np.abs(columns(X[q], R[q]) - columns(X[q], M[q])) <= E[q]).astype(np.int16))
            M[q] = np.where(near >= 9, R[q], M[q])
    return {"yr": R.reshape(N, 128, P).astype(np.float32), "ym": M.reshape(N, 128, P).astype(np.float32), "ya": A.reshape(N, 128, 1).astype(np.float32)}

@@ -1,0 +1,599 @@
+import numpy as np
+from concourse.mybir import dt, AluOpType, AxisListType, ActivationFunctionType
+
+OP = AluOpType
+N, W, P, L, ROUNDS = 8, 2048, 256, 32, 3
+CK = 64
+FW = 1616
+CE = 16 * CK
+BANK = 512
+
+_F, _B, _I, _U = "float32", "bfloat16", "int32", "uint16"
+SCRATCH = {
+    "fl": ("sbuf", [128, 2 * W], _B),
+    "xm": ("sbuf", [128, 4096], _B), "xp": ("sbuf", [128, 4096], _B),
+    "ones": ("sbuf", [128, 128], _B), "ident": ("sbuf", [128, 128], _B), "nident": ("sbuf", [128, 128], _B),
+    "g8": ("sbuf", [128, 8], _B), "g8b": ("sbuf", [128, 8], _B),
+    "b1": ("sbuf", [128, 144], _B), "b4096": ("sbuf", [128, 144], _B),
+    "b8192": ("sbuf", [128, 144], _B), "b16384": ("sbuf", [128, 144], _B),
+    "ck": ("sbuf", [128, 320], _B), "cy": ("sbuf", [128, 192], _B), "cz": ("sbuf", [128, 128], _B),
+    "iot": ("sbuf", [128, 256], _F), "i16": ("sbuf", [128, 64], _I), "ipt": ("sbuf", [128, 64], _I),
+    "ip2": ("sbuf", [128, 64], _I), "cpos": ("sbuf", [128, 64], _F),
+    "dgi": ("sbuf", [128, 512], _I), "dgj": ("sbuf", [128, 512], _I), "diag": ("sbuf", [128, 512], _F), "seg": ("sbuf", [128, 512], _F),
+    "thi": ("sbuf", [128, 1], _I), "epi": ("sbuf", [128, 1], _I), "epf": ("sbuf", [128, 2], _F),
+    "tha": ("sbuf", [128, 8], _F), "nk": ("sbuf", [128, 64], _F), "aout": ("sbuf", [128, 4], _F),
+    "ru0": ("sbuf", [128, 256], _U), "lu": ("sbuf", [128, 32], _U),
+    "lg": ("sbuf", [128, 512], _F), "ls": ("sbuf", [128, 512], _F),
+    "l1": ("sbuf", [128, 32], _F), "lm": ("sbuf", [128, 32], _F), "lo": ("sbuf", [128, 32], _F), "l2": ("sbuf", [128, 32], _F),
+    "yrf": ("sbuf", [128, 256], _F), "ymf": ("sbuf", [128, 256], _F),
+    "pv": ("psum", [128, 512], _F), "sc0": ("psum", [128, 512], _F), "sc1": ("psum", [128, 512], _F),
+    "cnt": ("psum", [128, 512], _F), "sub0": ("psum", [128, 1024], _F), "sub1": ("psum", [128, 1024], _F),
+}
+for _k in range(3):
+    SCRATCH["lout%d" % _k] = ("sbuf", [128, 32], _F)
+    SCRATCH["land%d" % _k] = ("sbuf", [128, 32], _F)
+for _k in range(2):
+    for _n, _c, _d in (("rn", 264, _I), ("rf", 264, _F), ("mn", 264, _I), ("mf", 264, _F), ("rp", 296, _I),
+                       ("rpu", 256, _U), ("r2u", 256, _U), ("mu", 256, _U), ("xr", 4112, _B),
+                       ("me", 64, _F), ("pr", 256, _I), ("v", 256, _I), ("u", 256, _U), ("xd", 4096, _B), ("win", 5120, _B),
+                       ("now", 1024, _B), ("nb", 1024, _B), ("kb", 128, _F), ("kc", 128, _F), ("k4", 64, _I), ("ka", 64, _I),
+                       ("kv", 64, _I), ("w", 64, _F), ("o", 64, _F), ("ou", 64, _U), ("d", 64, _F), ("rr", 64, _I),
+                       ("a2", 1024, _B), ("nf", 64, _F), ("q", 64, _F), ("df", 64, _F), ("a3", 1024, _B), ("c3", 1024, _B), ("mm", 64, _I)):
+        SCRATCH[_n + "_%d" % _k] = ("sbuf", [128, _c], _d)
+NDMA = 16
+SEMAPHORES = ["sV", "sS", "sP", "sG", "ls", "arr0", "arr1", "arr2"] + ["d%d" % k for k in range(NDMA)]
+
+CY = 0.000833
+GA = 1.47
+PEC = 0.00053
+WAKE = 0.069
+BONUS = {"nearer": 4.0, "loop": -3.2, "score": -7.1, "nk-": -5.2, "now||": -1.0, "cnt3": 5.2, "XM'": -0.3, "ac||": 0.1, "now-": 0.9,
+         "nk||": 3.4, "ac-": -2.2, "df": -0.6, "c5||": 0.9, "c3": -0.3, "rf": 5.4, "cand||": 0.1, "u": 2.1, "XR'": -1.2, "me": -0.8,
+         "cand": 1.0, "c5-": -1.6, "v": -1.8, "dist": -0.1, "kmin": 3.7}
+VIAS = (0, 1, 2, 3)
+VW = 128
+NET = 5.5
+XMV = "SSSSSSSSSS"
+TAIL = 4 * ROUNDS - 1
+FIRST = ((0, 66, "S"), (66, 130, "V"), (130, 194, "S"), (194, 256, "S"))
+
+
+def _span(r):
+    return r[0], r[1], r[2]
+
+
+def _ap(T, r):
+    if len(r) == 4:
+        return T[r[0]][:, r[1]:r[2]:r[3]]
+    return T[r[0]][:, r[1]:r[2]]
+
+
+def _count(r):
+    return (r[2] - r[1] + (r[3] - 1 if len(r) == 4 else 0)) // (r[3] if len(r) == 4 else 1)
+
+
+def _psum(name):
+    return SCRATCH[name][0] == "psum" if name in SCRATCH else False
+
+
+def design():
+    ops = []
+
+    def op(eng, f, rd, wr, dur, lat=WAKE, name="", **kw):
+        o = {"eng": eng, "f": f, "rd": [_span(r) for r in rd], "wr": [_span(r) for r in wr], "dur": dur, "lat": lat, "name": name}
+        o.update(kw)
+        ops.append(o)
+
+    def tt(out, a, b, alu, name="tt"):
+        c = 1 if (_psum(a[0]) or _psum(b[0])) else 2
+        op("V", lambda q, T: q.tensor_tensor(_ap(T, out), _ap(T, a), _ap(T, b), alu), [a, b], [out],
+           0.02 + CY * max(64, c * _count(out)), name=name)
+
+    def ts(out, a, s1, s2, op0, op1=None, name="ts"):
+        aps = [s for s in (s1, s2) if isinstance(s, tuple)]
+        two = all(SCRATCH[r[0]][2] in (_B, _U) for r in (out, a))
+
+        def f(q, T):
+            x1 = _ap(T, s1) if isinstance(s1, tuple) else s1
+            x2 = _ap(T, s2) if isinstance(s2, tuple) else s2
+            if op1 is None:
+                return q.tensor_scalar(_ap(T, out), _ap(T, a), x1, None, op0)
+            return q.tensor_scalar(_ap(T, out), _ap(T, a), x1, x2, op0, op1)
+        op("V", f, [a] + aps, [out], 0.02 + CY * max(64, (0.5 if two else 1) * _count(out)), name=name)
+
+    def copy(out, a, name="copy"):
+        op("V", lambda q, T: q.tensor_copy(_ap(T, out), _ap(T, a)), [a], [out], 0.02 + CY * max(64, _count(out)), name=name)
+
+    def memset(buf, lo, hi, val, p0=0, p1=128):
+        op("V", lambda q, T: q.memset(T[buf][p0:p1, lo:hi], val), [], [(buf, lo, hi)], 0.02 + CY * max(64, 0.5 * (hi - lo)), name="memset")
+
+    def gtt(out, win, off, b, alu, name):
+        op("V", lambda q, T: q.tensor_tensor(_ap(T, out), _ap(T, win).indirect(_ap(T, off)), _ap(T, b), alu), [win, off, b], [out],
+           0.05 + CY * GA * _count(out), name=name)
+
+    def gather(out, win, off, name, eng="S"):
+        def f(q, T, e):
+            if e == "V":
+                return q.tensor_copy(_ap(T, out), _ap(T, win).indirect(_ap(T, off)))
+            return q.activation(_ap(T, out), _ap(T, win).indirect(_ap(T, off)), ActivationFunctionType.Copy)
+        op(eng, f, [win, off], [out], 0.06 + CY * GA * _count(out), name=name, flex=True)
+
+    def absS(out, a, name):
+        op("S", lambda q, T: q.activation(_ap(T, out), _ap(T, a), ActivationFunctionType.Abs), [a], [out],
+           0.1 + CY * _count(out), name=name)
+
+    def sub(out, a, b, name):
+        def f(q, T):
+            n = out[2] - out[1]
+            for s in range(0, n, BANK):
+                e = min(n, s + BANK)
+                q.matmul(T[out[0]][:, out[1] + s:out[1] + e], T["ident"][:], T[a[0]][:, a[1] + s:a[1] + e], True, False)
+                i = q.matmul(T[out[0]][:, out[1] + s:out[1] + e], T["nident"][:], T[b[0]][:, b[1] + s:b[1] + e], False, True)
+            return i
+        op("P", f, [a, b, ("ident", 0, 128), ("nident", 0, 128)], [out], PEC * 2 * _count(out), name=name)
+
+    def total(out, a, wb, const, name, *more):
+        def f(q, T):
+            o = _ap(T, out)
+            if const is not None:
+                q.matmul(o, T["ones"][:], T[const[0]][:, const[1]:const[1] + out[2] - out[1]], True, False)
+            todo = [(x, p) for x in (a,) + more for p in range(16)]
+            for n, (x, p) in enumerate(todo):
+                i = q.matmul(o, T[wb][:, 15 - p:143 - p], T[x[0]][:, x[1] + p:x[2]:16], const is None and n == 0, n == len(todo) - 1)
+            return i
+        op("P", f, [a, (wb, 0, 144), ("ones", 0, 128)] + list(more) + ([(const[0], const[1], const[1] + 64)] if const else []), [out],
+           PEC * 64 * (16 * (1 + len(more)) + (1 if const else 0)), name=name)
+
+    nd = [0]
+
+    def dma(q, fo, fi, rd, wr, name, nbytes=0):
+        k = nd[0]
+        nd[0] += 1
+        op(q, lambda e, T: e.dma_start(fo(T), fi(T)), rd, wr, 0.06, lat=2.0 + nbytes / 200e3, name=name, dma="d%d" % k)
+
+    dma("S", lambda T: T.fl[:, 0:W], lambda T: T.flood[:], [], [("fl", 0, W)], "ld flood", 524288)
+    dma("Y", lambda T: T["rn_0"][:, 0:P], lambda T: T.riv[:], [], [("rn_0", 0, P)], "ld riv", 131072)
+    dma("Y", lambda T: T["mn_0"][:, 0:P], lambda T: T.bord[:], [], [("mn_0", 0, P)], "ld bord", 131072)
+    dma("Y", lambda T: T.thi[:], lambda T: T.th[:], [], [("thi", 0, 1)], "ld th")
+    dma("Y", lambda T: T.epi[:], lambda T: T.eps[:], [], [("epi", 0, 1)], "ld eps")
+    dma("S", lambda T: T.fl[:, W:W + FW], lambda T: T.flood[:, 0:FW], [], [("fl", W, W + FW)], "ld flood2", 414000)
+    iota = lambda out, pat, base, cm, dtype=_I: op(
+        "G", lambda q, T: q.iota(_ap(T, out), pat, base, cm, allow_small_or_imprecise_dtypes=True) if dtype == _F else q.iota(_ap(T, out), pat, base, cm),
+        [], [out], 0.13 + 2 * CY * _count(out), name="iota")
+
+    def asel(out, a, pat, cmp, base, cm):
+        op("G", lambda q, T: q.affine_select(_ap(T, out), _ap(T, a), pat, cmp, 0.0, base, cm), [a], [out], 0.17 + 2 * CY * _count(out), name="asel")
+
+    memset("ones", 0, 128, 1.0)
+    iota(("ipt", 0, 64), [[0, 64]], 0, 1)
+    iota(("i16", 0, 64), [[16, 64]], 0, 0)
+    asel(("ident", 0, 128), ("ones", 0, 128), [[-1, 128]], OP.is_equal, 0, 1)
+    asel(("g8", 0, 8), ("ones", 0, 8), [[-16, 8]], OP.is_ge, 0, 1)
+    asel(("g8b", 0, 8), ("g8", 0, 8), [[16, 8]], OP.is_ge, 15, -1)
+    iota(("iot", 0, 256), [[1, 256]], 0, 0, _F)
+    iota(("dgi", 0, 512), [[0, 32], [1, 16]], 0, -1)
+    iota(("dgj", 0, 512), [[0, 32], [1, 16]], 0, 0)
+    ts(("nident", 0, 128), ("ident", 0, 128), -1.0, None, OP.mult)
+    memset("b1", 0, 144, 0.0)
+    copy(("b1", 15, 143, 16), ("g8b", 0, 8))
+    for w in (8192, 16384, 4096):
+        ts(("b%d" % w, 0, 144), ("b1", 0, 144), float(w), None, OP.mult)
+    memset("ck", 0, 320, -262144.0, 0, 64)
+    for m in range(4):
+        memset("ck", 64 * m, 64 * m + 64, 32.0 * m, 64, 128)
+    memset("ck", 256, 320, 128.0, 64, 128)
+    cons = [(77 * t - 592) % W for t in range(ROUNDS)]
+    memset("cy", 0, 192, -2176.0, 0, 64)
+    for t in range(ROUNDS):
+        x = cons[t] / 32.0
+        hi = int(x * 4) / 4.0
+        memset("cy", 64 * t, 64 * t + 64, hi, 64, 96)
+        memset("cy", 64 * t, 64 * t + 64, x - hi, 96, 128)
+    memset("cz", 0, 64, -544.0, 0, 64)
+    memset("cz", 64, 128, -1568.0, 0, 64)
+    memset("cz", 0, 128, 0.0, 64, 128)
+    ts(("ip2", 0, 64), ("ipt", 0, 64), 15, None, OP.bitwise_and)
+    tt(("cpos", 0, 64), ("ip2", 0, 64), ("i16", 0, 64), OP.add)
+    POS, IOT = ("pv", 0, 64), ("pv", 64, 128)
+    copy(POS, ("cpos", 0, 64))
+    copy(IOT, ("iot", 0, 64))
+    ts(("cpos", 0, 64), ("cpos", 0, 64), 4096.0, None, OP.add)
+    ts(("dgi", 0, 512), ("dgi", 0, 512), 15, None, OP.bitwise_and)
+    ts(("diag", 0, 512), ("dgi", 0, 512), 0.0, None, OP.is_equal)
+    ts(("seg", 0, 512), ("dgj", 0, 512), 0.0, None, OP.is_gt)
+    copy(("tha", 0, 1), ("thi", 0, 1))
+    copy(("epf", 0, 1), ("epi", 0, 1))
+    ts(("epf", 1, 2), ("epi", 0, 1), -1.0, None, OP.mult)
+    for k in range(2):
+        memset("rf_%d" % k, 257, 264, 592.0)
+        memset("mf_%d" % k, 256, 264, 592.0)
+        memset("rp_%d" % k, 256, 296, -4096)
+        memset("xr_%d" % k, 4096, 4112, 0.0)
+
+    FL = ("fl", 0, W)
+    FL2 = ("fl", 0, W + FW)
+    for lo, hi, e in FIRST:
+        copy(("ru0", lo, hi), ("rn_0", lo, hi), "R u16")
+        gather(("xr_0", 16 * lo, 16 * hi), FL, ("ru0", lo, hi), "XR0", e)
+    ts(("rf_0", 1, 257), ("rn_0", 0, 256), 592.0, None, OP.add)
+    copy(("rf_0", 0, 1), ("rf_0", 1, 2))
+    ts(("mf_0", 0, 256), ("mn_0", 0, 256), 592.0, None, OP.add)
+    for lo, hi in ((0, 64), (64, 128), (128, 192), (192, 256)):
+        copy(("mu_0", lo, hi), ("mn_0", lo, hi), "M u16")
+        gather(("xm", 16 * lo, 16 * hi), FL, ("mu_0", lo, hi), "XM0")
+
+    nkc = [0]
+
+    def nkcol():
+        c = nkc[0]
+        nkc[0] += 1
+        return ("nk", c, c + 1)
+    neck = {}
+
+    def halves(lo, hi, yes):
+        if not yes or hi - lo <= 32:
+            return [(lo, hi)]
+        m = (lo + hi) // 2
+        return [(lo, m), (m, hi)]
+
+    def step1(t, k):
+        s = (4 * t + k) % 2
+        z = t % 2
+        b = lambda n: n + "_%d" % s
+        c0 = CK * k
+        rn, rf, mn, mf = "rn_%d" % z, "rf_%d" % z, "mn_%d" % z, "mf_%d" % z
+        xr = "xr_%d" % z
+        R16, K12, M5, UU = ("pv", 128, 192), ("pv", 192, 320), ("pv", 320, 384), ("pv", 384, 448)
+        T5, ZZ, K2 = ("pv", 192, 256), ("pv", 256, 320), ("pv", 256, 320)
+        xn = (xr, 16 * (c0 + 1), 16 * (c0 + 65))
+        sc = "sc%d" % s
+        ts(R16, (rn, c0, c0 + 64), 16.0, None, OP.add, name="R16")
+        for m, (bf, o) in enumerate(((rf, c0), (rf, c0 + 2), (mf, c0), (mf, c0 + 1))):
+            tt((b("pr"), 64 * m, 64 * m + 64), R16, (bf, o, o + 64), OP.mult, name="prod")
+        for h in range(0, 256, VW):
+            ts((b("v"), h, h + VW), (b("pr"), h, h + VW), 4, W - 1, OP.arith_shift_right, OP.bitwise_and, name="v")
+            ts((b("u"), h, h + VW), (b("v"), h, h + VW), float(cons[t]), None, OP.add, name="u")
+        sub(("sub0", 0, CE), (xr, 16 * c0, 16 * (c0 + 64)), xn, "now-")
+        absS((b("now"), 0, CE), ("sub0", 0, CE), "now||")
+        sub(("sub0", 0, CE), ("xm", 16 * c0, 16 * (c0 + 64)), xn, "c5-")
+        absS((b("win"), 4 * CE, 5 * CE), ("sub0", 0, CE), "c5||")
+        for m in range(4):
+            gtt((b("xd"), CE * m, CE * m + CE), FL2, (b("u"), 64 * m, 64 * m + 64), xn, OP.subtract, "cand")
+            absS((b("win"), CE * m, CE * m + CE), (b("xd"), CE * m, CE * m + CE), "cand||")
+        for m in (4, 0, 1, 2, 3):
+            total((sc, 64 * m, 64 * m + 64), (b("win"), CE * m, CE * m + CE), "b8192", ("ck", 64 * m), "score")
+        tt(K12, (sc, 0, 128), (b("v"), 0, 128), OP.add, "key")
+        tt((b("kb"), 0, 128), (sc, 128, 256), (b("v"), 128, 256), OP.add, "key")
+        tt((b("kc"), 0, 64), ("pv", 192, 256), (b("kb"), 0, 64), OP.min, "kmin")
+        tt(K2, K2, (b("kb"), 64, 128), OP.min, "kmin")
+        tt((b("k4"), 0, 64), K2, (b("kc"), 0, 64), OP.min, "kmin")
+        tt(M5, (sc, 256, 320), (b("k4"), 0, 64), OP.is_le, "m5")
+        ts((b("ka"), 0, 64), (b("k4"), 0, 64), 6144, 1, OP.bitwise_and, OP.arith_shift_right, name="ka")
+        tt(UU, M5, ("cpos", 0, 64), OP.mult, "uu")
+        tt((b("w"), 0, 64), POS, (b("ka"), 0, 64), OP.add, "w")
+        tt((b("o"), 0, 64), UU, (b("w"), 0, 64), OP.max, "o")
+        copy((b("ou"), 0, 64), (b("o"), 0, 64), "ou")
+        gtt((b("nb"), 0, CE), (b("win"), 0, 5 * CE), (b("ou"), 0, 64), (b("now"), 0, CE), OP.is_lt, "nearer")
+        ts((b("kv"), 0, 64), (b("k4"), 0, 64), W - 1, None, OP.bitwise_and, name="kv")
+        ts((b("me"), 0, 64), (mn, c0, c0 + 64), 4096.0 - cons[t], None, OP.add, name="me")
+        tt(T5, M5, (b("me"), 0, 64), OP.mult, "t5")
+        tt((b("d"), 0, 64), T5, (b("kv"), 0, 64), OP.max, "d")
+        total((sc, 320, 384), (b("nb"), 0, CE), "b16384", ("cy", 64 * t), "cnt1")
+        tt(ZZ, (sc, 320, 384), (b("d"), 0, 64), OP.add, "z")
+        tt((b("rr"), 0, 64), ZZ, (rn, c0, c0 + 64), OP.max, "rr")
+        rp, rpu = "rp_%d" % z, "rpu_%d" % z
+        e = 63 if k == 3 else 64
+        ts((rp, c0, c0 + e), (b("rr"), 0, e), W - 1, None, OP.bitwise_and, name="R'")
+        if k == 3:
+            copy((rp, 255, 256), (rn, 255, 256), "R'255")
+        copy((rpu, c0, c0 + 64), (rp, c0, c0 + 64), "R'u")
+        for a, c in halves(c0, c0 + 64, 4 * t + k >= TAIL):
+            gather(("xp", 16 * a, 16 * c), FL, (rpu, a, c), "XR'", "VS" if 4 * t + k >= TAIL else "S")
+
+    def necks(t, k):
+        s = (4 * t + k) % 2
+        b = lambda n: n + "_%d" % s
+        lo, hi = max(0, 64 * k - 32), 64 * k + 32
+        n = hi - lo
+        for a, c in halves(lo, hi, 4 * t + k >= TAIL):
+            h0, h1 = 16 * (a - lo), 16 * (c - lo)
+            sub(("sub1", h0, h1), ("xp", 16 * a, 16 * c), ("xp", 16 * (a + 32), 16 * (c + 32)), "nk-")
+            absS((b("a2"), h0, h1), ("sub1", h0, h1), "nk||")
+        total(("cnt", 0, n), (b("a2"), 0, 16 * n), "b1", None, "dist")
+        ts((b("nf"), 0, n), ("cnt", 0, n), ("tha", t, t + 1), 256.0, OP.is_ge, OP.mult, name="nf")
+        tt((b("q"), 0, n), ("pv", 64, 64 + n), (b("nf"), 0, n), OP.add, "q")
+        m = nkcol()
+        qq = (b("q"), 0, n)
+        op("V", lambda e, T: e.tensor_reduce(_ap(T, m), _ap(T, qq), AxisListType.X, OP.min), [qq], [m], 0.02 + CY * 64, name="red")
+        m2 = nkcol()
+        ts(m2, m, float(lo), neck[t, k - 1] if k else 256.0, OP.add, OP.min, name="nk")
+        neck[t, k] = m2
+
+    def loops(t):
+        z = t % 2
+        nk = neck[t, 3]
+        lout = "lout%d" % t
+        ts(("lu", 0, 32), ("iot", 0, 32), nk, 1.0, OP.add, OP.add, name="lu")
+        gtt(("lg", 0, 512), ("rp_%d" % z, 0, 296), ("lu", 0, 32), ("diag", 0, 512), OP.mult, "loop")
+        op("V", lambda e, T: e.tensor_tensor_scan(T.ls[:], T.seg[:], T.lg[:], 0.0, OP.mult, OP.add), [("seg", 0, 512), ("lg", 0, 512)], [("ls", 0, 512)],
+           0.02 + CY * 512, name="scan")
+        copy((lout, 0, 32), ("ls", 15, 512, 16), "lout")
+        op("G", None, [(lout, 0, 32)], [], 1.0, name="send", send=t)
+        op("N", None, [(lout, 0, 32)], [("land%d" % t, 0, 32)], 0.0, lat=NET, name="recv", recv=t)
+        ts(("tha", 4 + t, 5 + t), nk, 256.0, 16.0, OP.is_lt, OP.mult, name="A")
+        tt(("tha", t + 1, t + 2), ("tha", t, t + 1), ("tha", 4 + t, 5 + t), OP.add, "A")
+
+    def landed(t):
+        rp, lout = ("rp_%d" % (t % 2), 224, 256), ("lout%d" % t, 0, 32)
+        ts(("lm", 0, 32), ("iot", 224, 256), neck[t, 3], None, OP.is_gt, name="l0")
+        tt(("lo", 0, 32), lout, rp, OP.subtract, "l0")
+        tt(("lo", 0, 32), ("lo", 0, 32), ("lm", 0, 32), OP.mult, "l0")
+        tt(("lo", 0, 32), ("lo", 0, 32), rp, OP.add, "l0")
+        ts(("lm", 0, 32), ("lm", 0, 32), 1.0, 8192.0, OP.subtract, OP.mult, name="l0")
+        tt(("l1", 0, 32), ("land%d" % t, 0, 32), ("lm", 0, 32), OP.add, "l1")
+        ts(("l2", 0, 32), ("l1", 0, 32), 0.0, -8192.0, OP.is_ge, OP.mult, name="l1")
+        tt(("l2", 0, 32), ("l2", 0, 32), ("lo", 0, 32), OP.add, "l2")
+
+    def moved(t, k):
+        s = (4 * t + k) % 2
+        b = lambda n: n + "_%d" % s
+        z, y = t % 2, (t + 1) % 2
+        last = t == ROUNDS - 1
+        cn, c0 = ("sc0", 0) if last and k < 4 else ("cnt", 64)
+        lo, hi = (max(0, 64 * k - 32), 64 * k + 32) if k < 4 else (224, 256)
+        n = hi - lo
+        rp = "rp_%d" % z
+        rn = ("yrf", lo, hi) if last else ("rn_%d" % y, lo, hi)
+        MK = ("pv", 448, 448 + n)
+        if k < 4:
+            tt((b("df"), 0, n), (rp, lo + 32, hi + 32), (rp, lo, hi), OP.subtract, "df")
+            ts(MK, ("iot", lo, hi), neck[t, k], None, OP.is_gt, name="mk")
+            tt(MK, MK, (b("df"), 0, n), OP.mult, "dm")
+            tt(rn, MK, (rp, lo, hi), OP.add, "R''")
+        else:
+            tt(rn, ("l2", 0, 32), ("l1", 0, 32), OP.max, "R''")
+        u = ("r2u_%d" % z, lo, hi)
+        copy(u, rn, "R''u")
+        if last and k in VIAS:
+            x = ("xr_%d" % y, 16 * lo, 16 * hi)
+            gather(x, FL, u, "XR''")
+            sub(("sub0", 0, 16 * n), x, ("xm", 16 * lo, 16 * hi), "ac-")
+            absS((b("a3"), 0, 16 * n), ("sub0", 0, 16 * n), "ac||")
+            ts((b("c3"), 0, 16 * n), (b("a3"), 0, 16 * n), ("epf", 0, 1), None, OP.is_le, name="c3")
+            total((cn, c0, c0 + n), (b("c3"), 0, 16 * n), "b4096", ("cz", 0), "cnt3")
+        elif last:
+            x3, c3, c4 = (b("a3"), 0, 16 * n), (b("c3"), 0, 16 * n), (b("nb"), 0, 16 * n)
+            gtt(x3, FL, u, ("xm", 16 * lo, 16 * hi), OP.subtract, "cand")
+            ts(c3, x3, ("epf", 0, 1), None, OP.is_le, name="c3")
+            ts(c4, x3, ("epf", 1, 2), None, OP.is_ge, name="c3")
+            total((cn, c0, c0 + n), c3, "b4096", ("cz", 64), "cnt3", c4)
+        else:
+            gather(("xr_%d" % y, 16 * lo, 16 * hi), FL, u, "XR''")
+        if not last:
+            rf = "rf_%d" % y
+            ts((rf, lo + 1, hi + 1), rn, 592.0, None, OP.add, name="rf")
+            if k == 0:
+                copy((rf, 0, 1), (rf, 1, 2), "rf0")
+            sub(("sub1", 0, 16 * n), ("xr_%d" % y, 16 * lo, 16 * hi), ("xm", 16 * lo, 16 * hi), "ac-")
+            absS((b("a3"), 0, 16 * n), ("sub1", 0, 16 * n), "ac||")
+            ts((b("c3"), 0, 16 * n), (b("a3"), 0, 16 * n), ("epf", 0, 1), None, OP.is_le, name="c3")
+            total((cn, c0, c0 + n), (b("c3"), 0, 16 * n), "b4096", ("cz", 0), "cnt3")
+        Z3 = ("pv", 448, 448 + n)
+        tt(Z3, (cn, c0, c0 + n), rn, OP.add, "z3")
+        tt((b("mm"), 0, n), Z3, ("mn_%d" % z, lo, hi), OP.max, "mm")
+        mn = ("mn_%d" % y, lo, hi)
+        ts(mn, (b("mm"), 0, n), W - 1, None, OP.bitwise_and, name="M'")
+        if last:
+            copy(("ymf", lo, hi), mn, "M f")
+            return
+        ts(("mf_%d" % y, lo, hi), mn, 592.0, None, OP.add, name="mf")
+        mu = ("mu_%d" % y, lo, hi)
+        copy(mu, mn, "M'u")
+        gather(("xm", 16 * lo, 16 * hi), FL, mu, "XM'", XMV[5 * t + k])
+
+    for slot in range(4 * ROUNDS + 3):
+        if slot < 4 * ROUNDS:
+            step1(slot // 4, slot % 4)
+        e = slot - 1
+        if 0 <= e < 4 * ROUNDS:
+            t, k = divmod(e, 4)
+            necks(t, k)
+            if k == 3:
+                loops(t)
+            if t < ROUNDS - 1:
+                moved(t, k)
+            elif k == 3:
+                for j in range(4):
+                    moved(t, j)
+        f = slot - 2
+        if f >= 0 and f % 4 == 3 and f < 4 * ROUNDS:
+            landed(f // 4)
+            moved(f // 4, 4)
+    tt(("aout", 0, 1), ("tha", ROUNDS, ROUNDS + 1), ("tha", 0, 1), OP.subtract)
+    ts(("aout", 1, 2), ("aout", 0, 1), 0.0625, None, OP.mult)
+    dma("Y", lambda T: T.ya[:], lambda T: T.aout[:, 1:2], [("aout", 1, 2)], [], "st ya")
+    dma("Y", lambda T: T.yr[:, 0:224], lambda T: T.yrf[:, 0:224], [("yrf", 0, 224)], [], "st yr")
+    dma("Y", lambda T: T.ym[:, 0:224], lambda T: T.ymf[:, 0:224], [("ymf", 0, 224)], [], "st ym")
+    dma("Y", lambda T: T.yr[:, 224:256], lambda T: T.yrf[:, 224:256], [("yrf", 224, 256)], [], "st yr")
+    dma("Y", lambda T: T.ym[:, 224:256], lambda T: T.ymf[:, 224:256], [("ymf", 224, 256)], [], "st ym")
+    return ops
+
+
+def depend(ops):
+    acc = {}
+    for i, o in enumerate(ops):
+        dep = set()
+        touches = [(r, False) for r in o["rd"]] + [(r, True) for r in o["wr"]]
+        for (buf, lo, hi), wr in touches:
+            lst = acc.setdefault(buf, [])
+            ps = _psum(buf)
+            for (j, l2, h2, w2) in lst:
+                if j == i:
+                    continue
+                hit = lo < h2 and l2 < hi and (wr or w2)
+                if ps and not hit:
+                    hit = ops[j]["eng"] != o["eng"] and lo // BANK <= (h2 - 1) // BANK and l2 // BANK <= (hi - 1) // BANK
+                if hit:
+                    dep.add(j)
+        for (buf, lo, hi), wr in touches:
+            lst = acc[buf]
+            if wr and not _psum(buf):
+                lst[:] = [a for a in lst if not (lo <= a[1] and a[2] <= hi)]
+            lst.append((i, lo, hi, wr))
+        o["dep"] = dep
+
+
+def arrange(ops):
+    n = len(ops)
+    succ = [[] for _ in range(n)]
+    for i, o in enumerate(ops):
+        for j in o["dep"]:
+            succ[j].append(i)
+    rank = [0.0] * n
+    for i in range(n - 1, -1, -1):
+        o = ops[i]
+        rank[i] = o["dur"] + o["lat"] + max([rank[j] for j in succ[i]], default=0.0)
+    for i, o in enumerate(ops):
+        rank[i] += BONUS.get(o["name"], 0.0)
+    left = [len(o["dep"]) for o in ops]
+    at = [0.0] * n
+    free = {"V": 0.0, "S": 0.0, "P": 0.0, "G": 0.0, "Y": 0.0, "N": 0.0}
+    ready = {e: [] for e in free}
+
+    def push(i):
+        for e in ops[i]["eng"]:
+            ready[e].append(i)
+    for i in range(n):
+        if not left[i]:
+            push(i)
+    order = {e: [] for e in free}
+    done = 0
+    end = 0.0
+    while done < n:
+        best = None
+        for e in free:
+            if ready[e]:
+                t = max(free[e], min(at[i] for i in ready[e]))
+                if best is None or t < best[0]:
+                    best = (t, e)
+        t, e = best
+        i = max((j for j in ready[e] if at[j] <= t), key=lambda j: (rank[j], -j))
+        o = ops[i]
+        for x in o["eng"]:
+            ready[x].remove(i)
+        o["on"] = e
+        o["t0"] = t
+        order[e].append(i)
+        free[e] = t + o["dur"] if e != "N" else 0.0
+        f = t + o["dur"] + o["lat"]
+        end = max(end, f)
+        done += 1
+        for j in succ[i]:
+            at[j] = max(at[j], f)
+            left[j] -= 1
+            if not left[j]:
+                push(j)
+    return order, end
+
+
+_made = {}
+
+
+def made():
+    if not _made:
+        ops = design()
+        depend(ops)
+        order, end = arrange(ops)
+        _made["ops"], _made["order"], _made["end"] = ops, order, end
+        num = {}
+        for e in "VSPG":
+            c = 0
+            for i in order[e]:
+                if "dma" in ops[i] or "send" in ops[i]:
+                    continue
+                c += 1
+                num[i] = c
+        _made["num"] = num
+        seq = sorted(range(len(ops)), key=lambda i: (ops[i]["t0"], i))
+        pos = {i: n for e in order for n, i in enumerate(order[e])}
+        state = {e: {} for e in order}
+        after = {}
+        waits = {}
+        todo = {e: 0 for e in order}
+        ndone = 0
+        while ndone < len(seq):
+            for e in order:
+                while todo[e] < len(order[e]) and all(j in after for j in ops[order[e][todo[e]]]["dep"]):
+                    i = order[e][todo[e]]
+                    o = ops[i]
+                    st = state[e] if e != "N" else {}
+                    need = {}
+                    for j in o["dep"]:
+                        key, val = _key(j, ops, num)
+                        if key is not None and st.get(key, 0) < val and need.get(key, (0, 0))[0] < val:
+                            need[key] = (val, j)
+                    out = []
+                    for key, (val, j) in sorted(need.items(), key=lambda kv: -pos[kv[1][1]]):
+                        if st.get(key, 0) >= val:
+                            continue
+                        out.append((key, val))
+                        for a, c in after[j].items():
+                            st[a] = max(st.get(a, 0), c)
+                        st[key] = max(st.get(key, 0), val)
+                    waits[i] = out
+                    me = dict(st)
+                    key, val = _key(i, ops, num)
+                    if key is not None:
+                        me[key] = val
+                    after[i] = me
+                    todo[e] += 1
+                    ndone += 1
+        _made["waits"] = waits
+    return _made
+
+
+def _key(i, ops, num):
+    o = ops[i]
+    if "dma" in o:
+        return o["dma"], 16
+    if "send" in o:
+        return None, 0
+    if "recv" in o:
+        return "arr%d" % o["recv"], 8
+    return "s" + o["on"], num[i]
+
+
+def rank_program(g, core, T, topo):
+    rank = T.rank_of(core)
+    if rank is None:
+        return
+    m = made()
+    ops, order, waits = m["ops"], m["order"], m["waits"]
+    queues = {"V": g.vector, "S": g.scalar, "P": g.tensor, "G": g, "Y": g.sync}
+    sent = 0
+    for e in ("G", "Y", "S", "V", "P"):
+        q = queues[e]
+        for i in order[e]:
+            o = ops[i]
+            for key, val in waits[i]:
+                q.wait_ge(T.sem[key], val)
+            if "send" in o:
+                t = o["send"]
+                dst = T.cores[(rank + 1 + t % (N - 1)) % N]
+                rid, pid, _ = topo.addr(dst)
+                eng = topo.engines(core, dst)[:8]
+                g.remote_dma(out_ap=T["land%d" % t][:], in_ap=T["lout%d" % t][:], remote_sem=T.sem["arr%d" % t], local_sem=T.sem.ls,
+                             pid=pid, routing_id=rid, dma_engine_mask=sum(1 << x for x in eng))
+                sent += len(eng)
+            elif "dma" in o:
+                o["f"](q, T).then_inc(T.sem[o["dma"]], 16)
+            elif "flex" in o:
+                o["f"](q, T, e).then_inc(T.sem["s" + e], 1)
+            else:
+                o["f"](q, T).then_inc(T.sem["s" + e], 1)
+    g.wait_ge(T.sem.ls, sent)
+    for i, o in enumerate(ops):
+        if "dma" in o and o["name"].startswith("st"):
+            g.sync.wait_ge(T.sem[o["dma"]], 16)
+    for e in "VSPG":
+        g.sync.wait_ge(T.sem["s" + e], max(c for i, c in m["num"].items() if ops[i]["on"] == e))

@@ -1,61 +1,80 @@
 import numpy as np
+from concourse.bass import DstId, RemoteDMATransfer
 from concourse.mybir import dt, AluOpType, AxisListType, ActivationFunctionType
 
 OP = AluOpType
+ACT = ActivationFunctionType
 N, W, P, L, ROUNDS = 8, 2048, 256, 32, 3
-CK = 64
-FW = 1616
-CE = 16 * CK
+TW = 64
+CE = 16 * TW
+FO = 592
 BANK = 512
+NB = 3
+BIG = 12582912.0
 
-_F, _B, _I, _U = "float32", "bfloat16", "int32", "uint16"
+_F, _B, _I, _U, _H = "float32", "bfloat16", "int32", "uint16", "float16"
 SCRATCH = {
-    "fl": ("sbuf", [128, 2 * W], _B),
-    "xm": ("sbuf", [128, 4096], _B), "xp": ("sbuf", [128, 4096], _B),
+    "fl": ("sbuf", [128, FO + W], _B),
+    "xm": ("sbuf", [128, 4096], _B),
     "ones": ("sbuf", [128, 128], _B), "ident": ("sbuf", [128, 128], _B), "nident": ("sbuf", [128, 128], _B),
+    "sgp": ("sbuf", [128, 128], _H), "sgn": ("sbuf", [128, 128], _H),
     "g8": ("sbuf", [128, 8], _B), "g8b": ("sbuf", [128, 8], _B),
     "b1": ("sbuf", [128, 144], _B), "b4096": ("sbuf", [128, 144], _B),
     "b8192": ("sbuf", [128, 144], _B), "b16384": ("sbuf", [128, 144], _B),
-    "ck": ("sbuf", [128, 320], _B), "cy": ("sbuf", [128, 192], _B), "cz": ("sbuf", [128, 128], _B),
-    "iot": ("sbuf", [128, 256], _F), "i16": ("sbuf", [128, 64], _I), "ipt": ("sbuf", [128, 64], _I),
-    "ip2": ("sbuf", [128, 64], _I), "cpos": ("sbuf", [128, 64], _F),
-    "dgi": ("sbuf", [128, 512], _I), "dgj": ("sbuf", [128, 512], _I), "diag": ("sbuf", [128, 512], _F), "seg": ("sbuf", [128, 512], _F),
-    "thi": ("sbuf", [128, 1], _I), "epi": ("sbuf", [128, 1], _I), "epf": ("sbuf", [128, 2], _F),
-    "tha": ("sbuf", [128, 8], _F), "nk": ("sbuf", [128, 64], _F), "aout": ("sbuf", [128, 4], _F),
-    "ru0": ("sbuf", [128, 256], _U), "lu": ("sbuf", [128, 32], _U),
+    "b2": ("sbuf", [128, 144], _B), "bn1": ("sbuf", [128, 144], _B), "bn8192": ("sbuf", [128, 144], _B),
+    "ident2": ("sbuf", [128, 128], _B), "zero": ("sbuf", [128, 16 * TW], _B), "half": ("sbuf", [128, 1], _F),
+    "ck": ("sbuf", [128, 640], _B), "cy": ("sbuf", [128, 768], _B), "cz": ("sbuf", [128, 384], _B),
+    "identf": ("sbuf", [128, 128], _F),
+    "iot": ("sbuf", [128, 32], _F), "i16": ("sbuf", [128, 128], _I), "far": ("sbuf", [128, 128], _F),
+    "ipt": ("sbuf", [128, 2], _I), "ipf": ("sbuf", [128, 2], _F), "cpos": ("sbuf", [128, 256], _F),
+    "dgj": ("sbuf", [128, 512], _F), "diag": ("sbuf", [128, 512], _F), "seg": ("sbuf", [128, 512], _F),
+    "thi": ("sbuf", [128, 1], _I), "epi": ("sbuf", [128, 1], _I), "epf": ("sbuf", [128, 8], _F),
+    "tha": ("sbuf", [128, 8], _F), "nk": ("sbuf", [128, 32], _F), "aout": ("sbuf", [128, 4], _F),
+    "ru0": ("sbuf", [128, 256], _U), "lu": ("sbuf", [128, 32], _U), "ge": ("sbuf", [128, 224], _F),
     "lg": ("sbuf", [128, 512], _F), "ls": ("sbuf", [128, 512], _F),
-    "l1": ("sbuf", [128, 32], _F), "lm": ("sbuf", [128, 32], _F), "lo": ("sbuf", [128, 32], _F), "l2": ("sbuf", [128, 32], _F),
+    "lo": ("sbuf", [128, 64], _F), "lx": ("sbuf", [128, 64], _I),
     "yrf": ("sbuf", [128, 256], _F), "ymf": ("sbuf", [128, 256], _F),
-    "pv": ("psum", [128, 512], _F), "sc0": ("psum", [128, 512], _F), "sc1": ("psum", [128, 512], _F),
+    "pv": ("psum", [128, 512], _F), "sc": ("psum", [128, 1024], _F),
     "cnt": ("psum", [128, 512], _F), "sub0": ("psum", [128, 1024], _F), "sub1": ("psum", [128, 1024], _F),
 }
 for _k in range(3):
     SCRATCH["lout%d" % _k] = ("sbuf", [128, 32], _F)
     SCRATCH["land%d" % _k] = ("sbuf", [128, 32], _F)
 for _k in range(2):
-    for _n, _c, _d in (("rn", 264, _I), ("rf", 264, _F), ("mn", 264, _I), ("mf", 264, _F), ("rp", 296, _I),
-                       ("rpu", 256, _U), ("r2u", 256, _U), ("mu", 256, _U), ("xr", 4112, _B),
-                       ("me", 64, _F), ("pr", 256, _I), ("v", 256, _I), ("u", 256, _U), ("xd", 4096, _B), ("win", 5120, _B),
-                       ("now", 1024, _B), ("nb", 1024, _B), ("kb", 128, _F), ("kc", 128, _F), ("k4", 64, _I), ("ka", 64, _I),
-                       ("kv", 64, _I), ("w", 64, _F), ("o", 64, _F), ("ou", 64, _U), ("d", 64, _F), ("rr", 64, _I),
-                       ("a2", 1024, _B), ("nf", 64, _F), ("q", 64, _F), ("df", 64, _F), ("a3", 1024, _B), ("c3", 1024, _B), ("mm", 64, _I)):
+    for _n, _c, _d in (("rn", 264, _I), ("rf", 264, _F), ("mn", 264, _I), ("mf", 264, _F), ("rp", 264, _I), ("rm", 232, _F),
+                       ("rpu", 256, _U), ("r2u", 256, _U), ("mu", 256, _U), ("xr", 4112, _B), ("xp", 4096, _B)):
+        SCRATCH[_n + "_%d" % _k] = ("sbuf", [128, _c], _d)
+for _k in range(NB):
+    for _n, _c, _d in (("pr", 4 * TW, _I), ("v", 4 * TW, _I), ("u", 4 * TW, _U), ("fs", 8 * TW, _F), ("js", 5 * TW, _I), ("ou", TW, _U),
+                       ("win", 5 * CE, _B), ("now", CE, _B), ("nb", CE, _B), ("a2", CE, _B), ("a3", CE, _B), ("c3", CE, _B),
+                       ("aw", CE, _B), ("hb", 4 * CE, _B)):
         SCRATCH[_n + "_%d" % _k] = ("sbuf", [128, _c], _d)
 NDMA = 16
-SEMAPHORES = ["sV", "sS", "sP", "sG", "ls", "arr0", "arr1", "arr2"] + ["d%d" % k for k in range(NDMA)]
+HELPERS = 3
+STAGE = [x + "_%d" % k for x in ("win", "hb") for k in range(NB)] + ["xm", "xp_0", "xp_1", "xr_0", "xr_1"]
+FOLDED = ["now_%d" % k for k in range(NB)] + [x + "_%d" % k for x in ("hb", "a2") for k in range(NB)]
+SEMAPHORES = (["sV", "sS", "sP", "sG", "ls", "arr0", "arr1", "arr2"] + ["d%d" % k for k in range(NDMA)]
+              + [x + b for b in FOLDED for x in ("left_", "there_", "back_")])
 
-CY = 0.000833
-GA = 1.47
-PEC = 0.00053
-WAKE = 0.069
-BONUS = {"nearer": 4.0, "loop": -3.2, "score": -7.1, "nk-": -5.2, "now||": -1.0, "cnt3": 5.2, "XM'": -0.3, "ac||": 0.1, "now-": 0.9,
-         "nk||": 3.4, "ac-": -2.2, "df": -0.6, "c5||": 0.9, "c3": -0.3, "rf": 5.4, "cand||": 0.1, "u": 2.1, "XR'": -1.2, "me": -0.8,
-         "cand": 1.0, "c5-": -1.6, "v": -1.8, "dist": -0.1, "kmin": 3.7}
-VIAS = (0, 1, 2, 3)
-VW = 128
-NET = 5.5
-XMV = "SSSSSSSSSS"
-TAIL = 4 * ROUNDS - 1
-FIRST = ((0, 66, "S"), (66, 130, "V"), (130, 194, "S"), (194, 256, "S"))
+COST = {"cy": 0.000833, "ga": 1.47, "pe": 0.00053, "v": 0.02, "s": 0.1, "wake": 0.069, "net": 5.5, "issue": 1.0, "hop": 2.0, "dma": 200e3}
+TILES = ((0, 64, 128, 192, 256), (0, 64, 128, 192, 256), (0, 64, 128, 192, 256))
+PLAN = {
+    "cand": 128,
+    "plain": 128,
+    "tail": 1,
+    "acS": (),
+    "first": "SV",
+    "R16": "V",
+    "me": "S",
+    "relu": ("......", "......", "......"),
+    "now": ("......", "......", "......"),
+    "neck": ("......", "......", "......"),
+    "c5": "sub1",
+    "lag": (2, 3, 3),
+    "skew": 256,
+    "passes": 4,
+}
+BONUS = {"cand||": 1, "XR0": 3, "df": -2, "iota": -1, "cnt3": 2, "me": 2}
 
 
 def _span(r):
@@ -76,8 +95,15 @@ def _psum(name):
     return SCRATCH[name][0] == "psum" if name in SCRATCH else False
 
 
+def _cut(lo, hi, w):
+    k = -(-(hi - lo) // w)
+    b = [lo + 2 * ((hi - lo) * j // (2 * k)) for j in range(k)] + [hi]
+    return list(zip(b[:-1], b[1:]))
+
+
 def design():
     ops = []
+    CY, GA, PEC, VF, SF, WAKE = (COST[k] for k in ("cy", "ga", "pe", "v", "s", "wake"))
 
     def op(eng, f, rd, wr, dur, lat=WAKE, name="", **kw):
         o = {"eng": eng, "f": f, "rd": [_span(r) for r in rd], "wr": [_span(r) for r in wr], "dur": dur, "lat": lat, "name": name}
@@ -87,11 +113,11 @@ def design():
     def tt(out, a, b, alu, name="tt"):
         c = 1 if (_psum(a[0]) or _psum(b[0])) else 2
         op("V", lambda q, T: q.tensor_tensor(_ap(T, out), _ap(T, a), _ap(T, b), alu), [a, b], [out],
-           0.02 + CY * max(64, c * _count(out)), name=name)
+           VF + CY * max(64, c * _count(out)), name=name)
 
     def ts(out, a, s1, s2, op0, op1=None, name="ts"):
         aps = [s for s in (s1, s2) if isinstance(s, tuple)]
-        two = all(SCRATCH[r[0]][2] in (_B, _U) for r in (out, a))
+        two = all(SCRATCH[r[0]][2] in (_B, _U, _H) for r in (out, a))
 
         def f(q, T):
             x1 = _ap(T, s1) if isinstance(s1, tuple) else s1
@@ -99,50 +125,81 @@ def design():
             if op1 is None:
                 return q.tensor_scalar(_ap(T, out), _ap(T, a), x1, None, op0)
             return q.tensor_scalar(_ap(T, out), _ap(T, a), x1, x2, op0, op1)
-        op("V", f, [a] + aps, [out], 0.02 + CY * max(64, (0.5 if two else 1) * _count(out)), name=name)
+        op("V", f, [a] + aps, [out], VF + CY * max(64, (0.5 if two else 1) * _count(out)), name=name)
 
     def copy(out, a, name="copy"):
-        op("V", lambda q, T: q.tensor_copy(_ap(T, out), _ap(T, a)), [a], [out], 0.02 + CY * max(64, _count(out)), name=name)
+        op("V", lambda q, T: q.tensor_copy(_ap(T, out), _ap(T, a)), [a], [out], VF + CY * max(64, _count(out)), name=name)
 
     def memset(buf, lo, hi, val, p0=0, p1=128):
-        op("V", lambda q, T: q.memset(T[buf][p0:p1, lo:hi], val), [], [(buf, lo, hi)], 0.02 + CY * max(64, 0.5 * (hi - lo)), name="memset")
+        op("V", lambda q, T: q.memset(T[buf][p0:p1, lo:hi], val), [], [(buf, lo, hi)], VF + CY * max(64, 0.5 * (hi - lo)), name="memset")
+
+    def reduce(out, a, alu, name):
+        op("V", lambda q, T: q.tensor_reduce(_ap(T, out), _ap(T, a), AxisListType.X, alu), [a], [out], VF + CY * max(64, _count(a)), name=name)
+
+    def scan(out, a, b, first, op0, op1, name):
+        aps = [first] if isinstance(first, tuple) else []
+        op("V", lambda q, T: q.tensor_tensor_scan(_ap(T, out), _ap(T, a), _ap(T, b), _ap(T, first) if aps else first, op0, op1),
+           [a, b] + aps, [out], VF + CY * max(64, _count(out)), name=name)
 
     def gtt(out, win, off, b, alu, name):
         op("V", lambda q, T: q.tensor_tensor(_ap(T, out), _ap(T, win).indirect(_ap(T, off)), _ap(T, b), alu), [win, off, b], [out],
-           0.05 + CY * GA * _count(out), name=name)
+           VF + 0.03 + CY * GA * _count(out), name=name)
 
     def gather(out, win, off, name, eng="S"):
         def f(q, T, e):
             if e == "V":
                 return q.tensor_copy(_ap(T, out), _ap(T, win).indirect(_ap(T, off)))
-            return q.activation(_ap(T, out), _ap(T, win).indirect(_ap(T, off)), ActivationFunctionType.Copy)
+            return q.activation(_ap(T, out), _ap(T, win).indirect(_ap(T, off)), ACT.Copy)
         op(eng, f, [win, off], [out], 0.06 + CY * GA * _count(out), name=name, flex=True)
 
     def absS(out, a, name):
-        op("S", lambda q, T: q.activation(_ap(T, out), _ap(T, a), ActivationFunctionType.Abs), [a], [out],
-           0.1 + CY * _count(out), name=name)
+        op("S", lambda q, T: q.activation(_ap(T, out), _ap(T, a), ACT.Abs), [a], [out], SF + CY * _count(out), name=name)
 
-    def sub(out, a, b, name):
+    def mix(out, terms, name):
         def f(q, T):
             n = out[2] - out[1]
             for s in range(0, n, BANK):
                 e = min(n, s + BANK)
-                q.matmul(T[out[0]][:, out[1] + s:out[1] + e], T["ident"][:], T[a[0]][:, a[1] + s:a[1] + e], True, False)
-                i = q.matmul(T[out[0]][:, out[1] + s:out[1] + e], T["nident"][:], T[b[0]][:, b[1] + s:b[1] + e], False, True)
+                for j, (a, dg) in enumerate(terms):
+                    i = q.matmul(T[out[0]][:, out[1] + s:out[1] + e], T[dg][:], T[a[0]][:, a[1] + s:a[1] + e], j == 0, j == len(terms) - 1)
             return i
-        op("P", f, [a, b, ("ident", 0, 128), ("nident", 0, 128)], [out], PEC * 2 * _count(out), name=name)
+        op("P", f, [a for a, _ in terms] + [(dg, 0, 128) for _, dg in terms], [out], PEC * len(terms) * _count(out), name=name)
 
-    def total(out, a, wb, const, name, *more):
+    def sub(out, a, b, name, plus="ident", minus="nident"):
+        mix(out, [(a, plus), (b, minus)], name)
+
+    def total(out, terms, const, name, plus=None):
+        n = out[2] - out[1]
+
         def f(q, T):
             o = _ap(T, out)
             if const is not None:
-                q.matmul(o, T["ones"][:], T[const[0]][:, const[1]:const[1] + out[2] - out[1]], True, False)
-            todo = [(x, p) for x in (a,) + more for p in range(16)]
-            for n, (x, p) in enumerate(todo):
-                i = q.matmul(o, T[wb][:, 15 - p:143 - p], T[x[0]][:, x[1] + p:x[2]:16], const is None and n == 0, n == len(todo) - 1)
+                q.matmul(o, T["ones"][:], T[const[0]][:, const[1]:const[1] + n], True, False)
+            if plus is not None:
+                q.matmul(o, T["identf"][:], _ap(T, plus), False, False)
+            todo = [(x, wb, p) for x, wb in terms for p in range(16)]
+            for j, (x, wb, p) in enumerate(todo):
+                i = q.matmul(o, T[wb][:, 15 - p:143 - p], T[x[0]][:, x[1] + p:x[2]:16], const is None and j == 0, j == len(todo) - 1)
             return i
-        op("P", f, [a, (wb, 0, 144), ("ones", 0, 128)] + list(more) + ([(const[0], const[1], const[1] + 64)] if const else []), [out],
-           PEC * 64 * (16 * (1 + len(more)) + (1 if const else 0)), name=name)
+        op("P", f, [a for a, _ in terms] + [(wb, 0, 144) for _, wb in terms] + [("ones", 0, 128)]
+           + ([(const[0], const[1], const[1] + n)] if const else []) + ([plus, ("identf", 0, 128)] if plus else []), [out],
+           PEC * max(64, n) * (16 * len(terms) + (1 if const else 0) + (4 if plus else 0)), name=name)
+
+    uses = {}
+    room = [[[b, 0] for b in STAGE] for _ in range(HELPERS)]
+
+    def fold(out, pairs, name):
+        n, h = out[2] - out[1], len(uses) % HELPERS if out[0] not in uses else uses[out[0]][1]
+        uses[out[0]] = (uses.get(out[0], (0, h))[0] + 1, h)
+        while room[h][0][1] + n > SCRATCH[room[h][0][0]][1][1]:
+            room[h].pop(0)
+        at = room[h][0]
+        stage = (at[0], at[1], at[1] + n)
+        at[1] += n
+        move = n * 256 / COST["dma"]
+        job = {"out": out, "pairs": pairs, "stage": stage, "helper": h, "count": uses[out[0]][0]}
+        op("G", None, [x for pair in pairs for x in pair], [out], max(COST["issue"], 2 * move), lat=COST["hop"], name=name, fold=job)
+        op("N", None, [], [out], 0.0, lat=COST["issue"] + COST["hop"] + move, name="back", back=job)
 
     nd = [0]
 
@@ -151,264 +208,364 @@ def design():
         nd[0] += 1
         op(q, lambda e, T: e.dma_start(fo(T), fi(T)), rd, wr, 0.06, lat=2.0 + nbytes / 200e3, name=name, dma="d%d" % k)
 
-    dma("S", lambda T: T.fl[:, 0:W], lambda T: T.flood[:], [], [("fl", 0, W)], "ld flood", 524288)
+    def iota(out, pat, base, cm, rows=(0, 128)):
+        def f(q, T):
+            o = T[out[0]][rows[0]:rows[1], out[1]:out[2]]
+            if SCRATCH[out[0]][2] == _I:
+                return q.iota(o, pat, base, cm)
+            return q.iota(o, pat, base, cm, allow_small_or_imprecise_dtypes=True)
+        op("G", f, [out] if rows[0] else [], [out], 0.13 + 2 * CY * _count(out), name="iota")
+
+    def asel(out, a, pat, cmp, base, cm, rows=(0, 128)):
+        part = lambda T, r: T[r[0]][rows[0]:rows[1], r[1]:r[2]]
+        op("G", lambda q, T: q.affine_select(part(T, out), part(T, a), pat, cmp, 0.0, base, cm), [a], [out], 0.17 + 2 * CY * _count(out), name="asel")
+
+    def scale(out, a, x, y=0.0, name="scale", eng="VS"):
+        def f(q, T, e):
+            if e == "V":
+                return q.tensor_scalar(_ap(T, out), _ap(T, a), x, y, OP.mult, OP.add)
+            return q.activation(_ap(T, out), _ap(T, a), ACT.Identity, bias=y, scale=x)
+        op(eng, f, [a], [out], VF + CY * max(64, _count(out)), name=name, flex=True, slow=SF + CY * _count(out))
+
+    dma("S", lambda T: T.fl[:, FO:FO + W], lambda T: T.flood[:], [], [("fl", FO, FO + W)], "ld flood", 524288)
     dma("Y", lambda T: T["rn_0"][:, 0:P], lambda T: T.riv[:], [], [("rn_0", 0, P)], "ld riv", 131072)
     dma("Y", lambda T: T["mn_0"][:, 0:P], lambda T: T.bord[:], [], [("mn_0", 0, P)], "ld bord", 131072)
+    dma("S", lambda T: T.fl[:, 0:FO], lambda T: T.flood[:, W - FO:W], [], [("fl", 0, FO)], "ld flood2", 700000)
     dma("Y", lambda T: T.thi[:], lambda T: T.th[:], [], [("thi", 0, 1)], "ld th")
     dma("Y", lambda T: T.epi[:], lambda T: T.eps[:], [], [("epi", 0, 1)], "ld eps")
-    dma("S", lambda T: T.fl[:, W:W + FW], lambda T: T.flood[:, 0:FW], [], [("fl", W, W + FW)], "ld flood2", 414000)
-    iota = lambda out, pat, base, cm, dtype=_I: op(
-        "G", lambda q, T: q.iota(_ap(T, out), pat, base, cm, allow_small_or_imprecise_dtypes=True) if dtype == _F else q.iota(_ap(T, out), pat, base, cm),
-        [], [out], 0.13 + 2 * CY * _count(out), name="iota")
 
-    def asel(out, a, pat, cmp, base, cm):
-        op("G", lambda q, T: q.affine_select(_ap(T, out), _ap(T, a), pat, cmp, 0.0, base, cm), [a], [out], 0.17 + 2 * CY * _count(out), name="asel")
-
+    folds = any(x.strip(".0") for key in ("relu", "now", "neck") for x in PLAN[key])
     memset("ones", 0, 128, 1.0)
-    iota(("ipt", 0, 64), [[0, 64]], 0, 1)
-    iota(("i16", 0, 64), [[16, 64]], 0, 0)
+    iota(("ipt", 0, 2), [[0, 2]], 0, 1)
+    iota(("i16", 0, TW), [[16, TW]], 0, 0)
     asel(("ident", 0, 128), ("ones", 0, 128), [[-1, 128]], OP.is_equal, 0, 1)
     asel(("g8", 0, 8), ("ones", 0, 8), [[-16, 8]], OP.is_ge, 0, 1)
     asel(("g8b", 0, 8), ("g8", 0, 8), [[16, 8]], OP.is_ge, 15, -1)
-    iota(("iot", 0, 256), [[1, 256]], 0, 0, _F)
-    iota(("dgi", 0, 512), [[0, 32], [1, 16]], 0, -1)
+    iota(("iot", 0, 32), [[1, 32]], 1, 0)
+    iota(("far", 0, TW), [[0, TW]], 8192, 0)
     iota(("dgj", 0, 512), [[0, 32], [1, 16]], 0, 0)
-    ts(("nident", 0, 128), ("ident", 0, 128), -1.0, None, OP.mult)
+    iota(("diag", 0, 512), [[0, 512]], 1, 0)
+    asel(("seg", 0, 512), ("diag", 0, 512), [[0, 32], [1, 16]], OP.is_gt, 0, 0)
+    scale(("nident", 0, 128), ("ident", 0, 128), -1.0)
+    scale(("identf", 0, 128), ("ident", 0, 128), 1.0)
     memset("b1", 0, 144, 0.0)
     copy(("b1", 15, 143, 16), ("g8b", 0, 8))
-    for w in (8192, 16384, 4096):
-        ts(("b%d" % w, 0, 144), ("b1", 0, 144), float(w), None, OP.mult)
-    memset("ck", 0, 320, -262144.0, 0, 64)
-    for m in range(4):
-        memset("ck", 64 * m, 64 * m + 64, 32.0 * m, 64, 128)
-    memset("ck", 256, 320, 128.0, 64, 128)
-    cons = [(77 * t - 592) % W for t in range(ROUNDS)]
-    memset("cy", 0, 192, -2176.0, 0, 64)
-    for t in range(ROUNDS):
-        x = cons[t] / 32.0
-        hi = int(x * 4) / 4.0
-        memset("cy", 64 * t, 64 * t + 64, hi, 64, 96)
-        memset("cy", 64 * t, 64 * t + 64, x - hi, 96, 128)
-    memset("cz", 0, 64, -544.0, 0, 64)
-    memset("cz", 64, 128, -1568.0, 0, 64)
-    memset("cz", 0, 128, 0.0, 64, 128)
-    ts(("ip2", 0, 64), ("ipt", 0, 64), 15, None, OP.bitwise_and)
-    tt(("cpos", 0, 64), ("ip2", 0, 64), ("i16", 0, 64), OP.add)
-    POS, IOT = ("pv", 0, 64), ("pv", 64, 128)
-    copy(POS, ("cpos", 0, 64))
-    copy(IOT, ("iot", 0, 64))
-    ts(("cpos", 0, 64), ("cpos", 0, 64), 4096.0, None, OP.add)
-    ts(("dgi", 0, 512), ("dgi", 0, 512), 15, None, OP.bitwise_and)
-    ts(("diag", 0, 512), ("dgi", 0, 512), 0.0, None, OP.is_equal)
-    ts(("seg", 0, 512), ("dgj", 0, 512), 0.0, None, OP.is_gt)
+    for w in (8192, 16384, 4096) + ((2, -1, -8192) if folds else ()):
+        scale((("b%d" % w).replace("-", "n"), 0, 144), ("b1", 0, 144), float(w))
+    if folds:
+        scale(("ident2", 0, 128), ("ident", 0, 128), 2.0)
+        iota(("zero", 0, 16 * TW), [[0, 16 * TW]], 0, 0)
+        memset("half", 0, 1, -0.5)
+    iota(("ck", 0, 5 * TW), [[0, 5 * TW]], -262144, 0, (0, 64))
+    iota(("ck", 0, 5 * TW), [[32, 5], [0, TW]], 0, 0, (64, 128))
+    cons = [(77 * t - FO) % W for t in range(ROUNDS)]
+    for x, val in ((0, -2176), (3 * TW, -128))[:1 + folds]:
+        iota(("cy", x, x + 3 * TW), [[0, 3 * TW]], val, 0, (0, 64))
+        for t in range(ROUNDS):
+            iota(("cy", x + TW * t, x + TW * t + TW), [[0, TW]], cons[t] // 32, 0, (64, 96))
+            asel(("cy", x + TW * t, x + TW * t + TW), ("ones", 0, TW), [[0, TW]], OP.is_gt, cons[t] % 32, -1, (96, 128))
+    iota(("cz", 0, 3 * TW), [[0, 3 * TW]], -544, 0, (0, 64))
+    iota(("cz", 0, 2 * TW), [[-1024, 2], [0, TW]], 0, 0, (64, 128))
+    memset("cz", 2 * TW, 3 * TW, -FO / 64.0, 64, 128)
+    ts(("ipt", 1, 2), ("ipt", 0, 1), 15, None, OP.bitwise_and)
+    copy(("ipf", 0, 1), ("ipt", 1, 2))
+    ts(("pv", 0, TW), ("i16", 0, TW), ("ipf", 0, 1), None, OP.add)
+    ts(("cpos", 0, TW), ("i16", 0, TW), ("ipf", 0, 1), 4.0 * CE, OP.add, OP.add)
+    ts(("diag", 0, 512), ("dgj", 0, 512), ("ipf", 0, 1), None, OP.is_equal)
     copy(("tha", 0, 1), ("thi", 0, 1))
     copy(("epf", 0, 1), ("epi", 0, 1))
     ts(("epf", 1, 2), ("epi", 0, 1), -1.0, None, OP.mult)
+    ts(("epf", 2, 3), ("epi", 0, 1), 2.0, 1.0, OP.mult, OP.add)
+    op("V", lambda q, T: q.reciprocal(T.epf[:, 3:4], T.epf[:, 2:3]), [("epf", 2, 3)], [("epf", 3, 4)], 0.25, name="recip")
+    ts(("sgp", 0, 128), ("ident", 0, 128), ("epf", 3, 4), None, OP.mult)
+    ts(("sgn", 0, 128), ("nident", 0, 128), ("epf", 3, 4), None, OP.mult)
     for k in range(2):
-        memset("rf_%d" % k, 257, 264, 592.0)
-        memset("mf_%d" % k, 256, 264, 592.0)
-        memset("rp_%d" % k, 256, 296, -4096)
-        memset("xr_%d" % k, 4096, 4112, 0.0)
+        for buf, lo, hi, val in (("rf", 257, 264, FO), ("mf", 256, 264, FO), ("rp", 256, 264, 0), ("rm", 0, 1, 8192), ("xr", 4096, 4112, 0)):
+            iota(("%s_%d" % (buf, k), lo, hi), [[0, hi - lo]], val, 0)
 
-    FL = ("fl", 0, W)
-    FL2 = ("fl", 0, W + FW)
-    for lo, hi, e in FIRST:
+    FL = ("fl", FO, FO + W)
+    FC = ("fl", 0, W + 160)
+    cuts = [0] + [b + 2 for b in TILES[0][1:-1]] + [P]
+    for j, (lo, hi) in enumerate(zip(cuts[:-1], cuts[1:])):
         copy(("ru0", lo, hi), ("rn_0", lo, hi), "R u16")
-        gather(("xr_0", 16 * lo, 16 * hi), FL, ("ru0", lo, hi), "XR0", e)
+        gather(("xr_0", 16 * lo, 16 * hi), FL, ("ru0", lo, hi), "XR0", PLAN["first"][j] if j < len(PLAN["first"]) else "S")
     ts(("rf_0", 1, 257), ("rn_0", 0, 256), 592.0, None, OP.add)
     copy(("rf_0", 0, 1), ("rf_0", 1, 2))
     ts(("mf_0", 0, 256), ("mn_0", 0, 256), 592.0, None, OP.add)
-    for lo, hi in ((0, 64), (64, 128), (128, 192), (192, 256)):
+    for lo, hi in zip(TILES[0][:-1], TILES[0][1:]):
         copy(("mu_0", lo, hi), ("mn_0", lo, hi), "M u16")
         gather(("xm", 16 * lo, 16 * hi), FL, ("mu_0", lo, hi), "XM0")
 
-    nkc = [0]
+    tiles = sorted([(t, k) for t in range(ROUNDS) for k in range(len(TILES[t]) - 1)],
+                   key=lambda x: (TILES[x[0]][x[1] + 1] + PLAN["skew"] * x[0], x[0]))
+    written = [np.zeros(5 * CE, bool) for _ in range(NB)]
 
-    def nkcol():
-        c = nkc[0]
-        nkc[0] += 1
-        return ("nk", c, c + 1)
-    neck = {}
-
-    def halves(lo, hi, yes):
-        if not yes or hi - lo <= 32:
-            return [(lo, hi)]
-        m = (lo + hi) // 2
-        return [(lo, m), (m, hi)]
-
-    def step1(t, k):
-        s = (4 * t + k) % 2
+    def step1(j):
+        t, k = tiles[j]
+        c0, c1 = TILES[t][k], TILES[t][k + 1]
+        n = c1 - c0
+        late = j >= len(tiles) - PLAN["tail"]
         z = t % 2
-        b = lambda n: n + "_%d" % s
-        c0 = CK * k
-        rn, rf, mn, mf = "rn_%d" % z, "rf_%d" % z, "mn_%d" % z, "mf_%d" % z
-        xr = "xr_%d" % z
-        R16, K12, M5, UU = ("pv", 128, 192), ("pv", 192, 320), ("pv", 320, 384), ("pv", 384, 448)
-        T5, ZZ, K2 = ("pv", 192, 256), ("pv", 256, 320), ("pv", 256, 320)
-        xn = (xr, 16 * (c0 + 1), 16 * (c0 + 65))
-        sc = "sc%d" % s
-        ts(R16, (rn, c0, c0 + 64), 16.0, None, OP.add, name="R16")
+        rn, rf, mn, mf, xr, xp = ("%s_%d" % (x, z) for x in ("rn", "rf", "mn", "mf", "xr", "xp"))
+        pr, v, u, fs, js, ou = ("%s_%d" % (x, j % NB) for x in ("pr", "v", "u", "fs", "js", "ou"))
+        win, now, nb = ("%s_%d" % (x, j % NB) for x in ("win", "now", "nb"))
+        s0 = (0, BANK - 2 * n, 2 * BANK - 5 * n)[j % 3]
+        S = lambda a, b=1: ("sc", s0 + a * n, s0 + (a + b) * n)
+        F = lambda a, b=1: (fs, a * TW, a * TW + b * n)
+        J = lambda a: (js, a * TW, a * TW + n)
+        slot = CE
+        R16 = ("pv", TW + TW * (j % 3), TW + TW * (j % 3) + n)
+        scale(R16, (rf, c0 + 1, c1 + 1), 1.0, 16.0 - FO, "R16", PLAN["R16"])
         for m, (bf, o) in enumerate(((rf, c0), (rf, c0 + 2), (mf, c0), (mf, c0 + 1))):
-            tt((b("pr"), 64 * m, 64 * m + 64), R16, (bf, o, o + 64), OP.mult, name="prod")
-        for h in range(0, 256, VW):
-            ts((b("v"), h, h + VW), (b("pr"), h, h + VW), 4, W - 1, OP.arith_shift_right, OP.bitwise_and, name="v")
-            ts((b("u"), h, h + VW), (b("v"), h, h + VW), float(cons[t]), None, OP.add, name="u")
-        sub(("sub0", 0, CE), (xr, 16 * c0, 16 * (c0 + 64)), xn, "now-")
-        absS((b("now"), 0, CE), ("sub0", 0, CE), "now||")
-        sub(("sub0", 0, CE), ("xm", 16 * c0, 16 * (c0 + 64)), xn, "c5-")
-        absS((b("win"), 4 * CE, 5 * CE), ("sub0", 0, CE), "c5||")
+            tt((pr, n * m, n * m + n), R16, (bf, o, o + n), OP.mult, name="prod")
+        for h0, h1 in ((0, 2 * n), (2 * n, 4 * n)):
+            ts((v, h0, h1), (pr, h0, h1), 4, W - 1, OP.arith_shift_right, OP.bitwise_and, name="v")
+            ts((u, h0, h1), (v, h0, h1), 77.0 * t, None, OP.add, name="u")
+        signed = PLAN["relu"][t][k] != "."
+        relu = int(PLAN["relu"][t][k]) if signed else 0
+        how = PLAN["now"][t][k] if signed else ""
+        xn = (xr, 16 * c0 + 16, 16 * c1 + 16)
+        hb, aw = "hb_%d" % (j % NB), "aw_%d" % (j % NB)
+        if how in ("D", "E"):
+            fold((now, 0, 16 * n), [((xr, 16 * c0, 16 * c1), xn)], "now^")
+        for src, dst, at, name in ((xr, now, 0, "now"), ("xm", win, 4 * slot, "c5"))[signed:]:
+            for a, c in _cut(c0, c1, 64):
+                x = (PLAN["c5"] if signed else "sub0", 0, 16 * (c - a))
+                sub(x, (src, 16 * a, 16 * c), (xr, 16 * a + 16, 16 * c + 16), name + "-")
+                absS((dst, at + 16 * (a - c0), at + 16 * (c - c0)), x, name + "||")
         for m in range(4):
-            gtt((b("xd"), CE * m, CE * m + CE), FL2, (b("u"), 64 * m, 64 * m + 64), xn, OP.subtract, "cand")
-            absS((b("win"), CE * m, CE * m + CE), (b("xd"), CE * m, CE * m + CE), "cand||")
+            for a, c in _cut(0, n, PLAN["cand"]):
+                x = (win, slot * m + 16 * a, slot * m + 16 * c)
+                gtt(x, FC, (u, n * m + a, n * m + c), (xr, 16 * (c0 + a + 1), 16 * (c0 + c + 1)), OP.subtract, "cand")
+                if m >= relu:
+                    absS(x, x, "cand||")
+            if m == relu - 1:
+                fold((hb, 0, 16 * n * relu), [((win, slot * i, slot * i + 16 * n), ("zero", 0, 16 * n)) for i in range(relu)], "relu^")
+        seen = written[j % NB]
+        for m in range(5):
+            seen[slot * m:slot * m + 16 * n] = True
+        for m in range(4):
+            gap = np.flatnonzero(~seen[slot * m:slot * (m + 1)])
+            if len(gap):
+                a, c = slot * m + int(gap[0]), slot * m + int(gap[-1]) + 1
+                iota((win, a, c), [[0, c - a]], 0, 0)
+                seen[a:c] = True
         for m in (4, 0, 1, 2, 3):
-            total((sc, 64 * m, 64 * m + 64), (b("win"), CE * m, CE * m + CE), "b8192", ("ck", 64 * m), "score")
-        tt(K12, (sc, 0, 128), (b("v"), 0, 128), OP.add, "key")
-        tt((b("kb"), 0, 128), (sc, 128, 256), (b("v"), 128, 256), OP.add, "key")
-        tt((b("kc"), 0, 64), ("pv", 192, 256), (b("kb"), 0, 64), OP.min, "kmin")
-        tt(K2, K2, (b("kb"), 64, 128), OP.min, "kmin")
-        tt((b("k4"), 0, 64), K2, (b("kc"), 0, 64), OP.min, "kmin")
-        tt(M5, (sc, 256, 320), (b("k4"), 0, 64), OP.is_le, "m5")
-        ts((b("ka"), 0, 64), (b("k4"), 0, 64), 6144, 1, OP.bitwise_and, OP.arith_shift_right, name="ka")
-        tt(UU, M5, ("cpos", 0, 64), OP.mult, "uu")
-        tt((b("w"), 0, 64), POS, (b("ka"), 0, 64), OP.add, "w")
-        tt((b("o"), 0, 64), UU, (b("w"), 0, 64), OP.max, "o")
-        copy((b("ou"), 0, 64), (b("o"), 0, 64), "ou")
-        gtt((b("nb"), 0, CE), (b("win"), 0, 5 * CE), (b("ou"), 0, 64), (b("now"), 0, CE), OP.is_lt, "nearer")
-        ts((b("kv"), 0, 64), (b("k4"), 0, 64), W - 1, None, OP.bitwise_and, name="kv")
-        ts((b("me"), 0, 64), (mn, c0, c0 + 64), 4096.0 - cons[t], None, OP.add, name="me")
-        tt(T5, M5, (b("me"), 0, 64), OP.mult, "t5")
-        tt((b("d"), 0, 64), T5, (b("kv"), 0, 64), OP.max, "d")
-        total((sc, 320, 384), (b("nb"), 0, CE), "b16384", ("cy", 64 * t), "cnt1")
-        tt(ZZ, (sc, 320, 384), (b("d"), 0, 64), OP.add, "z")
-        tt((b("rr"), 0, 64), ZZ, (rn, c0, c0 + 64), OP.max, "rr")
+            x = (win, slot * m, slot * m + 16 * n)
+            if m < relu:
+                total(S(m), [(x, "bn8192"), ((hb, 16 * n * m, 16 * n * (m + 1)), "b16384")], ("ck", TW * m), "score")
+            else:
+                total(S(m), [(x, "b8192")], ("ck", TW * m), "score")
+        kb, kc, w, o, me, d = F(0, 2), F(2), F(3), F(4), F(5), F(6)
+        k4, ka, kv, rr = J(0), J(1), J(2), J(3)
+        tt(S(0, 2), S(0, 2), (v, 0, 2 * n), OP.add, "key")
+        tt(kb, S(2, 2), (v, 2 * n, 4 * n), OP.add, "key")
+        tt(kc, S(0), (fs, 0, n), OP.min, "kmin")
+        tt(S(1), S(1), (fs, n, 2 * n), OP.min, "kmin")
+        tt(k4, S(1), kc, OP.min, "kmin")
+        tt(S(0), S(4), k4, OP.is_le, "m5")
+        ts(kv, k4, W - 1, None, OP.bitwise_and, name="kv")
+        scale(me, (mf, c0, c1), 1.0, 4096.0 - cons[t] - FO, "me", PLAN["me"])
+        ts(ka, k4, 6144, 1, OP.bitwise_and, OP.arith_shift_right, name="ka")
+        tt(S(1), S(0), ("cpos", 0, n), OP.mult, "uu")
+        tt(w, ("pv", 0, n), ka, OP.add, "w")
+        tt(o, S(1), w, OP.max, "o")
+        copy((ou, 0, n), o, "ou")
+        tt(S(2), S(0), me, OP.mult, "t5")
+        tt(d, S(2), kv, OP.max, "d")
+        yield
+        whole = (win, 0, 4 * slot + 16 * n)
+        for a, c in _cut(0, n, 32 if late else 64 if signed else PLAN["cand"]):
+            h = (16 * a, 16 * c)
+            if not signed:
+                gtt((nb,) + h, whole, (ou, a, c), (now,) + h, OP.is_lt, "nearer")
+                continue
+            op("S", lambda q, T, a=a, c=c, h=h: q.activation(_ap(T, (aw,) + h), _ap(T, whole).indirect(_ap(T, (ou, a, c))), ACT.Abs),
+               [whole, (ou, a, c)], [(aw,) + h], 0.06 + CY * GA * (h[1] - h[0]), name="nearer")
+            x, r0, r1 = ("sub0", 0, h[1] - h[0]), (xr, 16 * (c0 + a), 16 * (c0 + c)), (xr, 16 * (c0 + a + 1), 16 * (c0 + c + 1))
+            if how == "E":
+                mix(x, [(r0, "nident"), (r1, "nident"), ((now,) + h, "ident2"), ((aw,) + h, "nident")], "near-")
+                op("S", lambda q, T, x=x, h=h: q.activation(_ap(T, (nb,) + h), _ap(T, x), ACT.Sign, bias=T.half[:, 0:1]),
+                   [x, ("half", 0, 1)], [(nb,) + h], SF + CY * (h[1] - h[0]), name="sign")
+                continue
+            if how == "D":
+                mix(x, [(r0, "nident"), (r1, "nident"), ((now,) + h, "ident2")], "now-")
+            else:
+                sub(x, r0, r1, "now-")
+                absS(x, x, "now||")
+            tt((nb,) + h, x, (aw,) + h, OP.is_gt, "near<")
+        Z = ("cnt", 256 + TW * (j % 3), 256 + TW * (j % 3) + n)
+        if how == "E":
+            total(Z, [((nb, 0, 16 * n), "b8192")], ("cy", TW * (3 + t)), "cnt1", d)
+        else:
+            total(Z, [((nb, 0, 16 * n), "b16384")], ("cy", TW * t), "cnt1", d)
+        tt(rr, Z, (rn, c0, c1), OP.max, "rr")
         rp, rpu = "rp_%d" % z, "rpu_%d" % z
-        e = 63 if k == 3 else 64
-        ts((rp, c0, c0 + e), (b("rr"), 0, e), W - 1, None, OP.bitwise_and, name="R'")
-        if k == 3:
+        e = n - (c1 == P)
+        ts((rp, c0, c0 + e), (js, 3 * TW, 3 * TW + e), W - 1, None, OP.bitwise_and, name="R'")
+        if c1 == P:
             copy((rp, 255, 256), (rn, 255, 256), "R'255")
-        copy((rpu, c0, c0 + 64), (rp, c0, c0 + 64), "R'u")
-        for a, c in halves(c0, c0 + 64, 4 * t + k >= TAIL):
-            gather(("xp", 16 * a, 16 * c), FL, (rpu, a, c), "XR'", "VS" if 4 * t + k >= TAIL else "S")
+        copy((rpu, c0, c1), (rp, c0, c1), "R'u")
+        for a, c in _cut(c0, c1, 32 if late else PLAN["plain"]):
+            gather((xp, 16 * a, 16 * c), FL, (rpu, a, c), "XR'", "VS" if late else "S")
 
-    def necks(t, k):
-        s = (4 * t + k) % 2
-        b = lambda n: n + "_%d" % s
-        lo, hi = max(0, 64 * k - 32), 64 * k + 32
+    def piece(j):
+        t, k = tiles[j]
+        return max(0, TILES[t][k] - L), TILES[t][k + 1] - L
+
+    def necks(j):
+        t, k = tiles[j]
+        lo, hi = piece(j)
+        if hi <= lo:
+            return
+        late = j >= len(tiles) - PLAN["tail"]
+        xp, rm, a2 = "xp_%d" % (t % 2), "rm_%d" % (t % 2), "a2_%d" % (j % NB)
         n = hi - lo
-        for a, c in halves(lo, hi, 4 * t + k >= TAIL):
-            h0, h1 = 16 * (a - lo), 16 * (c - lo)
-            sub(("sub1", h0, h1), ("xp", 16 * a, 16 * c), ("xp", 16 * (a + 32), 16 * (c + 32)), "nk-")
-            absS((b("a2"), h0, h1), ("sub1", h0, h1), "nk||")
-        total(("cnt", 0, n), (b("a2"), 0, 16 * n), "b1", None, "dist")
-        ts((b("nf"), 0, n), ("cnt", 0, n), ("tha", t, t + 1), 256.0, OP.is_ge, OP.mult, name="nf")
-        tt((b("q"), 0, n), ("pv", 64, 64 + n), (b("nf"), 0, n), OP.add, "q")
-        m = nkcol()
-        qq = (b("q"), 0, n)
-        op("V", lambda e, T: e.tensor_reduce(_ap(T, m), _ap(T, qq), AxisListType.X, OP.min), [qq], [m], 0.02 + CY * 64, name="red")
-        m2 = nkcol()
-        ts(m2, m, float(lo), neck[t, k - 1] if k else 256.0, OP.add, OP.min, name="nk")
-        neck[t, k] = m2
+        ds = ("cnt", TW * (j % 2), TW * (j % 2) + n)
+        if PLAN["neck"][t][k] == "D":
+            x, y = (xp, 16 * lo, 16 * hi), (xp, 16 * (lo + L), 16 * (hi + L))
+            fold((a2, 0, 16 * n), [(x, y)], "nk^")
+            total(ds, [(x, "bn1"), (y, "bn1"), ((a2, 0, 16 * n), "b2")], None, "dist")
+        else:
+            for i, (a, c) in enumerate(_cut(lo, hi, 32 if late else 64)):
+                h0 = 512 * (i % 2) if late else 0
+                x = ("sub1", h0, h0 + 16 * (c - a))
+                sub(x, (xp, 16 * a, 16 * c), (xp, 16 * (a + L), 16 * (c + L)), "nk-")
+                absS((a2, 16 * (a - lo), 16 * (c - lo)), x, "nk||")
+            total(ds, [((a2, 0, 16 * n), "b1")], None, "dist")
+        scan((rm, 1 + lo, 1 + hi), ds, ("far", 0, n), (rm, lo, lo + 1), OP.min, OP.min, "rm")
 
-    def loops(t):
-        z = t % 2
-        nk = neck[t, 3]
-        lout = "lout%d" % t
-        ts(("lu", 0, 32), ("iot", 0, 32), nk, 1.0, OP.add, OP.add, name="lu")
-        gtt(("lg", 0, 512), ("rp_%d" % z, 0, 296), ("lu", 0, 32), ("diag", 0, 512), OP.mult, "loop")
-        op("V", lambda e, T: e.tensor_tensor_scan(T.ls[:], T.seg[:], T.lg[:], 0.0, OP.mult, OP.add), [("seg", 0, 512), ("lg", 0, 512)], [("ls", 0, 512)],
-           0.02 + CY * 512, name="scan")
-        copy((lout, 0, 32), ("ls", 15, 512, 16), "lout")
-        op("G", None, [(lout, 0, 32)], [], 1.0, name="send", send=t)
-        op("N", None, [(lout, 0, 32)], [("land%d" % t, 0, 32)], 0.0, lat=NET, name="recv", recv=t)
-        ts(("tha", 4 + t, 5 + t), nk, 256.0, 16.0, OP.is_lt, OP.mult, name="A")
-        tt(("tha", t + 1, t + 2), ("tha", t, t + 1), ("tha", 4 + t, 5 + t), OP.add, "A")
+    def before(j):
+        t, k = tiles[j]
+        lo = piece(j)[0]
+        ts(("ge", 0, lo), ("rm_%d" % (t % 2), 1, 1 + lo), ("tha", t, t + 1), None, OP.is_ge, name="ge")
+        reduce(("nk", 8 * t, 8 * t + 1), ("ge", 0, lo), OP.add, "ge")
 
-    def landed(t):
-        rp, lout = ("rp_%d" % (t % 2), 224, 256), ("lout%d" % t, 0, 32)
-        ts(("lm", 0, 32), ("iot", 224, 256), neck[t, 3], None, OP.is_gt, name="l0")
-        tt(("lo", 0, 32), lout, rp, OP.subtract, "l0")
-        tt(("lo", 0, 32), ("lo", 0, 32), ("lm", 0, 32), OP.mult, "l0")
-        tt(("lo", 0, 32), ("lo", 0, 32), rp, OP.add, "l0")
-        ts(("lm", 0, 32), ("lm", 0, 32), 1.0, 8192.0, OP.subtract, OP.mult, name="l0")
-        tt(("l1", 0, 32), ("land%d" % t, 0, 32), ("lm", 0, 32), OP.add, "l1")
-        ts(("l2", 0, 32), ("l1", 0, 32), 0.0, -8192.0, OP.is_ge, OP.mult, name="l1")
-        tt(("l2", 0, 32), ("l2", 0, 32), ("lo", 0, 32), OP.add, "l2")
+    def loops(j):
+        t, k = tiles[j]
+        lo = piece(j)[0]
+        rm, rp, th = "rm_%d" % (t % 2), "rp_%d" % (t % 2), ("tha", t, t + 1)
+        c = lambda i: ("nk", 8 * t + i, 8 * t + i + 1)
+        end = (rm, P - L, P - L + 1)
+        lout = ("lout%d" % t, 0, 32)
+        ts(("ge", lo, P - L), (rm, 1 + lo, 1 + P - L), th, None, OP.is_ge, name="ge2")
+        reduce(c(1), ("ge", lo, P - L), OP.add, "ge2")
+        ts(("lu", 0, 32), ("iot", 0, 32), c(0), c(1), OP.add, OP.add, name="lu")
+        ts(c(2), end, th, 12288.0, OP.is_lt, OP.mult, name="fl")
+        gtt(("lg", 0, 512), (rp, 0, 264), ("lu", 0, 32), ("diag", 0, 512), OP.mult, "loop")
+        scan(("ls", 0, 512), ("seg", 0, 512), ("lg", 0, 512), 0.0, OP.mult, OP.add, "scan")
+        own = ("ls", 15, 512, 16)
+        ts(lout, own, c(2), -8192.0, OP.add, OP.add, name="lout")
+        op("G", None, [lout], [], 1.0, name="send", send=t)
+        op("N", None, [lout], [("land%d" % t, 0, 32)], 0.0, lat=COST["net"], name="recv", recv=t)
+        ts(c(3), end, th, 16.0, OP.is_lt, OP.mult, name="A")
+        tt(("tha", t + 1, t + 2), th, c(3), OP.add, "A")
+        ts(c(4), end, th, 16384.0, OP.is_ge, OP.mult, name="l0")
+        ts(("lo", 32, 64), (rp, P - L, P), c(4), -8192.0, OP.add, OP.add, name="l0")
+        tt(("lo", 0, 32), own, ("lo", 32, 64), OP.max, "l0")
 
-    def moved(t, k):
-        s = (4 * t + k) % 2
-        b = lambda n: n + "_%d" % s
+    def moved(t, k, lo, hi, s):
         z, y = t % 2, (t + 1) % 2
-        last = t == ROUNDS - 1
-        cn, c0 = ("sc0", 0) if last and k < 4 else ("cnt", 64)
-        lo, hi = (max(0, 64 * k - 32), 64 * k + 32) if k < 4 else (224, 256)
+        last, end = t == ROUNDS - 1, hi == P
         n = hi - lo
+        if n <= 0:
+            return
+        a3, c3, fs, js = ("%s_%d" % (x, s) for x in ("a3", "c3", "fs", "js"))
+        cn, sb = ("cnt", 128 + TW * (s % 2), 128 + TW * (s % 2) + n), "sub0" if last and not end else "sub1"
         rp = "rp_%d" % z
-        rn = ("yrf", lo, hi) if last else ("rn_%d" % y, lo, hi)
-        MK = ("pv", 448, 448 + n)
-        if k < 4:
-            tt((b("df"), 0, n), (rp, lo + 32, hi + 32), (rp, lo, hi), OP.subtract, "df")
-            ts(MK, ("iot", lo, hi), neck[t, k], None, OP.is_gt, name="mk")
-            tt(MK, MK, (b("df"), 0, n), OP.mult, "dm")
+        rn = ("yrf", lo, hi) if last and not end else ("rn_%d" % y, lo, hi)
+        if not end:
+            MK, df = ("pv", 256 + TW * s, 256 + TW * s + n), (fs, 7 * TW, 7 * TW + n)
+            tt(df, (rp, lo + L, hi + L), (rp, lo, hi), OP.subtract, "df")
+            ts(MK, ("rm_%d" % z, lo, hi), ("tha", t, t + 1), None, OP.is_lt, name="mk")
+            tt(MK, MK, df, OP.mult, "dm")
             tt(rn, MK, (rp, lo, hi), OP.add, "R''")
         else:
-            tt(rn, ("l2", 0, 32), ("l1", 0, 32), OP.max, "R''")
-        u = ("r2u_%d" % z, lo, hi)
-        copy(u, rn, "R''u")
-        if last and k in VIAS:
-            x = ("xr_%d" % y, 16 * lo, 16 * hi)
-            gather(x, FL, u, "XR''")
-            sub(("sub0", 0, 16 * n), x, ("xm", 16 * lo, 16 * hi), "ac-")
-            absS((b("a3"), 0, 16 * n), ("sub0", 0, 16 * n), "ac||")
-            ts((b("c3"), 0, 16 * n), (b("a3"), 0, 16 * n), ("epf", 0, 1), None, OP.is_le, name="c3")
-            total((cn, c0, c0 + n), (b("c3"), 0, 16 * n), "b4096", ("cz", 0), "cnt3")
-        elif last:
-            x3, c3, c4 = (b("a3"), 0, 16 * n), (b("c3"), 0, 16 * n), (b("nb"), 0, 16 * n)
-            gtt(x3, FL, u, ("xm", 16 * lo, 16 * hi), OP.subtract, "cand")
-            ts(c3, x3, ("epf", 0, 1), None, OP.is_le, name="c3")
-            ts(c4, x3, ("epf", 1, 2), None, OP.is_ge, name="c3")
-            total((cn, c0, c0 + n), c3, "b4096", ("cz", 64), "cnt3", c4)
+            tt(("lx", 0, 32), ("land%d" % t, 0, 32), ("lo", 0, 32), OP.max, "l1")
+            ts(rn, ("lx", 0, 32), W - 1, None, OP.bitwise_and, name="l2")
+        u = "r2u_%d" % z
+        copy((u, lo, hi), rn, "R''u")
+        if last and end:
+            copy(("yrf", lo, hi), rn, "R f")
+            x3, c4, c5 = (a3, 0, 16 * n), (c3, 0, 16 * n), (c3, 16 * n, 32 * n)
+            gtt(x3, FL, (u, lo, hi), ("xm", 16 * lo, 16 * hi), OP.subtract, "cand")
+            ts(c4, x3, ("epf", 0, 1), None, OP.is_le, name="c3")
+            ts(c5, x3, ("epf", 1, 2), None, OP.is_ge, name="c3")
+            total(cn, [(c4, "b4096"), (c5, "b4096")], ("cz", TW), "cnt3", ("yrf", lo, hi))
         else:
-            gather(("xr_%d" % y, 16 * lo, 16 * hi), FL, u, "XR''")
-        if not last:
-            rf = "rf_%d" % y
-            ts((rf, lo + 1, hi + 1), rn, 592.0, None, OP.add, name="rf")
-            if k == 0:
-                copy((rf, 0, 1), (rf, 1, 2), "rf0")
-            sub(("sub1", 0, 16 * n), ("xr_%d" % y, 16 * lo, 16 * hi), ("xm", 16 * lo, 16 * hi), "ac-")
-            absS((b("a3"), 0, 16 * n), ("sub1", 0, 16 * n), "ac||")
-            ts((b("c3"), 0, 16 * n), (b("a3"), 0, 16 * n), ("epf", 0, 1), None, OP.is_le, name="c3")
-            total((cn, c0, c0 + n), (b("c3"), 0, 16 * n), "b4096", ("cz", 0), "cnt3")
-        Z3 = ("pv", 448, 448 + n)
-        tt(Z3, (cn, c0, c0 + n), rn, OP.add, "z3")
-        tt((b("mm"), 0, n), Z3, ("mn_%d" % z, lo, hi), OP.max, "mm")
-        mn = ("mn_%d" % y, lo, hi)
-        ts(mn, (b("mm"), 0, n), W - 1, None, OP.bitwise_and, name="M'")
+            xr = "xr_%d" % y
+            for a, c in _cut(lo, hi, PLAN["plain"]):
+                gather((xr, 16 * a, 16 * c), FL, (u, a, c), "XR''")
+            if not last:
+                rf = "rf_%d" % y
+                ts((rf, lo + 1, hi + 1), rn, 592.0, None, OP.add, name="rf")
+                if lo == 0:
+                    copy((rf, 0, 1), (rf, 1, 2), "rf0")
+            for a, c in _cut(lo, hi, 64):
+                x, h = (sb, 0, 16 * (c - a)), (16 * (a - lo), 16 * (c - lo))
+                if last or (t, k) in PLAN["acS"]:
+                    sub(x, (xr, 16 * a, 16 * c), ("xm", 16 * a, 16 * c), "ac-")
+                    absS((a3,) + h, x, "ac||")
+                else:
+                    sub(x, (xr, 16 * a, 16 * c), ("xm", 16 * a, 16 * c), "ac-", "sgp", "sgn")
+                    ts((c3,) + h, x, BIG, BIG, OP.add, OP.is_equal, name="ac=")
+            if last or (t, k) in PLAN["acS"]:
+                ts((c3, 0, 16 * n), (a3, 0, 16 * n), ("epf", 0, 1), None, OP.is_le, name="c3")
+            if last:
+                total(cn, [((c3, 0, 16 * n), "b4096")], ("cz", 0), "cnt3", rn)
+            else:
+                total(cn, [((c3, 0, 16 * n), "b4096")], ("cz", 2 * TW), "cnt3", ("rf_%d" % y, lo + 1, hi + 1))
+        mm, mn = (js, 4 * TW, 4 * TW + n), ("mn_%d" % y, lo, hi)
+        tt(mm, cn, ("mn_%d" % z, lo, hi), OP.max, "mm")
+        ts(mn, mm, W - 1, None, OP.bitwise_and, name="M'")
         if last:
             copy(("ymf", lo, hi), mn, "M f")
             return
         ts(("mf_%d" % y, lo, hi), mn, 592.0, None, OP.add, name="mf")
-        mu = ("mu_%d" % y, lo, hi)
-        copy(mu, mn, "M'u")
-        gather(("xm", 16 * lo, 16 * hi), FL, mu, "XM'", XMV[5 * t + k])
+        mu = "mu_%d" % y
+        copy((mu, lo, hi), mn, "M'u")
+        for a, c in _cut(lo, hi, PLAN["plain"]):
+            gather(("xm", 16 * a, 16 * c), FL, (mu, a, c), "XM'")
 
-    for slot in range(4 * ROUNDS + 3):
-        if slot < 4 * ROUNDS:
-            step1(slot // 4, slot % 4)
-        e = slot - 1
-        if 0 <= e < 4 * ROUNDS:
-            t, k = divmod(e, 4)
-            necks(t, k)
-            if k == 3:
-                loops(t)
-            if t < ROUNDS - 1:
-                moved(t, k)
-            elif k == 3:
-                for j in range(4):
-                    moved(t, j)
-        f = slot - 2
-        if f >= 0 and f % 4 == 3 and f < 4 * ROUNDS:
-            landed(f // 4)
-            moved(f // 4, 4)
+    def whole(j):
+        t, k = tiles[j]
+        final = TILES[t][k + 1] == P
+        yield from step1(j)
+        yield
+        if final:
+            before(j)
+        necks(j)
+        if final:
+            loops(j)
+        yield
+        if t < ROUNDS - 1:
+            moved(t, k, *piece(j), j % NB)
+        elif final:
+            for i in range(k + 1):
+                moved(t, i, *piece(tiles.index((t, i))), (j + i + 1) % NB)
+            moved(t, k + 1, P - L, P, (j + k + 2) % NB)
+        yield
+
+    runs = [whole(j) for j in range(len(tiles))]
+    part = [0] * len(tiles)
+
+    def upto(j, p):
+        for i in range(max(0, j + 1)):
+            while part[i] < p:
+                next(runs[i])
+                part[i] += 1
+
+    ended = 0
+    for j, (t, k) in enumerate(tiles):
+        for p in (4, 3, 2):
+            upto(j - PLAN["lag"][p - 2], p)
+        upto(max([i for i in range(j) if tiles[i][0] < t and piece(i)[0] <= TILES[t][k + 1]], default=-1), 4)
+        if ended < t and TILES[t][k + 1] >= P - L:
+            moved(ended, len(TILES[ended]) - 1, P - L, P, (j + 1) % NB)
+            ended += 1
+        upto(j, 1)
+    for p in (2, 3, 4):
+        upto(len(tiles) - 1, p)
     tt(("aout", 0, 1), ("tha", ROUNDS, ROUNDS + 1), ("tha", 0, 1), OP.subtract)
     ts(("aout", 1, 2), ("aout", 0, 1), 0.0625, None, OP.mult)
     dma("Y", lambda T: T.ya[:], lambda T: T.aout[:, 1:2], [("aout", 1, 2)], [], "st ya")
@@ -426,74 +583,88 @@ def depend(ops):
         touches = [(r, False) for r in o["rd"]] + [(r, True) for r in o["wr"]]
         for (buf, lo, hi), wr in touches:
             lst = acc.setdefault(buf, [])
-            ps = _psum(buf)
             for (j, l2, h2, w2) in lst:
-                if j == i:
-                    continue
-                hit = lo < h2 and l2 < hi and (wr or w2)
-                if ps and not hit:
-                    hit = ops[j]["eng"] != o["eng"] and lo // BANK <= (h2 - 1) // BANK and l2 // BANK <= (hi - 1) // BANK
-                if hit:
+                if j != i and lo < h2 and l2 < hi and (wr or w2):
                     dep.add(j)
         for (buf, lo, hi), wr in touches:
             lst = acc[buf]
-            if wr and not _psum(buf):
+            if wr:
                 lst[:] = [a for a in lst if not (lo <= a[1] and a[2] <= hi)]
             lst.append((i, lo, hi, wr))
         o["dep"] = dep
+        o["banks"] = {(buf, b) for (buf, lo, hi), _ in touches if _psum(buf) for b in range(lo // BANK, (hi - 1) // BANK + 1)}
+
+
+def lay(ops, rank, before, behind, back):
+    left = [len(x) for x in before]
+    at = [ops[i]["lat"] if back else 0.0 for i in range(len(ops))]
+    free = {e: 0.0 for e in "VSPGYN"}
+    ready = {e: [] for e in free}
+    held, out = {}, {}
+    for i in range(len(ops)):
+        if not left[i]:
+            for e in ops[i]["eng"]:
+                ready[e].append(i)
+
+    def when(i, e):
+        t = at[i]
+        for b in ops[i]["banks"]:
+            for x, f in held.get(b, {}).items():
+                if x != e and f > t:
+                    t = f
+        return t
+    while len(out) < len(ops):
+        t, e = min((max(free[e], min(when(i, e) for i in ready[e])), e) for e in free if ready[e])
+        i = max((j for j in ready[e] if when(j, e) <= t), key=lambda j: (rank[j], j if back else -j))
+        o = ops[i]
+        for x in o["eng"]:
+            ready[x].remove(i)
+        dur = o["slow"] if e == "S" and "slow" in o else o["dur"]
+        if e != "N":
+            free[e] = t + dur
+        end = t + dur + (0.0 if back else o["lat"])
+        out[i] = (t, end, e, len(out))
+        for b in o["banks"]:
+            held.setdefault(b, {})[e] = t + dur + COST["wake"]
+        for j in behind[i]:
+            at[j] = max(at[j], end + (ops[j]["lat"] if back else 0.0))
+            left[j] -= 1
+            if not left[j]:
+                for x in ops[j]["eng"]:
+                    ready[x].append(j)
+    return out
 
 
 def arrange(ops):
     n = len(ops)
-    succ = [[] for _ in range(n)]
+    pred, succ = [o["dep"] for o in ops], [[] for _ in ops]
     for i, o in enumerate(ops):
         for j in o["dep"]:
             succ[j].append(i)
     rank = [0.0] * n
     for i in range(n - 1, -1, -1):
+        rank[i] = ops[i]["dur"] + ops[i]["lat"] + max([rank[j] for j in succ[i]], default=0.0)
+    best = None
+    for _ in range(PLAN["passes"]):
+        there = lay(ops, [rank[i] + BONUS.get(ops[i]["name"], 0.0) for i in range(n)], pred, succ, False)
+        if best is None or max(x[1] for x in there.values()) < max(x[1] for x in best.values()):
+            best = there
+        home = lay(ops, [there[i][1] for i in range(n)], succ, pred, True)
+        rank = [home[i][1] for i in range(n)]
+    order = {e: [] for e in "VSPGYN"}
+    last = {}
+    for i in sorted(range(n), key=lambda i: best[i][3]):
         o = ops[i]
-        rank[i] = o["dur"] + o["lat"] + max([rank[j] for j in succ[i]], default=0.0)
-    for i, o in enumerate(ops):
-        rank[i] += BONUS.get(o["name"], 0.0)
-    left = [len(o["dep"]) for o in ops]
-    at = [0.0] * n
-    free = {"V": 0.0, "S": 0.0, "P": 0.0, "G": 0.0, "Y": 0.0, "N": 0.0}
-    ready = {e: [] for e in free}
-
-    def push(i):
-        for e in ops[i]["eng"]:
-            ready[e].append(i)
-    for i in range(n):
-        if not left[i]:
-            push(i)
-    order = {e: [] for e in free}
-    done = 0
-    end = 0.0
-    while done < n:
-        best = None
-        for e in free:
-            if ready[e]:
-                t = max(free[e], min(at[i] for i in ready[e]))
-                if best is None or t < best[0]:
-                    best = (t, e)
-        t, e = best
-        i = max((j for j in ready[e] if at[j] <= t), key=lambda j: (rank[j], -j))
-        o = ops[i]
-        for x in o["eng"]:
-            ready[x].remove(i)
-        o["on"] = e
-        o["t0"] = t
-        order[e].append(i)
-        free[e] = t + o["dur"] if e != "N" else 0.0
-        f = t + o["dur"] + o["lat"]
-        end = max(end, f)
-        done += 1
-        for j in succ[i]:
-            at[j] = max(at[j], f)
-            left[j] -= 1
-            if not left[j]:
-                push(j)
-    return order, end
+        o["t0"], o["on"] = best[i][0], best[i][2]
+        if o["on"] == "S" and "slow" in o:
+            o["dur"] = o["slow"]
+        if o["on"] == "G" and o["f"]:
+            o["dep"] = o["dep"] | set([j for j in order["G"] if ops[j]["f"]][-1:])
+        order[o["on"]].append(i)
+        for b in o["banks"]:
+            o["dep"] = o["dep"] | {j for x, j in last.setdefault(b, {}).items() if x != o["on"]}
+            last[b][o["on"]] = i
+    return order, max(x[1] for x in best.values())
 
 
 _made = {}
@@ -509,19 +680,18 @@ def made():
         for e in "VSPG":
             c = 0
             for i in order[e]:
-                if "dma" in ops[i] or "send" in ops[i]:
+                if "dma" in ops[i] or "send" in ops[i] or "fold" in ops[i]:
                     continue
                 c += 1
                 num[i] = c
         _made["num"] = num
-        seq = sorted(range(len(ops)), key=lambda i: (ops[i]["t0"], i))
         pos = {i: n for e in order for n, i in enumerate(order[e])}
         state = {e: {} for e in order}
         after = {}
         waits = {}
         todo = {e: 0 for e in order}
         ndone = 0
-        while ndone < len(seq):
+        while ndone < len(ops):
             for e in order:
                 while todo[e] < len(order[e]) and all(j in after for j in ops[order[e][todo[e]]]["dep"]):
                     i = order[e][todo[e]]
@@ -541,7 +711,7 @@ def made():
                             st[a] = max(st.get(a, 0), c)
                         st[key] = max(st.get(key, 0), val)
                     waits[i] = out
-                    me = dict(st)
+                    me = dict(st) if e != "N" else {}
                     key, val = _key(i, ops, num)
                     if key is not None:
                         me[key] = val
@@ -560,15 +730,35 @@ def _key(i, ops, num):
         return None, 0
     if "recv" in o:
         return "arr%d" % o["recv"], 8
+    if "fold" in o:
+        return "left_" + o["fold"]["out"][0], 16 * o["fold"]["count"]
+    if "back" in o:
+        return "back_" + o["back"]["out"][0], 16 * o["back"]["count"]
     return "s" + o["on"], num[i]
+
+
+def helpers(core, T, topo):
+    free = [c for c in topo.cores_of(core) if T.rank_of(c) is None]
+    return sorted(free, key=lambda c: topo.die(c) != topo.die(core))[:HELPERS]
 
 
 def rank_program(g, core, T, topo):
     rank = T.rank_of(core)
-    if rank is None:
-        return
     m = made()
     ops, order, waits = m["ops"], m["order"], m["waits"]
+    jobs = [ops[i]["fold"] for i in order["G"] if "fold" in ops[i]]
+    if rank is None:
+        for home in T.cores:
+            if core in helpers(home, T, topo):
+                mine = [job for job in jobs if job["helper"] == helpers(home, T, topo).index(core)]
+                rid, pid, _ = topo.addr(home)
+                for job in mine:
+                    g.wait_ge(T.sem["there_" + job["out"][0]], 16 * job["count"])
+                    g.remote_dma(out_ap=_ap(T, job["out"]), in_ap=_ap(T, job["stage"]), remote_sem=T.sem["back_" + job["out"][0]],
+                                 local_sem=T.sem.ls, pid=pid, routing_id=rid, dma_engine_mask=topo.mask(core, home))
+                if mine:
+                    g.wait_ge(T.sem.ls, 16 * len(mine))
+        return
     queues = {"V": g.vector, "S": g.scalar, "P": g.tensor, "G": g, "Y": g.sync}
     sent = 0
     for e in ("G", "Y", "S", "V", "P"):
@@ -585,6 +775,16 @@ def rank_program(g, core, T, topo):
                 g.remote_dma(out_ap=T["land%d" % t][:], in_ap=T["lout%d" % t][:], remote_sem=T.sem["arr%d" % t], local_sem=T.sem.ls,
                              pid=pid, routing_id=rid, dma_engine_mask=sum(1 << x for x in eng))
                 sent += len(eng)
+            elif "fold" in o:
+                job = o["fold"]
+                dst = helpers(core, T, topo)[job["helper"]]
+                rid, pid, _ = topo.addr(dst)
+                eng, (buf, at, end) = topo.engines(core, dst), job["stage"]
+                share, n = len(eng) // len(job["pairs"]), (end - at) // len(job["pairs"])
+                g.remote_dma_fused([RemoteDMATransfer(
+                    dst_ids=[DstId(rid=rid, pnc=pid)], dma_engine_mask=sum(1 << x for x in eng[share * p:share * (p + 1)]),
+                    remote_sem=T.sem["there_" + job["out"][0]], srcs=[_ap(T, a), _ap(T, b)], dsts=[T[buf][:, at + n * p:at + n * (p + 1)]],
+                    alu_op=2) for p, (a, b) in enumerate(job["pairs"])], local_sem=T.sem["left_" + job["out"][0]])
             elif "dma" in o:
                 o["f"](q, T).then_inc(T.sem[o["dma"]], 16)
             elif "flex" in o:
@@ -592,6 +792,8 @@ def rank_program(g, core, T, topo):
             else:
                 o["f"](q, T).then_inc(T.sem["s" + e], 1)
     g.wait_ge(T.sem.ls, sent)
+    for name, count in {job["out"][0]: job["count"] for job in jobs}.items():
+        g.wait_ge(T.sem["left_" + name], 16 * count)
     for i, o in enumerate(ops):
         if "dma" in o and o["name"].startswith("st"):
             g.sync.wait_ge(T.sem[o["dma"]], 16)

@@ -14,23 +14,21 @@ BIG = 12582912.0
 
 _F, _B, _I, _U, _H = "float32", "bfloat16", "int32", "uint16", "float16"
 SCRATCH = {
-    "fl": ("sbuf", [128, FO + W], _B),
-    "xm": ("sbuf", [128, 4096], _B),
+    "fl": ("sbuf", [128, FO + W], _B), "xm": ("sbuf", [128, 4096], _B),
     "ones": ("sbuf", [128, 128], _B), "ident": ("sbuf", [128, 128], _B), "nident": ("sbuf", [128, 128], _B),
-    "sgp": ("sbuf", [128, 128], _H), "sgn": ("sbuf", [128, 128], _H),
+    "identf": ("sbuf", [128, 128], _F), "sgp": ("sbuf", [128, 128], _H), "sgn": ("sbuf", [128, 128], _H),
     "g8": ("sbuf", [128, 8], _B), "g8b": ("sbuf", [128, 8], _B),
-    "b1": ("sbuf", [128, 144], _B), "b4096": ("sbuf", [128, 144], _B),
+    "b1": ("sbuf", [128, 144], _B), "b2": ("sbuf", [128, 144], _B), "b4096": ("sbuf", [128, 144], _B),
+    "bn8192": ("sbuf", [128, 144], _B), "bn2": ("sbuf", [128, 144], _B), "b4": ("sbuf", [128, 144], _B),
+    "ident2": ("sbuf", [128, 128], _B), "zero": ("sbuf", [128, 2 * CE], _B),
     "b8192": ("sbuf", [128, 144], _B), "b16384": ("sbuf", [128, 144], _B),
-    "b2": ("sbuf", [128, 144], _B), "bn1": ("sbuf", [128, 144], _B), "bn8192": ("sbuf", [128, 144], _B),
-    "ident2": ("sbuf", [128, 128], _B), "zero": ("sbuf", [128, 16 * TW], _B), "half": ("sbuf", [128, 1], _F),
-    "ck": ("sbuf", [128, 640], _B), "cy": ("sbuf", [128, 768], _B), "cz": ("sbuf", [128, 384], _B),
-    "identf": ("sbuf", [128, 128], _F),
-    "iot": ("sbuf", [128, 32], _F), "i16": ("sbuf", [128, 128], _I), "far": ("sbuf", [128, 128], _F),
-    "ipt": ("sbuf", [128, 2], _I), "ipf": ("sbuf", [128, 2], _F), "cpos": ("sbuf", [128, 256], _F),
+    "ck": ("sbuf", [128, 5 * TW], _B), "cy": ("sbuf", [128, 3 * TW], _B), "cz": ("sbuf", [128, 3 * TW], _B),
+    "iot": ("sbuf", [128, 32], _F), "i16": ("sbuf", [128, TW], _F), "neg": ("sbuf", [128, TW], _F), "thb": ("sbuf", [128, 3 * TW], _F),
+    "ipt": ("sbuf", [128, 2], _I), "ipf": ("sbuf", [128, 2], _F), "cpos": ("sbuf", [128, 2 * TW], _F),
     "dgj": ("sbuf", [128, 512], _F), "diag": ("sbuf", [128, 512], _F), "seg": ("sbuf", [128, 512], _F),
     "thi": ("sbuf", [128, 1], _I), "epi": ("sbuf", [128, 1], _I), "epf": ("sbuf", [128, 8], _F),
     "tha": ("sbuf", [128, 8], _F), "nk": ("sbuf", [128, 32], _F), "aout": ("sbuf", [128, 4], _F),
-    "ru0": ("sbuf", [128, 256], _U), "lu": ("sbuf", [128, 32], _U), "ge": ("sbuf", [128, 224], _F),
+    "ru0": ("sbuf", [128, 256], _U), "lu": ("sbuf", [128, 32], _U),
     "lg": ("sbuf", [128, 512], _F), "ls": ("sbuf", [128, 512], _F),
     "lo": ("sbuf", [128, 64], _F), "lx": ("sbuf", [128, 64], _I),
     "yrf": ("sbuf", [128, 256], _F), "ymf": ("sbuf", [128, 256], _F),
@@ -47,34 +45,47 @@ for _k in range(2):
 for _k in range(NB):
     for _n, _c, _d in (("pr", 4 * TW, _I), ("v", 4 * TW, _I), ("u", 4 * TW, _U), ("fs", 8 * TW, _F), ("js", 5 * TW, _I), ("ou", TW, _U),
                        ("win", 5 * CE, _B), ("now", CE, _B), ("nb", CE, _B), ("a2", CE, _B), ("a3", CE, _B), ("c3", CE, _B),
-                       ("aw", CE, _B), ("hb", 4 * CE, _B)):
+                       ("aw", CE, _B), ("hb", 2 * CE, _B)):
         SCRATCH[_n + "_%d" % _k] = ("sbuf", [128, _c], _d)
-NDMA = 16
+NDMA = 11
 HELPERS = 3
-STAGE = [x + "_%d" % k for x in ("win", "hb") for k in range(NB)] + ["xm", "xp_0", "xp_1", "xr_0", "xr_1"]
-FOLDED = ["now_%d" % k for k in range(NB)] + [x + "_%d" % k for x in ("hb", "a2") for k in range(NB)]
+STAGE = ["win_%d" % k for k in range(NB)] + ["xm", "xp_0", "xp_1", "xr_0", "xr_1"]
+FOLDED = [x + "_%d" % k for x in ("now", "hb", "a2") for k in range(NB)]
 SEMAPHORES = (["sV", "sS", "sP", "sG", "ls", "arr0", "arr1", "arr2"] + ["d%d" % k for k in range(NDMA)]
               + [x + b for b in FOLDED for x in ("left_", "there_", "back_")])
 
-COST = {"cy": 0.000833, "ga": 1.47, "pe": 0.00053, "v": 0.02, "s": 0.1, "wake": 0.069, "net": 5.5, "issue": 1.0, "hop": 2.0, "dma": 200e3}
+COST = {"cy": 0.000833, "ga": 1.48, "pe": 0.00058, "v": 0.01, "s": 0.06, "wake": 0.18, "same": 0.26, "net": 5.5,
+        "issue": 1.0, "hop": 2.0, "dma": 200e3}
 TILES = ((0, 64, 128, 192, 256), (0, 64, 128, 192, 256), (0, 64, 128, 192, 256))
 PLAN = {
-    "cand": 128,
-    "plain": 128,
+    "cand": (32, 32, 32, 32, 32),
+    "pair": (0, 0),
+    "viaS": (),
+    "via": "sub0",
+    "plain": 64,
     "tail": 1,
-    "acS": (),
-    "first": "SV",
-    "R16": "V",
+    "acS": ((2, 0), (2, 1), (2, 2), (2, 3)),
+    "first": "SVV",
     "me": "S",
+    "subs": "00110",
+    "test": 32,
+    "apart": 0,
+    "pad": (0, 0, 0),
+    "haste": 1e6,
+    "parts": 1,
+    "plus": 0,
     "relu": ("......", "......", "......"),
-    "now": ("......", "......", "......"),
+    "now": ("DDDD", "DDDD", "DDDD"),
     "neck": ("......", "......", "......"),
-    "c5": "sub1",
-    "lag": (2, 3, 3),
-    "skew": 256,
-    "passes": 4,
+    "near": 32,
+    "eng": ("S", "S", "S", "S"),
+    "split": 2,
+    "lag": (2, 3, 8),
+    "passes": 270,
+    "seed": 1,
+    "shake": 2.0,
 }
-BONUS = {"cand||": 1, "XR0": 3, "df": -2, "iota": -1, "cnt3": 2, "me": 2}
+RANGE = ((0.2, 0.26, 1.47, 0.00042), (0.15, 0.25, 1.9, 0.00042), (0.15, 0.25, 1.3, 0.0008), (0.15, 0.25, 1.6, 0.0007))
 
 
 def _span(r):
@@ -143,17 +154,24 @@ def design():
 
     def gtt(out, win, off, b, alu, name):
         op("V", lambda q, T: q.tensor_tensor(_ap(T, out), _ap(T, win).indirect(_ap(T, off)), _ap(T, b), alu), [win, off, b], [out],
-           VF + 0.03 + CY * GA * _count(out), name=name)
+           VF + 0.03 + CY * GA * _count(out), name=name, picks=_count(out))
 
     def gather(out, win, off, name, eng="S"):
         def f(q, T, e):
             if e == "V":
                 return q.tensor_copy(_ap(T, out), _ap(T, win).indirect(_ap(T, off)))
             return q.activation(_ap(T, out), _ap(T, win).indirect(_ap(T, off)), ACT.Copy)
-        op(eng, f, [win, off], [out], 0.06 + CY * GA * _count(out), name=name, flex=True)
+        op(eng, f, [win, off], [out], 0.06 + CY * GA * _count(out), name=name, flex=True, picks=_count(out))
 
     def absS(out, a, name):
         op("S", lambda q, T: q.activation(_ap(T, out), _ap(T, a), ACT.Abs), [a], [out], SF + CY * _count(out), name=name)
+
+    def scale(out, a, x, y=0.0, name="scale", eng="VS"):
+        def f(q, T, e):
+            if e == "V":
+                return q.tensor_scalar(_ap(T, out), _ap(T, a), x, y, OP.mult, OP.add)
+            return q.activation(_ap(T, out), _ap(T, a), ACT.Identity, bias=y, scale=x)
+        op(eng, f, [a], [out], VF + CY * max(64, _count(out)), name=name, flex=True, slow=SF + CY * _count(out))
 
     def mix(out, terms, name):
         def f(q, T):
@@ -168,37 +186,33 @@ def design():
     def sub(out, a, b, name, plus="ident", minus="nident"):
         mix(out, [(a, plus), (b, minus)], name)
 
-    def total(out, terms, const, name, plus=None):
+    def total(out, terms, const, plus, name):
         n = out[2] - out[1]
+        first = ([("ones", (const[0], const[1], const[1] + n))] if const else []) + ([("identf", plus)] if plus else [])
 
         def f(q, T):
-            o = _ap(T, out)
-            if const is not None:
-                q.matmul(o, T["ones"][:], T[const[0]][:, const[1]:const[1] + n], True, False)
-            if plus is not None:
-                q.matmul(o, T["identf"][:], _ap(T, plus), False, False)
-            todo = [(x, wb, p) for x, wb in terms for p in range(16)]
-            for j, (x, wb, p) in enumerate(todo):
-                i = q.matmul(o, T[wb][:, 15 - p:143 - p], T[x[0]][:, x[1] + p:x[2]:16], const is None and j == 0, j == len(todo) - 1)
+            todo = [(T[m][:], _ap(T, x)) for m, x in first]
+            todo += [(T[wb][:, 15 - p:143 - p], T[x[0]][:, x[1] + p:x[2]:16]) for x, wb in terms for p in range(16)]
+            for j, (m, x) in enumerate(todo):
+                i = q.matmul(_ap(T, out), m, x, j == 0, j == len(todo) - 1)
             return i
-        op("P", f, [a for a, _ in terms] + [(wb, 0, 144) for _, wb in terms] + [("ones", 0, 128)]
-           + ([(const[0], const[1], const[1] + n)] if const else []) + ([plus, ("identf", 0, 128)] if plus else []), [out],
+        op("P", f, [x for x, _ in terms] + [(wb, 0, 144) for _, wb in terms] + [x for _, x in first] + [(m, 0, 128) for m, _ in first], [out],
            PEC * max(64, n) * (16 * len(terms) + (1 if const else 0) + (4 if plus else 0)), name=name)
 
     uses = {}
     room = [[[b, 0] for b in STAGE] for _ in range(HELPERS)]
 
-    def fold(out, pairs, name):
-        n, h = out[2] - out[1], len(uses) % HELPERS if out[0] not in uses else uses[out[0]][1]
-        uses[out[0]] = (uses.get(out[0], (0, h))[0] + 1, h)
+    def fold(out, a, b, name):
+        n, h = out[2] - out[1], FOLDED.index(out[0]) % HELPERS
+        uses[out[0]] = uses.get(out[0], 0) + 1
         while room[h][0][1] + n > SCRATCH[room[h][0][0]][1][1]:
             room[h].pop(0)
         at = room[h][0]
         stage = (at[0], at[1], at[1] + n)
         at[1] += n
         move = n * 256 / COST["dma"]
-        job = {"out": out, "pairs": pairs, "stage": stage, "helper": h, "count": uses[out[0]][0]}
-        op("G", None, [x for pair in pairs for x in pair], [out], max(COST["issue"], 2 * move), lat=COST["hop"], name=name, fold=job)
+        job = {"out": out, "a": a, "b": b, "stage": stage, "helper": h, "count": uses[out[0]]}
+        op("G", None, [a, b], [out], max(COST["issue"], 2 * move), lat=COST["hop"], name=name, fold=job)
         op("N", None, [], [out], 0.0, lat=COST["issue"] + COST["hop"] + move, name="back", back=job)
 
     nd = [0]
@@ -214,18 +228,17 @@ def design():
             if SCRATCH[out[0]][2] == _I:
                 return q.iota(o, pat, base, cm)
             return q.iota(o, pat, base, cm, allow_small_or_imprecise_dtypes=True)
-        op("G", f, [out] if rows[0] else [], [out], 0.13 + 2 * CY * _count(out), name="iota")
+        op("G", f, [], [out], 0.13 + WAKE + 2 * CY * _count(out), name="iota")
 
     def asel(out, a, pat, cmp, base, cm, rows=(0, 128)):
         part = lambda T, r: T[r[0]][rows[0]:rows[1], r[1]:r[2]]
-        op("G", lambda q, T: q.affine_select(part(T, out), part(T, a), pat, cmp, 0.0, base, cm), [a], [out], 0.17 + 2 * CY * _count(out), name="asel")
+        op("G", lambda q, T: q.affine_select(part(T, out), part(T, a), pat, cmp, 0.0, base, cm), [a], [out],
+           0.17 + WAKE + 2 * CY * _count(out), name="asel")
 
-    def scale(out, a, x, y=0.0, name="scale", eng="VS"):
-        def f(q, T, e):
-            if e == "V":
-                return q.tensor_scalar(_ap(T, out), _ap(T, a), x, y, OP.mult, OP.add)
-            return q.activation(_ap(T, out), _ap(T, a), ACT.Identity, bias=y, scale=x)
-        op(eng, f, [a], [out], VF + CY * max(64, _count(out)), name=name, flex=True, slow=SF + CY * _count(out))
+    widths = {b - a for x in TILES for a, b in zip(x, x[1:])}
+    tw = max(widths)
+    sw = 64 if tw <= 64 else TW
+    place = lambda bank, first, count, j, n: (bank, sw * (first + j % count), sw * (first + j % count) + n)
 
     dma("S", lambda T: T.fl[:, FO:FO + W], lambda T: T.flood[:], [], [("fl", FO, FO + W)], "ld flood", 524288)
     dma("Y", lambda T: T["rn_0"][:, 0:P], lambda T: T.riv[:], [], [("rn_0", 0, P)], "ld riv", 131072)
@@ -234,15 +247,14 @@ def design():
     dma("Y", lambda T: T.thi[:], lambda T: T.th[:], [], [("thi", 0, 1)], "ld th")
     dma("Y", lambda T: T.epi[:], lambda T: T.eps[:], [], [("epi", 0, 1)], "ld eps")
 
-    folds = any(x.strip(".0") for key in ("relu", "now", "neck") for x in PLAN[key])
     memset("ones", 0, 128, 1.0)
     iota(("ipt", 0, 2), [[0, 2]], 0, 1)
-    iota(("i16", 0, TW), [[16, TW]], 0, 0)
+    iota(("i16", 0, tw), [[16, tw]], 0, 0)
     asel(("ident", 0, 128), ("ones", 0, 128), [[-1, 128]], OP.is_equal, 0, 1)
     asel(("g8", 0, 8), ("ones", 0, 8), [[-16, 8]], OP.is_ge, 0, 1)
     asel(("g8b", 0, 8), ("g8", 0, 8), [[16, 8]], OP.is_ge, 15, -1)
-    iota(("iot", 0, 32), [[1, 32]], 1, 0)
-    iota(("far", 0, TW), [[0, TW]], 8192, 0)
+    iota(("iot", 0, 32), [[1, 32]], P - L + 1, 0)
+    memset("neg", 0, tw, -1.0)
     iota(("dgj", 0, 512), [[0, 32], [1, 16]], 0, 0)
     iota(("diag", 0, 512), [[0, 512]], 1, 0)
     asel(("seg", 0, 512), ("diag", 0, 512), [[0, 32], [1, 16]], OP.is_gt, 0, 0)
@@ -250,29 +262,25 @@ def design():
     scale(("identf", 0, 128), ("ident", 0, 128), 1.0)
     memset("b1", 0, 144, 0.0)
     copy(("b1", 15, 143, 16), ("g8b", 0, 8))
-    for w in (8192, 16384, 4096) + ((2, -1, -8192) if folds else ()):
-        scale((("b%d" % w).replace("-", "n"), 0, 144), ("b1", 0, 144), float(w))
-    if folds:
-        scale(("ident2", 0, 128), ("ident", 0, 128), 2.0)
-        iota(("zero", 0, 16 * TW), [[0, 16 * TW]], 0, 0)
-        memset("half", 0, 1, -0.5)
-    iota(("ck", 0, 5 * TW), [[0, 5 * TW]], -262144, 0, (0, 64))
-    iota(("ck", 0, 5 * TW), [[32, 5], [0, TW]], 0, 0, (64, 128))
+    for w in (8192, 16384, 4096, 2):
+        scale(("b%d" % w, 0, 144), ("b1", 0, 144), float(w))
+    iota(("ck", 0, 5 * tw), [[0, 5 * tw]], -262144, 0, (0, 64))
+    iota(("ck", 0, 5 * tw), [[32, 5], [0, tw]], 0, 0, (64, 128))
     cons = [(77 * t - FO) % W for t in range(ROUNDS)]
-    for x, val in ((0, -2176), (3 * TW, -128))[:1 + folds]:
-        iota(("cy", x, x + 3 * TW), [[0, 3 * TW]], val, 0, (0, 64))
-        for t in range(ROUNDS):
-            iota(("cy", x + TW * t, x + TW * t + TW), [[0, TW]], cons[t] // 32, 0, (64, 96))
-            asel(("cy", x + TW * t, x + TW * t + TW), ("ones", 0, TW), [[0, TW]], OP.is_gt, cons[t] % 32, -1, (96, 128))
-    iota(("cz", 0, 3 * TW), [[0, 3 * TW]], -544, 0, (0, 64))
-    iota(("cz", 0, 2 * TW), [[-1024, 2], [0, TW]], 0, 0, (64, 128))
-    memset("cz", 2 * TW, 3 * TW, -FO / 64.0, 64, 128)
+    iota(("cy", 0, 3 * tw), [[0, 3 * tw]], -2176, 0, (0, 64))
+    for t in range(ROUNDS):
+        iota(("cy", tw * t, tw * t + tw), [[0, tw]], cons[t] // 32, 0, (64, 96))
+        asel(("cy", tw * t, tw * t + tw), ("ones", 0, tw), [[0, tw]], OP.is_gt, cons[t] % 32, -1, (96, 128))
+    iota(("cz", 0, 3 * tw), [[0, 3 * tw]], -544, 0, (0, 64))
+    iota(("cz", 0, 2 * tw), [[-1024, 2], [0, tw]], 0, 0, (64, 128))
+    memset("cz", 2 * tw, 3 * tw, -FO / 64.0, 64, 128)
     ts(("ipt", 1, 2), ("ipt", 0, 1), 15, None, OP.bitwise_and)
     copy(("ipf", 0, 1), ("ipt", 1, 2))
-    ts(("pv", 0, TW), ("i16", 0, TW), ("ipf", 0, 1), None, OP.add)
-    ts(("cpos", 0, TW), ("i16", 0, TW), ("ipf", 0, 1), 4.0 * CE, OP.add, OP.add)
+    ts(("pv", 0, tw), ("i16", 0, tw), ("ipf", 0, 1), 1.0 / 512, OP.add, OP.mult)
+    for wide in {n > 64 for n in widths}:
+        ts(("cpos", TW * wide, TW * wide + tw), ("pv", 0, tw), 8.0 * (1 + wide), None, OP.add)
     ts(("diag", 0, 512), ("dgj", 0, 512), ("ipf", 0, 1), None, OP.is_equal)
-    copy(("tha", 0, 1), ("thi", 0, 1))
+    ts(("tha", 0, 1), ("thi", 0, 1), 2.0, -1.0, OP.mult, OP.add)
     copy(("epf", 0, 1), ("epi", 0, 1))
     ts(("epf", 1, 2), ("epi", 0, 1), -1.0, None, OP.mult)
     ts(("epf", 2, 3), ("epi", 0, 1), 2.0, 1.0, OP.mult, OP.add)
@@ -280,24 +288,23 @@ def design():
     ts(("sgp", 0, 128), ("ident", 0, 128), ("epf", 3, 4), None, OP.mult)
     ts(("sgn", 0, 128), ("nident", 0, 128), ("epf", 3, 4), None, OP.mult)
     for k in range(2):
-        for buf, lo, hi, val in (("rf", 257, 264, FO), ("mf", 256, 264, FO), ("rp", 256, 264, 0), ("rm", 0, 1, 8192), ("xr", 4096, 4112, 0)):
+        for buf, lo, hi, val in (("rf", 257, 264, FO), ("mf", 256, 264, FO), ("rp", 256, 264, 0), ("rm", 0, 1, 0), ("xr", 4096, 4112, 0)):
             iota(("%s_%d" % (buf, k), lo, hi), [[0, hi - lo]], val, 0)
 
     FL = ("fl", FO, FO + W)
     FC = ("fl", 0, W + 160)
     cuts = [0] + [b + 2 for b in TILES[0][1:-1]] + [P]
-    for j, (lo, hi) in enumerate(zip(cuts[:-1], cuts[1:])):
+    for j, (lo, hi) in enumerate(_cut(0, cuts[1], (cuts[1] + 3) // 2) + list(zip(cuts[1:-1], cuts[2:]))):
         copy(("ru0", lo, hi), ("rn_0", lo, hi), "R u16")
         gather(("xr_0", 16 * lo, 16 * hi), FL, ("ru0", lo, hi), "XR0", PLAN["first"][j] if j < len(PLAN["first"]) else "S")
-    ts(("rf_0", 1, 257), ("rn_0", 0, 256), 592.0, None, OP.add)
+    ts(("rf_0", 1, 257), ("rn_0", 0, 256), float(FO), None, OP.add)
     copy(("rf_0", 0, 1), ("rf_0", 1, 2))
-    ts(("mf_0", 0, 256), ("mn_0", 0, 256), 592.0, None, OP.add)
+    ts(("mf_0", 0, 256), ("mn_0", 0, 256), float(FO), None, OP.add)
+    copy(("mu_0", 0, P), ("mn_0", 0, P), "M u16")
     for lo, hi in zip(TILES[0][:-1], TILES[0][1:]):
-        copy(("mu_0", lo, hi), ("mn_0", lo, hi), "M u16")
-        gather(("xm", 16 * lo, 16 * hi), FL, ("mu_0", lo, hi), "XM0")
+        gather(("xm", 16 * lo, 16 * hi), FL, ("mu_0", lo, hi), "XM0", PLAN["eng"][3])
 
-    tiles = sorted([(t, k) for t in range(ROUNDS) for k in range(len(TILES[t]) - 1)],
-                   key=lambda x: (TILES[x[0]][x[1] + 1] + PLAN["skew"] * x[0], x[0]))
+    tiles = [(t, k) for t in range(ROUNDS) for k in range(len(TILES[t]) - 1)]
     written = [np.zeros(5 * CE, bool) for _ in range(NB)]
 
     def step1(j):
@@ -307,40 +314,50 @@ def design():
         late = j >= len(tiles) - PLAN["tail"]
         z = t % 2
         rn, rf, mn, mf, xr, xp = ("%s_%d" % (x, z) for x in ("rn", "rf", "mn", "mf", "xr", "xp"))
-        pr, v, u, fs, js, ou = ("%s_%d" % (x, j % NB) for x in ("pr", "v", "u", "fs", "js", "ou"))
-        win, now, nb = ("%s_%d" % (x, j % NB) for x in ("win", "now", "nb"))
-        s0 = (0, BANK - 2 * n, 2 * BANK - 5 * n)[j % 3]
+        pr, v, u, fs, js, ou, win, now, nb = ("%s_%d" % (x, j % NB) for x in ("pr", "v", "u", "fs", "js", "ou", "win", "now", "nb"))
+        s0 = (0, BANK - 2 * n, 2 * BANK - 5 * n)[j % 3] if sw == 64 else BANK * (j % 2)
         S = lambda a, b=1: ("sc", s0 + a * n, s0 + (a + b) * n)
         F = lambda a, b=1: (fs, a * TW, a * TW + b * n)
         J = lambda a: (js, a * TW, a * TW + n)
-        slot = CE
-        R16 = ("pv", TW + TW * (j % 3), TW + TW * (j % 3) + n)
-        scale(R16, (rf, c0 + 1, c1 + 1), 1.0, 16.0 - FO, "R16", PLAN["R16"])
+        wide = n > 64
+        slot = 2048 if wide else 1024
+        R16 = place("pv", 1, 3 if sw == 64 else 2, j, n)
+        ts(R16, (rn, c0, c1), 16.0, None, OP.add, name="R16")
         for m, (bf, o) in enumerate(((rf, c0), (rf, c0 + 2), (mf, c0), (mf, c0 + 1))):
             tt((pr, n * m, n * m + n), R16, (bf, o, o + n), OP.mult, name="prod")
-        for h0, h1 in ((0, 2 * n), (2 * n, 4 * n)):
+        for h0, h1 in ((0, 2 * n), (2 * n, 4 * n)) if PLAN["split"] == 2 or late else ((0, 4 * n),):
             ts((v, h0, h1), (pr, h0, h1), 4, W - 1, OP.arith_shift_right, OP.bitwise_and, name="v")
             ts((u, h0, h1), (v, h0, h1), 77.0 * t, None, OP.add, name="u")
         signed = PLAN["relu"][t][k] != "."
         relu = int(PLAN["relu"][t][k]) if signed else 0
-        how = PLAN["now"][t][k] if signed else ""
-        xn = (xr, 16 * c0 + 16, 16 * c1 + 16)
+        far = signed and PLAN["now"][t][k] == "D"
         hb, aw = "hb_%d" % (j % NB), "aw_%d" % (j % NB)
-        if how in ("D", "E"):
-            fold((now, 0, 16 * n), [((xr, 16 * c0, 16 * c1), xn)], "now^")
+        if far:
+            fold((now, 0, 16 * n), (xr, 16 * c0, 16 * c1), (xr, 16 * c0 + 16, 16 * c1 + 16), "now^")
         for src, dst, at, name in ((xr, now, 0, "now"), ("xm", win, 4 * slot, "c5"))[signed:]:
             for a, c in _cut(c0, c1, 64):
-                x = (PLAN["c5"] if signed else "sub0", 0, 16 * (c - a))
+                x = ("sub" + PLAN["subs"][name == "c5"], 0, 16 * (c - a))
                 sub(x, (src, 16 * a, 16 * c), (xr, 16 * a + 16, 16 * c + 16), name + "-")
                 absS((dst, at + 16 * (a - c0), at + 16 * (c - c0)), x, name + "||")
         for m in range(4):
-            for a, c in _cut(0, n, PLAN["cand"]):
-                x = (win, slot * m + 16 * a, slot * m + 16 * c)
-                gtt(x, FC, (u, n * m + a, n * m + c), (xr, 16 * (c0 + a + 1), 16 * (c0 + c + 1)), OP.subtract, "cand")
-                if m >= relu:
-                    absS(x, x, "cand||")
-            if m == relu - 1:
-                fold((hb, 0, 16 * n * relu), [((win, slot * i, slot * i + 16 * n), ("zero", 0, 16 * n)) for i in range(relu)], "relu^")
+            x = (win, slot * m, slot * m + 16 * n)
+            if m == 0 and j in PLAN["viaS"]:
+                gather(x, FC, (u, 0, n), "c1")
+                sub((PLAN["via"], 0, 16 * n), x, (xr, 16 * (c0 + 1), 16 * (c1 + 1)), "c1-")
+                absS(x, (PLAN["via"], 0, 16 * n), "c1||")
+                continue
+            for a, c in _cut(0, n, PLAN["cand"][m]):
+                gtt((win, slot * m + 16 * a, slot * m + 16 * c), FC, (u, n * m + a, n * m + c),
+                    (xr, 16 * (c0 + a + 1), 16 * (c0 + c + 1)), OP.subtract, "cand")
+            pair = 16 * n == slot and not late and PLAN["pair"][m // 2] and not (m < 2 and (j in PLAN["viaS"] or relu))
+            if m < relu:
+                if m == relu - 1:
+                    fold((hb, 0, slot * relu), (win, 0, slot * relu), ("zero", 0, slot * relu), "relu^")
+            elif not pair:
+                absS(x, x, "cand||")
+            elif m % 2:
+                x = (win, slot * (m - 1), slot * (m + 1))
+                absS(x, x, "cand||")
         seen = written[j % NB]
         for m in range(5):
             seen[slot * m:slot * m + 16 * n] = True
@@ -353,9 +370,9 @@ def design():
         for m in (4, 0, 1, 2, 3):
             x = (win, slot * m, slot * m + 16 * n)
             if m < relu:
-                total(S(m), [(x, "bn8192"), ((hb, 16 * n * m, 16 * n * (m + 1)), "b16384")], ("ck", TW * m), "score")
+                total(S(m), [(x, "bn8192"), ((hb, slot * m, slot * m + 16 * n), "b16384")], ("ck", tw * m), None, "score")
             else:
-                total(S(m), [(x, "b8192")], ("ck", TW * m), "score")
+                total(S(m), [(x, "b8192")], ("ck", tw * m), None, "score")
         kb, kc, w, o, me, d = F(0, 2), F(2), F(3), F(4), F(5), F(6)
         k4, ka, kv, rr = J(0), J(1), J(2), J(3)
         tt(S(0, 2), S(0, 2), (v, 0, 2 * n), OP.add, "key")
@@ -366,39 +383,35 @@ def design():
         tt(S(0), S(4), k4, OP.is_le, "m5")
         ts(kv, k4, W - 1, None, OP.bitwise_and, name="kv")
         scale(me, (mf, c0, c1), 1.0, 4096.0 - cons[t] - FO, "me", PLAN["me"])
-        ts(ka, k4, 6144, 1, OP.bitwise_and, OP.arith_shift_right, name="ka")
-        tt(S(1), S(0), ("cpos", 0, n), OP.mult, "uu")
+        ts(ka, k4, 6144, 10 - wide, OP.bitwise_and, OP.arith_shift_right, name="ka")
+        tt(S(1), S(0), ("cpos", TW * wide, TW * wide + n), OP.mult, "uu")
         tt(w, ("pv", 0, n), ka, OP.add, "w")
         tt(o, S(1), w, OP.max, "o")
-        copy((ou, 0, n), o, "ou")
+        ts((ou, 0, n), o, 512.0, None, OP.mult, name="ou")
         tt(S(2), S(0), me, OP.mult, "t5")
         tt(d, S(2), kv, OP.max, "d")
         yield
         whole = (win, 0, 4 * slot + 16 * n)
-        for a, c in _cut(0, n, 32 if late else 64 if signed else PLAN["cand"]):
+        for i, (a, c) in enumerate(_cut(0, n, PLAN["near"] if signed else 32 if late else PLAN["cand"][4])):
             h = (16 * a, 16 * c)
             if not signed:
                 gtt((nb,) + h, whole, (ou, a, c), (now,) + h, OP.is_lt, "nearer")
                 continue
             op("S", lambda q, T, a=a, c=c, h=h: q.activation(_ap(T, (aw,) + h), _ap(T, whole).indirect(_ap(T, (ou, a, c))), ACT.Abs),
-               [whole, (ou, a, c)], [(aw,) + h], 0.06 + CY * GA * (h[1] - h[0]), name="nearer")
-            x, r0, r1 = ("sub0", 0, h[1] - h[0]), (xr, 16 * (c0 + a), 16 * (c0 + c)), (xr, 16 * (c0 + a + 1), 16 * (c0 + c + 1))
-            if how == "E":
-                mix(x, [(r0, "nident"), (r1, "nident"), ((now,) + h, "ident2"), ((aw,) + h, "nident")], "near-")
-                op("S", lambda q, T, x=x, h=h: q.activation(_ap(T, (nb,) + h), _ap(T, x), ACT.Sign, bias=T.half[:, 0:1]),
-                   [x, ("half", 0, 1)], [(nb,) + h], SF + CY * (h[1] - h[0]), name="sign")
-                continue
-            if how == "D":
+               [whole, (ou, a, c)], [(aw,) + h], 0.06 + CY * GA * (h[1] - h[0]), name="nearer", picks=h[1] - h[0])
+            h0 = BANK * (i % 2) if c - a <= 32 else 0
+            x = ("sub" + PLAN["subs"][0], h0, h0 + h[1] - h[0])
+            r0, r1 = (xr, 16 * (c0 + a), 16 * (c0 + c)), (xr, 16 * (c0 + a + 1), 16 * (c0 + c + 1))
+            if far:
                 mix(x, [(r0, "nident"), (r1, "nident"), ((now,) + h, "ident2")], "now-")
             else:
                 sub(x, r0, r1, "now-")
                 absS(x, x, "now||")
             tt((nb,) + h, x, (aw,) + h, OP.is_gt, "near<")
-        Z = ("cnt", 256 + TW * (j % 3), 256 + TW * (j % 3) + n)
-        if how == "E":
-            total(Z, [((nb, 0, 16 * n), "b8192")], ("cy", TW * (3 + t)), "cnt1", d)
-        else:
-            total(Z, [((nb, 0, 16 * n), "b16384")], ("cy", TW * t), "cnt1", d)
+        Z = place("cnt", 4, 3, j, n) if sw == 64 else place("cnt", 3, 2, j, n)
+        total(Z, [((nb, 0, 16 * n), "b16384")], ("cy", tw * t), d if late or PLAN["plus"] else None, "cnt1")
+        if not (late or PLAN["plus"]):
+            tt(Z, Z, d, OP.add, "z")
         tt(rr, Z, (rn, c0, c1), OP.max, "rr")
         rp, rpu = "rp_%d" % z, "rpu_%d" % z
         e = n - (c1 == P)
@@ -407,7 +420,7 @@ def design():
             copy((rp, 255, 256), (rn, 255, 256), "R'255")
         copy((rpu, c0, c1), (rp, c0, c1), "R'u")
         for a, c in _cut(c0, c1, 32 if late else PLAN["plain"]):
-            gather((xp, 16 * a, 16 * c), FL, (rpu, a, c), "XR'", "VS" if late else "S")
+            gather((xp, 16 * a, 16 * c), FL, (rpu, a, c), "XR'", "VS" if late else PLAN["eng"][0])
 
     def piece(j):
         t, k = tiles[j]
@@ -416,52 +429,47 @@ def design():
     def necks(j):
         t, k = tiles[j]
         lo, hi = piece(j)
+        if k == 0:
+            ts(("thb", TW * t, TW * t + tw), ("neg", 0, tw), ("tha", t, t + 1), None, OP.mult, name="thb")
         if hi <= lo:
             return
         late = j >= len(tiles) - PLAN["tail"]
         xp, rm, a2 = "xp_%d" % (t % 2), "rm_%d" % (t % 2), "a2_%d" % (j % NB)
         n = hi - lo
-        ds = ("cnt", TW * (j % 2), TW * (j % 2) + n)
+        ds = place("cnt", 0, 2 if sw == 64 else 1, j, n)
         if PLAN["neck"][t][k] == "D":
             x, y = (xp, 16 * lo, 16 * hi), (xp, 16 * (lo + L), 16 * (hi + L))
-            fold((a2, 0, 16 * n), [(x, y)], "nk^")
-            total(ds, [(x, "bn1"), (y, "bn1"), ((a2, 0, 16 * n), "b2")], None, "dist")
+            fold((a2, 0, 16 * n), x, y, "nk^")
+            total(ds, [(x, "bn2"), (y, "bn2"), ((a2, 0, 16 * n), "b4")], None, ("thb", TW * t, TW * t + n), "dist")
         else:
-            for i, (a, c) in enumerate(_cut(lo, hi, 32 if late else 64)):
-                h0 = 512 * (i % 2) if late else 0
-                x = ("sub1", h0, h0 + 16 * (c - a))
+            for i, (a, c) in enumerate(_cut(lo, hi, 32 if late or PLAN["apart"] else 64)):
+                h0 = BANK * (i % 2) if late else 0
+                x = ("sub" + PLAN["subs"][2], h0, h0 + 16 * (c - a))
                 sub(x, (xp, 16 * a, 16 * c), (xp, 16 * (a + L), 16 * (c + L)), "nk-")
                 absS((a2, 16 * (a - lo), 16 * (c - lo)), x, "nk||")
-            total(ds, [((a2, 0, 16 * n), "b1")], None, "dist")
-        scan((rm, 1 + lo, 1 + hi), ds, ("far", 0, n), (rm, lo, lo + 1), OP.min, OP.min, "rm")
-
-    def before(j):
-        t, k = tiles[j]
-        lo = piece(j)[0]
-        ts(("ge", 0, lo), ("rm_%d" % (t % 2), 1, 1 + lo), ("tha", t, t + 1), None, OP.is_ge, name="ge")
-        reduce(("nk", 8 * t, 8 * t + 1), ("ge", 0, lo), OP.add, "ge")
+            total(ds, [((a2, 0, 16 * n), "b2")], None, ("thb", TW * t, TW * t + n), "dist")
+        scan((rm, 1 + lo, 1 + hi), ds, ("neg", 0, n), (rm, lo, lo + 1), OP.min, OP.max, "rm")
 
     def loops(j):
         t, k = tiles[j]
         lo = piece(j)[0]
-        rm, rp, th = "rm_%d" % (t % 2), "rp_%d" % (t % 2), ("tha", t, t + 1)
+        rm, rp = "rm_%d" % (t % 2), "rp_%d" % (t % 2)
         c = lambda i: ("nk", 8 * t + i, 8 * t + i + 1)
         end = (rm, P - L, P - L + 1)
         lout = ("lout%d" % t, 0, 32)
-        ts(("ge", lo, P - L), (rm, 1 + lo, 1 + P - L), th, None, OP.is_ge, name="ge2")
-        reduce(c(1), ("ge", lo, P - L), OP.add, "ge2")
+        reduce(c(0), (rm, 1, 1 + lo), OP.add, "ge")
+        reduce(c(1), (rm, 1 + lo, 1 + P - L), OP.add, "ge2")
         ts(("lu", 0, 32), ("iot", 0, 32), c(0), c(1), OP.add, OP.add, name="lu")
-        ts(c(2), end, th, 12288.0, OP.is_lt, OP.mult, name="fl")
+        ts(c(2), end, -12288.0, -8192.0, OP.mult, OP.add, name="fl")
         gtt(("lg", 0, 512), (rp, 0, 264), ("lu", 0, 32), ("diag", 0, 512), OP.mult, "loop")
         scan(("ls", 0, 512), ("seg", 0, 512), ("lg", 0, 512), 0.0, OP.mult, OP.add, "scan")
         own = ("ls", 15, 512, 16)
-        ts(lout, own, c(2), -8192.0, OP.add, OP.add, name="lout")
+        ts(lout, own, c(2), None, OP.add, name="lout")
         op("G", None, [lout], [], 1.0, name="send", send=t)
-        op("N", None, [lout], [("land%d" % t, 0, 32)], 0.0, lat=COST["net"], name="recv", recv=t)
-        ts(c(3), end, th, 16.0, OP.is_lt, OP.mult, name="A")
-        tt(("tha", t + 1, t + 2), th, c(3), OP.add, "A")
-        ts(c(4), end, th, 16384.0, OP.is_ge, OP.mult, name="l0")
-        ts(("lo", 32, 64), (rp, P - L, P), c(4), -8192.0, OP.add, OP.add, name="l0")
+        op("N", None, [lout], [("land%d" % t, 0, 32)], 0.0, lat=COST["net"] + PLAN["pad"][t], name="recv", recv=t, pad=PLAN["pad"][t])
+        ts(("tha", t + 1, t + 2), end, -32.0, ("tha", t, t + 1), OP.mult, OP.add, name="A")
+        ts(c(4), end, 16384.0, 8192.0, OP.mult, OP.add, name="l0")
+        ts(("lo", 32, 64), (rp, P - L, P), c(4), None, OP.add, name="l0")
         tt(("lo", 0, 32), own, ("lo", 32, 64), OP.max, "l0")
 
     def moved(t, k, lo, hi, s):
@@ -471,69 +479,74 @@ def design():
         if n <= 0:
             return
         a3, c3, fs, js = ("%s_%d" % (x, s) for x in ("a3", "c3", "fs", "js"))
-        cn, sb = ("cnt", 128 + TW * (s % 2), 128 + TW * (s % 2) + n), "sub0" if last and not end else "sub1"
-        rp = "rp_%d" % z
+        cn, sb = place("cnt", 2 if sw == 64 else 1, 2, s, n), "sub" + PLAN["subs"][4 if last and not end else 3]
+        rp, rm, u = "rp_%d" % z, ("rm_%d" % z, lo, hi), "r2u_%d" % z
         rn = ("yrf", lo, hi) if last and not end else ("rn_%d" % y, lo, hi)
         if not end:
-            MK, df = ("pv", 256 + TW * s, 256 + TW * s + n), (fs, 7 * TW, 7 * TW + n)
-            tt(df, (rp, lo + L, hi + L), (rp, lo, hi), OP.subtract, "df")
-            ts(MK, ("rm_%d" % z, lo, hi), ("tha", t, t + 1), None, OP.is_lt, name="mk")
-            tt(MK, MK, df, OP.mult, "dm")
-            tt(rn, MK, (rp, lo, hi), OP.add, "R''")
+            df, ix = place("pv", 4 if sw == 64 else 3, 3 if sw == 64 else 2, s, n), (fs, 7 * TW, 7 * TW + n)
+            tt(ix, ("pv", 0, n), rm, OP.subtract, "ix")
+            ts((u, lo, hi), ix, 512.0, None, OP.mult, name="R''u")
+            tt(df, (rp, lo, hi), (rp, lo + L, hi + L), OP.subtract, "df")
+            tt(df, df, rm, OP.mult, "dm")
+            tt(rn, df, (rp, lo, hi), OP.add, "R''")
+            src = ("xp_%d" % z, 16 * lo, 16 * (hi + L))
         else:
             tt(("lx", 0, 32), ("land%d" % t, 0, 32), ("lo", 0, 32), OP.max, "l1")
             ts(rn, ("lx", 0, 32), W - 1, None, OP.bitwise_and, name="l2")
-        u = "r2u_%d" % z
-        copy((u, lo, hi), rn, "R''u")
+            copy((u, lo, hi), rn, "R''u")
+            src = FL
         if last and end:
             copy(("yrf", lo, hi), rn, "R f")
             x3, c4, c5 = (a3, 0, 16 * n), (c3, 0, 16 * n), (c3, 16 * n, 32 * n)
-            gtt(x3, FL, (u, lo, hi), ("xm", 16 * lo, 16 * hi), OP.subtract, "cand")
+            gtt(x3, src, (u, lo, hi), ("xm", 16 * lo, 16 * hi), OP.subtract, "cand")
             ts(c4, x3, ("epf", 0, 1), None, OP.is_le, name="c3")
             ts(c5, x3, ("epf", 1, 2), None, OP.is_ge, name="c3")
-            total(cn, [(c4, "b4096"), (c5, "b4096")], ("cz", TW), "cnt3", ("yrf", lo, hi))
+            total(cn, [(c4, "b4096"), (c5, "b4096")], ("cz", tw), ("yrf", lo, hi), "cnt3")
         else:
             xr = "xr_%d" % y
             for a, c in _cut(lo, hi, PLAN["plain"]):
-                gather((xr, 16 * a, 16 * c), FL, (u, a, c), "XR''")
+                gather((xr, 16 * a, 16 * c), src, (u, a, c), "XR''", PLAN["eng"][1])
             if not last:
                 rf = "rf_%d" % y
-                ts((rf, lo + 1, hi + 1), rn, 592.0, None, OP.add, name="rf")
+                ts((rf, lo + 1, hi + 1), rn, float(FO), None, OP.add, name="rf")
                 if lo == 0:
                     copy((rf, 0, 1), (rf, 1, 2), "rf0")
-            for a, c in _cut(lo, hi, 64):
-                x, h = (sb, 0, 16 * (c - a)), (16 * (a - lo), 16 * (c - lo))
-                if last or (t, k) in PLAN["acS"]:
+            sizes = (t, k) in PLAN["acS"]
+            for i, (a, c) in enumerate(_cut(lo, hi, 64 if sizes else PLAN["test"])):
+                h0 = BANK if PLAN["apart"] and not last else BANK * (i % 2) if c - a <= 32 else 0
+                x, h = (sb, h0, h0 + 16 * (c - a)), (16 * (a - lo), 16 * (c - lo))
+                if sizes:
                     sub(x, (xr, 16 * a, 16 * c), ("xm", 16 * a, 16 * c), "ac-")
                     absS((a3,) + h, x, "ac||")
                 else:
                     sub(x, (xr, 16 * a, 16 * c), ("xm", 16 * a, 16 * c), "ac-", "sgp", "sgn")
                     ts((c3,) + h, x, BIG, BIG, OP.add, OP.is_equal, name="ac=")
-            if last or (t, k) in PLAN["acS"]:
+            if sizes:
                 ts((c3, 0, 16 * n), (a3, 0, 16 * n), ("epf", 0, 1), None, OP.is_le, name="c3")
-            if last:
-                total(cn, [((c3, 0, 16 * n), "b4096")], ("cz", 0), "cnt3", rn)
+            if not PLAN["plus"]:
+                total(cn, [((c3, 0, 16 * n), "b4096")], ("cz", 0), None, "cnt3")
+                tt(cn, cn, rn, OP.add, "z3")
+            elif last:
+                total(cn, [((c3, 0, 16 * n), "b4096")], ("cz", 0), rn, "cnt3")
             else:
-                total(cn, [((c3, 0, 16 * n), "b4096")], ("cz", 2 * TW), "cnt3", ("rf_%d" % y, lo + 1, hi + 1))
+                total(cn, [((c3, 0, 16 * n), "b4096")], ("cz", 2 * tw), (rf, lo + 1, hi + 1), "cnt3")
         mm, mn = (js, 4 * TW, 4 * TW + n), ("mn_%d" % y, lo, hi)
         tt(mm, cn, ("mn_%d" % z, lo, hi), OP.max, "mm")
         ts(mn, mm, W - 1, None, OP.bitwise_and, name="M'")
         if last:
             copy(("ymf", lo, hi), mn, "M f")
             return
-        ts(("mf_%d" % y, lo, hi), mn, 592.0, None, OP.add, name="mf")
+        ts(("mf_%d" % y, lo, hi), mn, float(FO), None, OP.add, name="mf")
         mu = "mu_%d" % y
         copy((mu, lo, hi), mn, "M'u")
         for a, c in _cut(lo, hi, PLAN["plain"]):
-            gather(("xm", 16 * a, 16 * c), FL, (mu, a, c), "XM'")
+            gather(("xm", 16 * a, 16 * c), FL, (mu, a, c), "XM'", PLAN["eng"][2])
 
     def whole(j):
         t, k = tiles[j]
         final = TILES[t][k + 1] == P
         yield from step1(j)
         yield
-        if final:
-            before(j)
         necks(j)
         if final:
             loops(j)
@@ -542,7 +555,7 @@ def design():
             moved(t, k, *piece(j), j % NB)
         elif final:
             for i in range(k + 1):
-                moved(t, i, *piece(tiles.index((t, i))), (j + i + 1) % NB)
+                moved(t, i, *piece(j - k + i), (j + i + 1) % NB)
             moved(t, k + 1, P - L, P, (j + k + 2) % NB)
         yield
 
@@ -566,8 +579,7 @@ def design():
         upto(j, 1)
     for p in (2, 3, 4):
         upto(len(tiles) - 1, p)
-    tt(("aout", 0, 1), ("tha", ROUNDS, ROUNDS + 1), ("tha", 0, 1), OP.subtract)
-    ts(("aout", 1, 2), ("aout", 0, 1), 0.0625, None, OP.mult)
+    ts(("aout", 1, 2), ("tha", ROUNDS, ROUNDS + 1), ("tha", 0, 1), 1.0 / 32, OP.subtract, OP.mult)
     dma("Y", lambda T: T.ya[:], lambda T: T.aout[:, 1:2], [("aout", 1, 2)], [], "st ya")
     dma("Y", lambda T: T.yr[:, 0:224], lambda T: T.yrf[:, 0:224], [("yrf", 0, 224)], [], "st yr")
     dma("Y", lambda T: T.ym[:, 0:224], lambda T: T.ymf[:, 0:224], [("ymf", 0, 224)], [], "st ym")
@@ -582,8 +594,7 @@ def depend(ops):
         dep = set()
         touches = [(r, False) for r in o["rd"]] + [(r, True) for r in o["wr"]]
         for (buf, lo, hi), wr in touches:
-            lst = acc.setdefault(buf, [])
-            for (j, l2, h2, w2) in lst:
+            for (j, l2, h2, w2) in acc.setdefault(buf, []):
                 if j != i and lo < h2 and l2 < hi and (wr or w2):
                     dep.add(j)
         for (buf, lo, hi), wr in touches:
@@ -615,7 +626,8 @@ def lay(ops, rank, before, behind, back):
         return t
     while len(out) < len(ops):
         t, e = min((max(free[e], min(when(i, e) for i in ready[e])), e) for e in free if ready[e])
-        i = max((j for j in ready[e] if when(j, e) <= t), key=lambda j: (rank[j], j if back else -j))
+        i = max(ready[e], key=lambda j: (rank[j] - PLAN["haste"] * max(0.0, when(j, e) - t), j if back else -j))
+        t = max(t, when(i, e))
         o = ops[i]
         for x in o["eng"]:
             ready[x].remove(i)
@@ -627,7 +639,7 @@ def lay(ops, rank, before, behind, back):
         for b in o["banks"]:
             held.setdefault(b, {})[e] = t + dur + COST["wake"]
         for j in behind[i]:
-            at[j] = max(at[j], end + (ops[j]["lat"] if back else 0.0))
+            at[j] = max(at[j], end + (ops[j]["lat"] if back else 0.0) + (COST["same"] - COST["wake"] if ops[j]["eng"] == e else 0.0))
             left[j] -= 1
             if not left[j]:
                 for x in ops[j]["eng"]:
@@ -644,27 +656,52 @@ def arrange(ops):
     rank = [0.0] * n
     for i in range(n - 1, -1, -1):
         rank[i] = ops[i]["dur"] + ops[i]["lat"] + max([rank[j] for j in succ[i]], default=0.0)
-    best = None
-    for _ in range(PLAN["passes"]):
-        there = lay(ops, [rank[i] + BONUS.get(ops[i]["name"], 0.0) for i in range(n)], pred, succ, False)
-        if best is None or max(x[1] for x in there.values()) < max(x[1] for x in best.values()):
-            best = there
-        home = lay(ops, [there[i][1] for i in range(n)], succ, pred, True)
-        rank = [home[i][1] for i in range(n)]
+    best, rng = None, np.random.default_rng(PLAN["seed"])
+    kind_of = ["%s %d" % (o["name"], PLAN["parts"] * i // n) for i, o in enumerate(ops)]
+    first, kinds = rank, sorted(set(kind_of))
+    for turn in range(PLAN["passes"]):
+        if turn % 3 == 0:
+            lean = dict(best[4]) if best else {}
+            for kind in rng.choice(kinds, 3 * PLAN["parts"]) if best else ():
+                lean[kind] = lean.get(kind, 0.0) + float(rng.normal(0.0, PLAN["shake"]))
+            rank = list(first)
+        there = lay(ops, [rank[i] + lean.get(kind_of[i], 0.0) for i in range(n)], pred, succ, False)
+        seq = sorted(range(n), key=lambda i: there[i][3])
+        deps, last, fill = {}, {}, set()
+        for i in seq:
+            e, d = there[i][2], set(pred[i])
+            if e == "G" and ops[i]["f"]:
+                d, fill = d | fill, {i}
+            for b in ops[i]["banks"]:
+                d |= {j for x, j in last.setdefault(b, {}).items() if x != e}
+                last[b][e] = i
+            deps[i] = d
+        worth = sum(replay(ops, seq, there, deps, *x) for x in RANGE)
+        if best is None or worth < best[0]:
+            best = (worth, there, seq, deps, lean)
+        if turn % 3 < 2:
+            home = lay(ops, [there[i][1] for i in range(n)], succ, pred, True)
+            rank = [home[i][1] for i in range(n)]
     order = {e: [] for e in "VSPGYN"}
-    last = {}
-    for i in sorted(range(n), key=lambda i: best[i][3]):
+    for i in best[2]:
         o = ops[i]
-        o["t0"], o["on"] = best[i][0], best[i][2]
+        o["t0"], o["on"], o["dep"] = best[1][i][0], best[1][i][2], best[3][i]
         if o["on"] == "S" and "slow" in o:
             o["dur"] = o["slow"]
-        if o["on"] == "G" and o["f"]:
-            o["dep"] = o["dep"] | set([j for j in order["G"] if ops[j]["f"]][-1:])
         order[o["on"]].append(i)
-        for b in o["banks"]:
-            o["dep"] = o["dep"] | {j for x, j in last.setdefault(b, {}).items() if x != o["on"]}
-            last[b][o["on"]] = i
-    return order, max(x[1] for x in best.values())
+    return order, best[0]
+
+
+def replay(ops, seq, laid, deps, wake, same, ga, pe):
+    free, over = {}, {}
+    for i in seq:
+        o, e = ops[i], laid[i][2]
+        t = max([free.get(e, 0.0)] + [over[j] + (same - wake if laid[j][2] == e else 0.0) for j in deps[i]])
+        t += (o["slow"] if e == "S" and "slow" in o else o["dur"] * pe / COST["pe"] if e == "P" else o["dur"]) + o.get("picks", 0) * COST["cy"] * (ga - COST["ga"])
+        if e != "N":
+            free[e] = t
+        over[i] = t + (wake if o["lat"] == COST["wake"] else o["lat"] - o.get("pad", 0))
+    return max(over.values())
 
 
 _made = {}
@@ -779,12 +816,9 @@ def rank_program(g, core, T, topo):
                 job = o["fold"]
                 dst = helpers(core, T, topo)[job["helper"]]
                 rid, pid, _ = topo.addr(dst)
-                eng, (buf, at, end) = topo.engines(core, dst), job["stage"]
-                share, n = len(eng) // len(job["pairs"]), (end - at) // len(job["pairs"])
-                g.remote_dma_fused([RemoteDMATransfer(
-                    dst_ids=[DstId(rid=rid, pnc=pid)], dma_engine_mask=sum(1 << x for x in eng[share * p:share * (p + 1)]),
-                    remote_sem=T.sem["there_" + job["out"][0]], srcs=[_ap(T, a), _ap(T, b)], dsts=[T[buf][:, at + n * p:at + n * (p + 1)]],
-                    alu_op=2) for p, (a, b) in enumerate(job["pairs"])], local_sem=T.sem["left_" + job["out"][0]])
+                g.remote_dma_fused([RemoteDMATransfer(dst_ids=[DstId(rid=rid, pnc=pid)], dma_engine_mask=topo.mask(core, dst),
+                                                      remote_sem=T.sem["there_" + job["out"][0]], srcs=[_ap(T, job["a"]), _ap(T, job["b"])],
+                                                      dsts=[_ap(T, job["stage"])], alu_op=2)], local_sem=T.sem["left_" + job["out"][0]])
             elif "dma" in o:
                 o["f"](q, T).then_inc(T.sem[o["dma"]], 16)
             elif "flex" in o:

@@ -1,5 +1,4 @@
 import numpy as np
-from concourse.bass import DstId, RemoteDMATransfer
 from concourse.mybir import dt, AluOpType, AxisListType, ActivationFunctionType
 
 OP = AluOpType
@@ -9,22 +8,21 @@ TW = 64
 CE = 16 * TW
 FO = 592
 BANK = 512
-NB = 3
+FREE = 4
+NB = 4
 BIG = 12582912.0
 
 _F, _B, _I, _U, _H = "float32", "bfloat16", "int32", "uint16", "float16"
 SCRATCH = {
     "fl": ("sbuf", [128, FO + W], _B), "xm": ("sbuf", [128, 4096], _B),
     "ones": ("sbuf", [128, 128], _B), "ident": ("sbuf", [128, 128], _B), "nident": ("sbuf", [128, 128], _B),
-    "identf": ("sbuf", [128, 128], _F), "sgp": ("sbuf", [128, 128], _H), "sgn": ("sbuf", [128, 128], _H),
+    "identf": ("sbuf", [128, 128], _F), "sgp": ("sbuf", [128, 128], _H),
     "g8": ("sbuf", [128, 8], _B), "g8b": ("sbuf", [128, 8], _B),
     "b1": ("sbuf", [128, 144], _B), "b2": ("sbuf", [128, 144], _B), "b4096": ("sbuf", [128, 144], _B),
-    "bn8192": ("sbuf", [128, 144], _B), "bn2": ("sbuf", [128, 144], _B), "b4": ("sbuf", [128, 144], _B),
-    "ident2": ("sbuf", [128, 128], _B), "zero": ("sbuf", [128, 2 * CE], _B),
     "b8192": ("sbuf", [128, 144], _B), "b16384": ("sbuf", [128, 144], _B),
-    "ck": ("sbuf", [128, 5 * TW], _B), "cy": ("sbuf", [128, 3 * TW], _B), "cz": ("sbuf", [128, 3 * TW], _B),
+    "ck": ("sbuf", [128, 5 * TW], _B), "cy": ("sbuf", [128, 3 * TW], _B), "cz": ("sbuf", [128, 2 * TW], _B),
     "iot": ("sbuf", [128, 32], _F), "i16": ("sbuf", [128, TW], _F), "neg": ("sbuf", [128, TW], _F), "thb": ("sbuf", [128, 3 * TW], _F),
-    "ipt": ("sbuf", [128, 2], _I), "ipf": ("sbuf", [128, 2], _F), "cpos": ("sbuf", [128, 2 * TW], _F),
+    "ipt": ("sbuf", [128, 2], _I), "ipf": ("sbuf", [128, 2], _F), "cpos": ("sbuf", [128, TW], _F),
     "dgj": ("sbuf", [128, 512], _F), "diag": ("sbuf", [128, 512], _F), "seg": ("sbuf", [128, 512], _F),
     "thi": ("sbuf", [128, 1], _I), "epi": ("sbuf", [128, 1], _I), "epf": ("sbuf", [128, 8], _F),
     "tha": ("sbuf", [128, 8], _F), "nk": ("sbuf", [128, 32], _F), "aout": ("sbuf", [128, 4], _F),
@@ -33,7 +31,7 @@ SCRATCH = {
     "lo": ("sbuf", [128, 64], _F), "lx": ("sbuf", [128, 64], _I),
     "yrf": ("sbuf", [128, 256], _F), "ymf": ("sbuf", [128, 256], _F),
     "pv": ("psum", [128, 512], _F), "sc": ("psum", [128, 1024], _F),
-    "cnt": ("psum", [128, 512], _F), "sub0": ("psum", [128, 1024], _F), "sub1": ("psum", [128, 1024], _F),
+    "cnt": ("psum", [128, 512], _F), "sub": ("psum", [128, FREE * BANK], _F),
 }
 for _k in range(3):
     SCRATCH["lout%d" % _k] = ("sbuf", [128, 32], _F)
@@ -45,47 +43,36 @@ for _k in range(2):
 for _k in range(NB):
     for _n, _c, _d in (("pr", 4 * TW, _I), ("v", 4 * TW, _I), ("u", 4 * TW, _U), ("fs", 8 * TW, _F), ("js", 5 * TW, _I), ("ou", TW, _U),
                        ("win", 5 * CE, _B), ("now", CE, _B), ("nb", CE, _B), ("a2", CE, _B), ("a3", CE, _B), ("c3", CE, _B),
-                       ("aw", CE, _B), ("hb", 2 * CE, _B)):
+                       ("hb", 4 * CE, _B)):
         SCRATCH[_n + "_%d" % _k] = ("sbuf", [128, _c], _d)
-NDMA = 11
-HELPERS = 3
-STAGE = ["win_%d" % k for k in range(NB)] + ["xm", "xp_0", "xp_1", "xr_0", "xr_1"]
-FOLDED = [x + "_%d" % k for x in ("now", "hb", "a2") for k in range(NB)]
-SEMAPHORES = (["sV", "sS", "sP", "sG", "ls", "arr0", "arr1", "arr2"] + ["d%d" % k for k in range(NDMA)]
-              + [x + b for b in FOLDED for x in ("left_", "there_", "back_")])
+NDMA = 130
+SEMAPHORES = ["sV", "sS", "sP", "sG", "ls", "arr0", "arr1", "arr2"] + ["d%d" % k for k in range(NDMA)]
 
 COST = {"cy": 0.000833, "ga": 1.48, "pe": 0.00058, "v": 0.01, "s": 0.06, "wake": 0.18, "same": 0.26, "net": 5.5,
-        "issue": 1.0, "hop": 2.0, "dma": 200e3}
+        "issue": 0.8, "hop": 1.5, "dma": 250e3, "add": 1.1}
 TILES = ((0, 64, 128, 192, 256), (0, 64, 128, 192, 256), (0, 64, 128, 192, 256))
 PLAN = {
     "cand": (32, 32, 32, 32, 32),
-    "pair": (0, 0),
-    "viaS": (),
-    "via": "sub0",
+    "mode": (("aaaaT", "hhgae", "hhgae", "hhgae"), ("hhgae", "hhgae", "hhgae", "hhgae"), ("hhgae", "hhgae", "hhgae", "aaaaT")),
+    "pair": 0,
+    "join": 0,
+    "half": 1,
     "plain": 64,
     "tail": 1,
     "acS": ((2, 0), (2, 1), (2, 2), (2, 3)),
     "first": "SVV",
     "me": "S",
-    "subs": "00110",
-    "test": 32,
-    "apart": 0,
-    "pad": (0, 0, 0),
-    "haste": 1e6,
-    "parts": 1,
-    "plus": 0,
-    "relu": ("......", "......", "......"),
-    "now": ("DDDD", "DDDD", "DDDD"),
-    "neck": ("......", "......", "......"),
-    "near": 32,
+    "wide": (32, 32, 32, 32, 32),
+    "haste": 30.0,
     "eng": ("S", "S", "S", "S"),
     "split": 2,
-    "lag": (2, 3, 8),
-    "passes": 270,
+    "lag": (3, 4, 8),
+    "passes": 400,
     "seed": 1,
-    "shake": 2.0,
+    "shake": 0.9,
 }
-RANGE = ((0.2, 0.26, 1.47, 0.00042), (0.15, 0.25, 1.9, 0.00042), (0.15, 0.25, 1.3, 0.0008), (0.15, 0.25, 1.6, 0.0007))
+RANGE = ((0.2, 0.26, 1.47, 0.00042, 1.0), (0.15, 0.25, 1.9, 0.00042, 1.3), (0.15, 0.25, 1.3, 0.0008, 1.0), (0.15, 0.25, 1.6, 0.0007, 0.8))
+LENT = {}
 
 
 def _span(r):
@@ -93,6 +80,9 @@ def _span(r):
 
 
 def _ap(T, r):
+    if r[0][0] == "#":
+        at = BANK * LENT.get(r[0], 0)
+        return T.sub[:, at + r[1]:at + r[2]]
     if len(r) == 4:
         return T[r[0]][:, r[1]:r[2]:r[3]]
     return T[r[0]][:, r[1]:r[2]]
@@ -103,7 +93,7 @@ def _count(r):
 
 
 def _psum(name):
-    return SCRATCH[name][0] == "psum" if name in SCRATCH else False
+    return SCRATCH[name][0] == "psum" if name in SCRATCH else name[0] == "#"
 
 
 def _cut(lo, hi, w):
@@ -128,7 +118,7 @@ def design():
 
     def ts(out, a, s1, s2, op0, op1=None, name="ts"):
         aps = [s for s in (s1, s2) if isinstance(s, tuple)]
-        two = all(SCRATCH[r[0]][2] in (_B, _U, _H) for r in (out, a))
+        two = all(not _psum(r[0]) and SCRATCH[r[0]][2] in (_B, _U, _H) for r in (out, a))
 
         def f(q, T):
             x1 = _ap(T, s1) if isinstance(s1, tuple) else s1
@@ -156,11 +146,12 @@ def design():
         op("V", lambda q, T: q.tensor_tensor(_ap(T, out), _ap(T, win).indirect(_ap(T, off)), _ap(T, b), alu), [win, off, b], [out],
            VF + 0.03 + CY * GA * _count(out), name=name, picks=_count(out))
 
-    def gather(out, win, off, name, eng="S"):
+    def gather(out, win, off, name, eng="S", sign=1.0):
         def f(q, T, e):
-            if e == "V":
-                return q.tensor_copy(_ap(T, out), _ap(T, win).indirect(_ap(T, off)))
-            return q.activation(_ap(T, out), _ap(T, win).indirect(_ap(T, off)), ACT.Copy)
+            x = _ap(T, win).indirect(_ap(T, off))
+            if e == "S":
+                return q.activation(_ap(T, out), x, ACT.Copy, scale=sign)
+            return q.tensor_copy(_ap(T, out), x) if sign == 1.0 else q.tensor_scalar(_ap(T, out), x, sign, None, OP.mult)
         op(eng, f, [win, off], [out], 0.06 + CY * GA * _count(out), name=name, flex=True, picks=_count(out))
 
     def absS(out, a, name):
@@ -173,18 +164,18 @@ def design():
             return q.activation(_ap(T, out), _ap(T, a), ACT.Identity, bias=y, scale=x)
         op(eng, f, [a], [out], VF + CY * max(64, _count(out)), name=name, flex=True, slow=SF + CY * _count(out))
 
-    def mix(out, terms, name):
+    def sub(a, b, name, plus="ident", minus="nident"):
+        n = _count(a)
+        out = ("#%d" % len(ops), 0, n)
+
         def f(q, T):
-            n = out[2] - out[1]
             for s in range(0, n, BANK):
                 e = min(n, s + BANK)
-                for j, (a, dg) in enumerate(terms):
-                    i = q.matmul(T[out[0]][:, out[1] + s:out[1] + e], T[dg][:], T[a[0]][:, a[1] + s:a[1] + e], j == 0, j == len(terms) - 1)
+                q.matmul(_ap(T, (out[0], s, e)), T[plus][:], T[a[0]][:, a[1] + s:a[1] + e], True, False)
+                i = q.matmul(_ap(T, (out[0], s, e)), T[minus][:], T[b[0]][:, b[1] + s:b[1] + e], False, True)
             return i
-        op("P", f, [a for a, _ in terms] + [(dg, 0, 128) for _, dg in terms], [out], PEC * len(terms) * _count(out), name=name)
-
-    def sub(out, a, b, name, plus="ident", minus="nident"):
-        mix(out, [(a, plus), (b, minus)], name)
+        op("P", f, [a, b, (plus, 0, 128), (minus, 0, 128)], [out], PEC * 2 * n, name=name, lend=-(-n // BANK))
+        return out
 
     def total(out, terms, const, plus, name):
         n = out[2] - out[1]
@@ -199,28 +190,22 @@ def design():
         op("P", f, [x for x, _ in terms] + [(wb, 0, 144) for _, wb in terms] + [x for _, x in first] + [(m, 0, 128) for m, _ in first], [out],
            PEC * max(64, n) * (16 * len(terms) + (1 if const else 0) + (4 if plus else 0)), name=name)
 
-    uses = {}
-    room = [[[b, 0] for b in STAGE] for _ in range(HELPERS)]
-
-    def fold(out, a, b, name):
-        n, h = out[2] - out[1], FOLDED.index(out[0]) % HELPERS
-        uses[out[0]] = uses.get(out[0], 0) + 1
-        while room[h][0][1] + n > SCRATCH[room[h][0][0]][1][1]:
-            room[h].pop(0)
-        at = room[h][0]
-        stage = (at[0], at[1], at[1] + n)
-        at[1] += n
-        move = n * 256 / COST["dma"]
-        job = {"out": out, "a": a, "b": b, "stage": stage, "helper": h, "count": uses[out[0]]}
-        op("G", None, [a, b], [out], max(COST["issue"], 2 * move), lat=COST["hop"], name=name, fold=job)
-        op("N", None, [], [out], 0.0, lat=COST["issue"] + COST["hop"] + move, name="back", back=job)
-
     nd = [0]
 
     def dma(q, fo, fi, rd, wr, name, nbytes=0):
         k = nd[0]
         nd[0] += 1
-        op(q, lambda e, T: e.dma_start(fo(T), fi(T)), rd, wr, 0.06, lat=2.0 + nbytes / 200e3, name=name, dma="d%d" % k)
+        op(q, lambda e, T: e.dma_start(fo(T), fi(T)), rd, wr, COST["issue"] if q == "G" else 0.06, lat=2.0 + nbytes / 200e3, name=name, dma="d%d" % k)
+
+    def carry(out, a, add, name):
+        k = nd[0]
+        nd[0] += 1
+        move = 256 * _count(out) / COST["dma"] * (COST["add"] if add else 1.0)
+        if add:
+            op("G", lambda e, T: e.dma_start(_ap(T, out), _ap(T, a), accum_op=OP.add), [a, out], [out], COST["issue"], lat=COST["hop"] + move,
+               name=name, dma="d%d" % k, move=move)
+        else:
+            op("Y", lambda e, T: e.dma_start(_ap(T, out), _ap(T, a)), [a], [out], 0.06, lat=COST["hop"] + move, name=name, dma="d%d" % k, move=move)
 
     def iota(out, pat, base, cm, rows=(0, 128)):
         def f(q, T):
@@ -235,17 +220,15 @@ def design():
         op("G", lambda q, T: q.affine_select(part(T, out), part(T, a), pat, cmp, 0.0, base, cm), [a], [out],
            0.17 + WAKE + 2 * CY * _count(out), name="asel")
 
-    widths = {b - a for x in TILES for a, b in zip(x, x[1:])}
-    tw = max(widths)
-    sw = 64 if tw <= 64 else TW
-    place = lambda bank, first, count, j, n: (bank, sw * (first + j % count), sw * (first + j % count) + n)
+    tw = TW
+    place = lambda bank, first, count, j, n: (bank, TW * (first + j % count), TW * (first + j % count) + n)
 
     dma("S", lambda T: T.fl[:, FO:FO + W], lambda T: T.flood[:], [], [("fl", FO, FO + W)], "ld flood", 524288)
     dma("Y", lambda T: T["rn_0"][:, 0:P], lambda T: T.riv[:], [], [("rn_0", 0, P)], "ld riv", 131072)
     dma("Y", lambda T: T["mn_0"][:, 0:P], lambda T: T.bord[:], [], [("mn_0", 0, P)], "ld bord", 131072)
     dma("S", lambda T: T.fl[:, 0:FO], lambda T: T.flood[:, W - FO:W], [], [("fl", 0, FO)], "ld flood2", 700000)
     dma("Y", lambda T: T.thi[:], lambda T: T.th[:], [], [("thi", 0, 1)], "ld th")
-    dma("Y", lambda T: T.epi[:], lambda T: T.eps[:], [], [("epi", 0, 1)], "ld eps")
+    dma("G", lambda T: T.epi[:], lambda T: T.eps[:], [], [("epi", 0, 1)], "ld eps")
 
     memset("ones", 0, 128, 1.0)
     iota(("ipt", 0, 2), [[0, 2]], 0, 1)
@@ -271,14 +254,12 @@ def design():
     for t in range(ROUNDS):
         iota(("cy", tw * t, tw * t + tw), [[0, tw]], cons[t] // 32, 0, (64, 96))
         asel(("cy", tw * t, tw * t + tw), ("ones", 0, tw), [[0, tw]], OP.is_gt, cons[t] % 32, -1, (96, 128))
-    iota(("cz", 0, 3 * tw), [[0, 3 * tw]], -544, 0, (0, 64))
+    iota(("cz", 0, 2 * tw), [[0, 2 * tw]], -544, 0, (0, 64))
     iota(("cz", 0, 2 * tw), [[-1024, 2], [0, tw]], 0, 0, (64, 128))
-    memset("cz", 2 * tw, 3 * tw, -FO / 64.0, 64, 128)
     ts(("ipt", 1, 2), ("ipt", 0, 1), 15, None, OP.bitwise_and)
     copy(("ipf", 0, 1), ("ipt", 1, 2))
     ts(("pv", 0, tw), ("i16", 0, tw), ("ipf", 0, 1), 1.0 / 512, OP.add, OP.mult)
-    for wide in {n > 64 for n in widths}:
-        ts(("cpos", TW * wide, TW * wide + tw), ("pv", 0, tw), 8.0 * (1 + wide), None, OP.add)
+    ts(("cpos", 0, tw), ("pv", 0, tw), 8.0, None, OP.add)
     ts(("diag", 0, 512), ("dgj", 0, 512), ("ipf", 0, 1), None, OP.is_equal)
     ts(("tha", 0, 1), ("thi", 0, 1), 2.0, -1.0, OP.mult, OP.add)
     copy(("epf", 0, 1), ("epi", 0, 1))
@@ -286,7 +267,6 @@ def design():
     ts(("epf", 2, 3), ("epi", 0, 1), 2.0, 1.0, OP.mult, OP.add)
     op("V", lambda q, T: q.reciprocal(T.epf[:, 3:4], T.epf[:, 2:3]), [("epf", 2, 3)], [("epf", 3, 4)], 0.25, name="recip")
     ts(("sgp", 0, 128), ("ident", 0, 128), ("epf", 3, 4), None, OP.mult)
-    ts(("sgn", 0, 128), ("nident", 0, 128), ("epf", 3, 4), None, OP.mult)
     for k in range(2):
         for buf, lo, hi, val in (("rf", 257, 264, FO), ("mf", 256, 264, FO), ("rp", 256, 264, 0), ("rm", 0, 1, 0), ("xr", 4096, 4112, 0)):
             iota(("%s_%d" % (buf, k), lo, hi), [[0, hi - lo]], val, 0)
@@ -302,7 +282,7 @@ def design():
     ts(("mf_0", 0, 256), ("mn_0", 0, 256), float(FO), None, OP.add)
     copy(("mu_0", 0, P), ("mn_0", 0, P), "M u16")
     for lo, hi in zip(TILES[0][:-1], TILES[0][1:]):
-        gather(("xm", 16 * lo, 16 * hi), FL, ("mu_0", lo, hi), "XM0", PLAN["eng"][3])
+        gather(("xm", 16 * lo, 16 * hi), FL, ("mu_0", lo, hi), "XM0", PLAN["eng"][3], -1.0)
 
     tiles = [(t, k) for t in range(ROUNDS) for k in range(len(TILES[t]) - 1)]
     written = [np.zeros(5 * CE, bool) for _ in range(NB)]
@@ -314,65 +294,66 @@ def design():
         late = j >= len(tiles) - PLAN["tail"]
         z = t % 2
         rn, rf, mn, mf, xr, xp = ("%s_%d" % (x, z) for x in ("rn", "rf", "mn", "mf", "xr", "xp"))
-        pr, v, u, fs, js, ou, win, now, nb = ("%s_%d" % (x, j % NB) for x in ("pr", "v", "u", "fs", "js", "ou", "win", "now", "nb"))
-        s0 = (0, BANK - 2 * n, 2 * BANK - 5 * n)[j % 3] if sw == 64 else BANK * (j % 2)
+        pr, v, u, fs, js, ou, win, now, nb, hb = ("%s_%d" % (x, j % NB) for x in ("pr", "v", "u", "fs", "js", "ou", "win", "now", "nb", "hb"))
+        s0 = (0, BANK - 2 * n, 2 * BANK - 5 * n)[j % 3]
         S = lambda a, b=1: ("sc", s0 + a * n, s0 + (a + b) * n)
         F = lambda a, b=1: (fs, a * TW, a * TW + b * n)
         J = lambda a: (js, a * TW, a * TW + n)
-        wide = n > 64
-        slot = 2048 if wide else 1024
-        R16 = place("pv", 1, 3 if sw == 64 else 2, j, n)
+        X = lambda m, b=1: (win, CE * m, CE * (m + b - 1) + 16 * n)
+        R16 = place("pv", 1, 3, j, n)
         ts(R16, (rn, c0, c1), 16.0, None, OP.add, name="R16")
         for m, (bf, o) in enumerate(((rf, c0), (rf, c0 + 2), (mf, c0), (mf, c0 + 1))):
             tt((pr, n * m, n * m + n), R16, (bf, o, o + n), OP.mult, name="prod")
         for h0, h1 in ((0, 2 * n), (2 * n, 4 * n)) if PLAN["split"] == 2 or late else ((0, 4 * n),):
             ts((v, h0, h1), (pr, h0, h1), 4, W - 1, OP.arith_shift_right, OP.bitwise_and, name="v")
             ts((u, h0, h1), (v, h0, h1), 77.0 * t, None, OP.add, name="u")
-        signed = PLAN["relu"][t][k] != "."
-        relu = int(PLAN["relu"][t][k]) if signed else 0
-        far = signed and PLAN["now"][t][k] == "D"
-        hb, aw = "hb_%d" % (j % NB), "aw_%d" % (j % NB)
-        if far:
-            fold((now, 0, 16 * n), (xr, 16 * c0, 16 * c1), (xr, 16 * c0 + 16, 16 * c1 + 16), "now^")
-        for src, dst, at, name in ((xr, now, 0, "now"), ("xm", win, 4 * slot, "c5"))[signed:]:
-            for a, c in _cut(c0, c1, 64):
-                x = ("sub" + PLAN["subs"][name == "c5"], 0, 16 * (c - a))
-                sub(x, (src, 16 * a, 16 * c), (xr, 16 * a + 16, 16 * c + 16), name + "-")
-                absS((dst, at + 16 * (a - c0), at + 16 * (c - c0)), x, name + "||")
-        for m in range(4):
-            x = (win, slot * m, slot * m + 16 * n)
-            if m == 0 and j in PLAN["viaS"]:
-                gather(x, FC, (u, 0, n), "c1")
-                sub((PLAN["via"], 0, 16 * n), x, (xr, 16 * (c0 + 1), 16 * (c1 + 1)), "c1-")
-                absS(x, (PLAN["via"], 0, 16 * n), "c1||")
-                continue
-            for a, c in _cut(0, n, PLAN["cand"][m]):
-                gtt((win, slot * m + 16 * a, slot * m + 16 * c), FC, (u, n * m + a, n * m + c),
-                    (xr, 16 * (c0 + a + 1), 16 * (c0 + c + 1)), OP.subtract, "cand")
-            pair = 16 * n == slot and not late and PLAN["pair"][m // 2] and not (m < 2 and (j in PLAN["viaS"] or relu))
-            if m < relu:
-                if m == relu - 1:
-                    fold((hb, 0, slot * relu), (win, 0, slot * relu), ("zero", 0, slot * relu), "relu^")
-            elif not pair:
-                absS(x, x, "cand||")
-            elif m % 2:
-                x = (win, slot * (m - 1), slot * (m + 1))
-                absS(x, x, "cand||")
+        mode = PLAN["mode"][t][k]
+        nxt = (xr, 16 * (c0 + 1), 16 * (c1 + 1))
+        for a, c in _cut(c0, c1, PLAN["wide"][0]):
+            absS((now, 16 * (a - c0), 16 * (c - c0)), sub((xr, 16 * a, 16 * c), (xr, 16 * a + 16, 16 * c + 16), "now-"), "now||")
+        for m in (4, 0, 1, 2, 3):
+            if mode[m] == "T":
+                for a, c in _cut(c0, c1, PLAN["wide"][1]):
+                    x = sub(("xm", 16 * a, 16 * c), (xr, 16 * a + 16, 16 * c + 16), "c5-", "ident", "ident")
+                    absS((win, CE * m + 16 * (a - c0), CE * m + 16 * (c - c0)), x, "c5||")
+            elif m == 4:
+                carry(X(m), nxt, False, "c5=")
+                carry(X(m), ("xm", 16 * c0, 16 * c1), True, "c5+")
+            elif mode[m] in "eh":
+                gather(X(m), FC, (u, n * m, n * m + n), "candS", "S", -1.0)
+                carry(X(m), nxt, True, "+next")
+            else:
+                for a, c in _cut(0, n, PLAN["cand"][m]):
+                    gtt((win, CE * m + 16 * a, CE * m + 16 * c), FC, (u, n * m + a, n * m + c),
+                        (xr, 16 * (c0 + a + 1), 16 * (c0 + c + 1)), OP.subtract, "cand")
+        m, at = 0, 0
+        while m < 5:
+            far = mode[m] in "gh"
+            b = 1 + (m < 4 and n == TW and mode[m] != "T" and mode[m + 1] != "T" and far == (mode[m + 1] in "gh")
+                     and PLAN["join" if far else "pair"] and not late)
+            if far:
+                h = (hb, at, at + _count(X(m, b)))
+                at = h[2]
+                if PLAN["half"]:
+                    for i in range(b):
+                        ts((hb, h[1] + i * CE, h[1] + i * CE + 16 * n), X(m + i), -2.0, 0.0, OP.mult, OP.max, name="relu")
+                else:
+                    ts(h, X(m, b), -2.0, 0.0, OP.mult, OP.max, name="relu")
+                carry(X(m, b), h, True, "+relu")
+            elif mode[m] != "T":
+                absS(X(m, b), X(m, b), "cand||")
+            m += b
         seen = written[j % NB]
         for m in range(5):
-            seen[slot * m:slot * m + 16 * n] = True
+            seen[CE * m:CE * m + 16 * n] = True
         for m in range(4):
-            gap = np.flatnonzero(~seen[slot * m:slot * (m + 1)])
+            gap = np.flatnonzero(~seen[CE * m:CE * (m + 1)])
             if len(gap):
-                a, c = slot * m + int(gap[0]), slot * m + int(gap[-1]) + 1
+                a, c = CE * m + int(gap[0]), CE * m + int(gap[-1]) + 1
                 iota((win, a, c), [[0, c - a]], 0, 0)
                 seen[a:c] = True
         for m in (4, 0, 1, 2, 3):
-            x = (win, slot * m, slot * m + 16 * n)
-            if m < relu:
-                total(S(m), [(x, "bn8192"), ((hb, slot * m, slot * m + 16 * n), "b16384")], ("ck", tw * m), None, "score")
-            else:
-                total(S(m), [(x, "b8192")], ("ck", tw * m), None, "score")
+            total(S(m), [(X(m), "b8192")], ("ck", tw * m), None, "score")
         kb, kc, w, o, me, d = F(0, 2), F(2), F(3), F(4), F(5), F(6)
         k4, ka, kv, rr = J(0), J(1), J(2), J(3)
         tt(S(0, 2), S(0, 2), (v, 0, 2 * n), OP.add, "key")
@@ -383,34 +364,20 @@ def design():
         tt(S(0), S(4), k4, OP.is_le, "m5")
         ts(kv, k4, W - 1, None, OP.bitwise_and, name="kv")
         scale(me, (mf, c0, c1), 1.0, 4096.0 - cons[t] - FO, "me", PLAN["me"])
-        ts(ka, k4, 6144, 10 - wide, OP.bitwise_and, OP.arith_shift_right, name="ka")
-        tt(S(1), S(0), ("cpos", TW * wide, TW * wide + n), OP.mult, "uu")
+        ts(ka, k4, 6144, 10, OP.bitwise_and, OP.arith_shift_right, name="ka")
+        tt(S(1), S(0), ("cpos", 0, n), OP.mult, "uu")
         tt(w, ("pv", 0, n), ka, OP.add, "w")
         tt(o, S(1), w, OP.max, "o")
         ts((ou, 0, n), o, 512.0, None, OP.mult, name="ou")
         tt(S(2), S(0), me, OP.mult, "t5")
         tt(d, S(2), kv, OP.max, "d")
         yield
-        whole = (win, 0, 4 * slot + 16 * n)
-        for i, (a, c) in enumerate(_cut(0, n, PLAN["near"] if signed else 32 if late else PLAN["cand"][4])):
-            h = (16 * a, 16 * c)
-            if not signed:
-                gtt((nb,) + h, whole, (ou, a, c), (now,) + h, OP.is_lt, "nearer")
-                continue
-            op("S", lambda q, T, a=a, c=c, h=h: q.activation(_ap(T, (aw,) + h), _ap(T, whole).indirect(_ap(T, (ou, a, c))), ACT.Abs),
-               [whole, (ou, a, c)], [(aw,) + h], 0.06 + CY * GA * (h[1] - h[0]), name="nearer", picks=h[1] - h[0])
-            h0 = BANK * (i % 2) if c - a <= 32 else 0
-            x = ("sub" + PLAN["subs"][0], h0, h0 + h[1] - h[0])
-            r0, r1 = (xr, 16 * (c0 + a), 16 * (c0 + c)), (xr, 16 * (c0 + a + 1), 16 * (c0 + c + 1))
-            if far:
-                mix(x, [(r0, "nident"), (r1, "nident"), ((now,) + h, "ident2")], "now-")
-            else:
-                sub(x, r0, r1, "now-")
-                absS(x, x, "now||")
-            tt((nb,) + h, x, (aw,) + h, OP.is_gt, "near<")
-        Z = place("cnt", 4, 3, j, n) if sw == 64 else place("cnt", 3, 2, j, n)
-        total(Z, [((nb, 0, 16 * n), "b16384")], ("cy", tw * t), d if late or PLAN["plus"] else None, "cnt1")
-        if not (late or PLAN["plus"]):
+        whole = (win, 0, 4 * CE + 16 * n)
+        for a, c in _cut(0, n, 32 if late else PLAN["cand"][4]):
+            gtt((nb, 16 * a, 16 * c), whole, (ou, a, c), (now, 16 * a, 16 * c), OP.is_lt, "nearer")
+        Z = place("cnt", 4, 3, j, n)
+        total(Z, [((nb, 0, 16 * n), "b16384")], ("cy", tw * t), d if late else None, "cnt1")
+        if not late:
             tt(Z, Z, d, OP.add, "z")
         tt(rr, Z, (rn, c0, c1), OP.max, "rr")
         rp, rpu = "rp_%d" % z, "rpu_%d" % z
@@ -436,18 +403,10 @@ def design():
         late = j >= len(tiles) - PLAN["tail"]
         xp, rm, a2 = "xp_%d" % (t % 2), "rm_%d" % (t % 2), "a2_%d" % (j % NB)
         n = hi - lo
-        ds = place("cnt", 0, 2 if sw == 64 else 1, j, n)
-        if PLAN["neck"][t][k] == "D":
-            x, y = (xp, 16 * lo, 16 * hi), (xp, 16 * (lo + L), 16 * (hi + L))
-            fold((a2, 0, 16 * n), x, y, "nk^")
-            total(ds, [(x, "bn2"), (y, "bn2"), ((a2, 0, 16 * n), "b4")], None, ("thb", TW * t, TW * t + n), "dist")
-        else:
-            for i, (a, c) in enumerate(_cut(lo, hi, 32 if late or PLAN["apart"] else 64)):
-                h0 = BANK * (i % 2) if late else 0
-                x = ("sub" + PLAN["subs"][2], h0, h0 + 16 * (c - a))
-                sub(x, (xp, 16 * a, 16 * c), (xp, 16 * (a + L), 16 * (c + L)), "nk-")
-                absS((a2, 16 * (a - lo), 16 * (c - lo)), x, "nk||")
-            total(ds, [((a2, 0, 16 * n), "b2")], None, ("thb", TW * t, TW * t + n), "dist")
+        ds = place("cnt", 0, 2, j, n)
+        for a, c in _cut(lo, hi, 32 if late else PLAN["wide"][2]):
+            absS((a2, 16 * (a - lo), 16 * (c - lo)), sub((xp, 16 * a, 16 * c), (xp, 16 * (a + L), 16 * (c + L)), "nk-"), "nk||")
+        total(ds, [((a2, 0, 16 * n), "b2")], None, ("thb", TW * t, TW * t + n), "dist")
         scan((rm, 1 + lo, 1 + hi), ds, ("neg", 0, n), (rm, lo, lo + 1), OP.min, OP.max, "rm")
 
     def loops(j):
@@ -466,7 +425,7 @@ def design():
         own = ("ls", 15, 512, 16)
         ts(lout, own, c(2), None, OP.add, name="lout")
         op("G", None, [lout], [], 1.0, name="send", send=t)
-        op("N", None, [lout], [("land%d" % t, 0, 32)], 0.0, lat=COST["net"] + PLAN["pad"][t], name="recv", recv=t, pad=PLAN["pad"][t])
+        op("N", None, [lout], [("land%d" % t, 0, 32)], 0.0, lat=COST["net"], name="recv", recv=t)
         ts(("tha", t + 1, t + 2), end, -32.0, ("tha", t, t + 1), OP.mult, OP.add, name="A")
         ts(c(4), end, 16384.0, 8192.0, OP.mult, OP.add, name="l0")
         ts(("lo", 32, 64), (rp, P - L, P), c(4), None, OP.add, name="l0")
@@ -479,11 +438,11 @@ def design():
         if n <= 0:
             return
         a3, c3, fs, js = ("%s_%d" % (x, s) for x in ("a3", "c3", "fs", "js"))
-        cn, sb = place("cnt", 2 if sw == 64 else 1, 2, s, n), "sub" + PLAN["subs"][4 if last and not end else 3]
+        cn = place("cnt", 2, 2, s, n)
         rp, rm, u = "rp_%d" % z, ("rm_%d" % z, lo, hi), "r2u_%d" % z
         rn = ("yrf", lo, hi) if last and not end else ("rn_%d" % y, lo, hi)
         if not end:
-            df, ix = place("pv", 4 if sw == 64 else 3, 3 if sw == 64 else 2, s, n), (fs, 7 * TW, 7 * TW + n)
+            df, ix = place("pv", 4, 3, s, n), (fs, 7 * TW, 7 * TW + n)
             tt(ix, ("pv", 0, n), rm, OP.subtract, "ix")
             ts((u, lo, hi), ix, 512.0, None, OP.mult, name="R''u")
             tt(df, (rp, lo, hi), (rp, lo + L, hi + L), OP.subtract, "df")
@@ -498,7 +457,7 @@ def design():
         if last and end:
             copy(("yrf", lo, hi), rn, "R f")
             x3, c4, c5 = (a3, 0, 16 * n), (c3, 0, 16 * n), (c3, 16 * n, 32 * n)
-            gtt(x3, src, (u, lo, hi), ("xm", 16 * lo, 16 * hi), OP.subtract, "cand")
+            gtt(x3, src, (u, lo, hi), ("xm", 16 * lo, 16 * hi), OP.add, "cand")
             ts(c4, x3, ("epf", 0, 1), None, OP.is_le, name="c3")
             ts(c5, x3, ("epf", 1, 2), None, OP.is_ge, name="c3")
             total(cn, [(c4, "b4096"), (c5, "b4096")], ("cz", tw), ("yrf", lo, hi), "cnt3")
@@ -512,24 +471,16 @@ def design():
                 if lo == 0:
                     copy((rf, 0, 1), (rf, 1, 2), "rf0")
             sizes = (t, k) in PLAN["acS"]
-            for i, (a, c) in enumerate(_cut(lo, hi, 64 if sizes else PLAN["test"])):
-                h0 = BANK if PLAN["apart"] and not last else BANK * (i % 2) if c - a <= 32 else 0
-                x, h = (sb, h0, h0 + 16 * (c - a)), (16 * (a - lo), 16 * (c - lo))
+            for a, c in _cut(lo, hi, PLAN["wide"][4 if sizes else 3]):
+                h = (16 * (a - lo), 16 * (c - lo))
                 if sizes:
-                    sub(x, (xr, 16 * a, 16 * c), ("xm", 16 * a, 16 * c), "ac-")
-                    absS((a3,) + h, x, "ac||")
+                    absS((a3,) + h, sub((xr, 16 * a, 16 * c), ("xm", 16 * a, 16 * c), "ac-", "ident", "ident"), "ac||")
                 else:
-                    sub(x, (xr, 16 * a, 16 * c), ("xm", 16 * a, 16 * c), "ac-", "sgp", "sgn")
-                    ts((c3,) + h, x, BIG, BIG, OP.add, OP.is_equal, name="ac=")
+                    ts((c3,) + h, sub((xr, 16 * a, 16 * c), ("xm", 16 * a, 16 * c), "ac-", "sgp", "sgp"), BIG, BIG, OP.add, OP.is_equal, name="ac=")
             if sizes:
                 ts((c3, 0, 16 * n), (a3, 0, 16 * n), ("epf", 0, 1), None, OP.is_le, name="c3")
-            if not PLAN["plus"]:
-                total(cn, [((c3, 0, 16 * n), "b4096")], ("cz", 0), None, "cnt3")
-                tt(cn, cn, rn, OP.add, "z3")
-            elif last:
-                total(cn, [((c3, 0, 16 * n), "b4096")], ("cz", 0), rn, "cnt3")
-            else:
-                total(cn, [((c3, 0, 16 * n), "b4096")], ("cz", 2 * tw), (rf, lo + 1, hi + 1), "cnt3")
+            total(cn, [((c3, 0, 16 * n), "b4096")], ("cz", 0), None, "cnt3")
+            tt(cn, cn, rn, OP.add, "z3")
         mm, mn = (js, 4 * TW, 4 * TW + n), ("mn_%d" % y, lo, hi)
         tt(mm, cn, ("mn_%d" % z, lo, hi), OP.max, "mm")
         ts(mn, mm, W - 1, None, OP.bitwise_and, name="M'")
@@ -540,7 +491,7 @@ def design():
         mu = "mu_%d" % y
         copy((mu, lo, hi), mn, "M'u")
         for a, c in _cut(lo, hi, PLAN["plain"]):
-            gather(("xm", 16 * a, 16 * c), FL, (mu, a, c), "XM'", PLAN["eng"][2])
+            gather(("xm", 16 * a, 16 * c), FL, (mu, a, c), "XM'", PLAN["eng"][2], -1.0)
 
     def whole(j):
         t, k = tiles[j]
@@ -603,19 +554,25 @@ def depend(ops):
                 lst[:] = [a for a in lst if not (lo <= a[1] and a[2] <= hi)]
             lst.append((i, lo, hi, wr))
         o["dep"] = dep
-        o["banks"] = {(buf, b) for (buf, lo, hi), _ in touches if _psum(buf) for b in range(lo // BANK, (hi - 1) // BANK + 1)}
+        o["banks"] = {(buf, b) for (buf, lo, hi), _ in touches if buf in SCRATCH and _psum(buf) for b in range(lo // BANK, (hi - 1) // BANK + 1)}
 
 
 def lay(ops, rank, before, behind, back):
+    n = len(ops)
     left = [len(x) for x in before]
-    at = [ops[i]["lat"] if back else 0.0 for i in range(len(ops))]
-    free = {e: 0.0 for e in "VSPGYN"}
-    ready = {e: [] for e in free}
+    at = [ops[i]["lat"] if back else 0.0 for i in range(n)]
+    free = {e: 0.0 for e in "VSPGYND"}
+    ready = {e: [] for e in "VSPGYN"}
     held, out = {}, {}
-    for i in range(len(ops)):
+    lent = [0.0] * FREE
+    takes = {i + back: o["lend"] for i, o in enumerate(ops) if "lend" in o}
+    for i in range(n):
         if not left[i]:
             for e in ops[i]["eng"]:
                 ready[e].append(i)
+
+    def room(k):
+        return min((max(lent[b:b + k]), b) for b in range(0, FREE - k + 1, k))
 
     def when(i, e):
         t = at[i]
@@ -623,9 +580,9 @@ def lay(ops, rank, before, behind, back):
             for x, f in held.get(b, {}).items():
                 if x != e and f > t:
                     t = f
-        return t
-    while len(out) < len(ops):
-        t, e = min((max(free[e], min(when(i, e) for i in ready[e])), e) for e in free if ready[e])
+        return max(t, room(takes[i])[0]) if i in takes else t
+    while len(out) < n:
+        t, e = min((max(free[e], min(when(i, e) for i in ready[e])), e) for e in ready if ready[e])
         i = max(ready[e], key=lambda j: (rank[j] - PLAN["haste"] * max(0.0, when(j, e) - t), j if back else -j))
         t = max(t, when(i, e))
         o = ops[i]
@@ -635,9 +592,20 @@ def lay(ops, rank, before, behind, back):
         if e != "N":
             free[e] = t + dur
         end = t + dur + (0.0 if back else o["lat"])
-        out[i] = (t, end, e, len(out))
-        for b in o["banks"]:
-            held.setdefault(b, {})[e] = t + dur + COST["wake"]
+        if "move" in o and not back:
+            free["D"] = max(t + dur, free["D"]) + o["move"]
+            end = free["D"] + o["lat"] - o["move"]
+        b = None
+        if i in takes:
+            b = room(takes[i])[1]
+            lent[b:b + takes[i]] = [1e9] * takes[i]
+        mate = i + 1 if back else i - 1
+        if mate in takes:
+            b = out[mate][4]
+            lent[b:b + takes[mate]] = [t + dur + COST["wake"]] * takes[mate]
+        out[i] = (t, end, e, len(out), b)
+        for x in o["banks"]:
+            held.setdefault(x, {})[e] = t + dur + COST["wake"]
         for j in behind[i]:
             at[j] = max(at[j], end + (ops[j]["lat"] if back else 0.0) + (COST["same"] - COST["wake"] if ops[j]["eng"] == e else 0.0))
             left[j] -= 1
@@ -649,58 +617,72 @@ def lay(ops, rank, before, behind, back):
 
 def arrange(ops):
     n = len(ops)
-    pred, succ = [o["dep"] for o in ops], [[] for _ in ops]
-    for i, o in enumerate(ops):
-        for j in o["dep"]:
-            succ[j].append(i)
+    pred = [o["dep"] for o in ops]
+    ways = []
+    for back in (0, 1):
+        before = [set() if back else set(x) for x in pred]
+        for i in range(n) if back else ():
+            for j in pred[i]:
+                before[j].add(i)
+        for i, o in enumerate(ops):
+            if "lend" in o:
+                before[i + back] |= before[i + 1 - back] - {i + back}
+        behind = [[] for _ in ops]
+        for i in range(n):
+            for j in before[i]:
+                behind[j].append(i)
+        ways.append((before, behind))
     rank = [0.0] * n
     for i in range(n - 1, -1, -1):
-        rank[i] = ops[i]["dur"] + ops[i]["lat"] + max([rank[j] for j in succ[i]], default=0.0)
+        rank[i] = ops[i]["dur"] + ops[i]["lat"] + max([rank[j] for j in ways[0][1][i]], default=0.0)
     best, rng = None, np.random.default_rng(PLAN["seed"])
-    kind_of = ["%s %d" % (o["name"], PLAN["parts"] * i // n) for i, o in enumerate(ops)]
-    first, kinds = rank, sorted(set(kind_of))
     for turn in range(PLAN["passes"]):
-        if turn % 3 == 0:
-            lean = dict(best[4]) if best else {}
-            for kind in rng.choice(kinds, 3 * PLAN["parts"]) if best else ():
-                lean[kind] = lean.get(kind, 0.0) + float(rng.normal(0.0, PLAN["shake"]))
-            rank = list(first)
-        there = lay(ops, [rank[i] + lean.get(kind_of[i], 0.0) for i in range(n)], pred, succ, False)
+        if best:
+            home = lay(ops, [best[1][i][1] + x for i, x in enumerate(rng.normal(0.0, PLAN["shake"], n))], *ways[1], True)
+            rank = [home[i][1] for i in range(n)]
+        there = lay(ops, rank, *ways[0], False)
         seq = sorted(range(n), key=lambda i: there[i][3])
         deps, last, fill = {}, {}, set()
         for i in seq:
             e, d = there[i][2], set(pred[i])
-            if e == "G" and ops[i]["f"]:
+            if e == "G" and ops[i]["f"] and "dma" not in ops[i]:
                 d, fill = d | fill, {i}
-            for b in ops[i]["banks"]:
+            banks = set(ops[i]["banks"])
+            if there[i][4] is not None:
+                banks |= {("sub", there[i][4] + b) for b in range(ops[i if "lend" in ops[i] else i - 1]["lend"])}
+            for b in banks:
                 d |= {j for x, j in last.setdefault(b, {}).items() if x != e}
                 last[b][e] = i
             deps[i] = d
         worth = sum(replay(ops, seq, there, deps, *x) for x in RANGE)
-        if best is None or worth < best[0]:
-            best = (worth, there, seq, deps, lean)
-        if turn % 3 < 2:
-            home = lay(ops, [there[i][1] for i in range(n)], succ, pred, True)
-            rank = [home[i][1] for i in range(n)]
+        if best is None or worth <= best[0]:
+            best = (worth, there, seq, deps)
     order = {e: [] for e in "VSPGYN"}
     for i in best[2]:
         o = ops[i]
-        o["t0"], o["on"], o["dep"] = best[1][i][0], best[1][i][2], best[3][i]
+        o["t0"], o["on"], o["turn"], o["dep"] = best[1][i][0], best[1][i][2], best[1][i][3], best[3][i]
         if o["on"] == "S" and "slow" in o:
             o["dur"] = o["slow"]
+        if "lend" in o:
+            LENT[o["wr"][0][0]] = best[1][i][4]
         order[o["on"]].append(i)
     return order, best[0]
 
 
-def replay(ops, seq, laid, deps, wake, same, ga, pe):
+def replay(ops, seq, laid, deps, wake, same, ga, pe, slow):
     free, over = {}, {}
     for i in seq:
         o, e = ops[i], laid[i][2]
         t = max([free.get(e, 0.0)] + [over[j] + (same - wake if laid[j][2] == e else 0.0) for j in deps[i]])
         t += (o["slow"] if e == "S" and "slow" in o else o["dur"] * pe / COST["pe"] if e == "P" else o["dur"]) + o.get("picks", 0) * COST["cy"] * (ga - COST["ga"])
+        if "move" in o:
+            free[e] = t + o["dur"] * (slow - 1.0)
+            free["D"] = max(free[e], free.get("D", 0.0)) + o["move"] * slow
+            over[i] = free["D"] + (o["lat"] - o["move"]) * slow
+            continue
         if e != "N":
             free[e] = t
-        over[i] = t + (wake if o["lat"] == COST["wake"] else o["lat"] - o.get("pad", 0))
+        over[i] = t + (wake if o["lat"] == COST["wake"] else o["lat"])
     return max(over.values())
 
 
@@ -717,7 +699,7 @@ def made():
         for e in "VSPG":
             c = 0
             for i in order[e]:
-                if "dma" in ops[i] or "send" in ops[i] or "fold" in ops[i]:
+                if "dma" in ops[i] or "send" in ops[i]:
                     continue
                 c += 1
                 num[i] = c
@@ -767,35 +749,15 @@ def _key(i, ops, num):
         return None, 0
     if "recv" in o:
         return "arr%d" % o["recv"], 8
-    if "fold" in o:
-        return "left_" + o["fold"]["out"][0], 16 * o["fold"]["count"]
-    if "back" in o:
-        return "back_" + o["back"]["out"][0], 16 * o["back"]["count"]
     return "s" + o["on"], num[i]
-
-
-def helpers(core, T, topo):
-    free = [c for c in topo.cores_of(core) if T.rank_of(c) is None]
-    return sorted(free, key=lambda c: topo.die(c) != topo.die(core))[:HELPERS]
 
 
 def rank_program(g, core, T, topo):
     rank = T.rank_of(core)
+    if rank is None:
+        return
     m = made()
     ops, order, waits = m["ops"], m["order"], m["waits"]
-    jobs = [ops[i]["fold"] for i in order["G"] if "fold" in ops[i]]
-    if rank is None:
-        for home in T.cores:
-            if core in helpers(home, T, topo):
-                mine = [job for job in jobs if job["helper"] == helpers(home, T, topo).index(core)]
-                rid, pid, _ = topo.addr(home)
-                for job in mine:
-                    g.wait_ge(T.sem["there_" + job["out"][0]], 16 * job["count"])
-                    g.remote_dma(out_ap=_ap(T, job["out"]), in_ap=_ap(T, job["stage"]), remote_sem=T.sem["back_" + job["out"][0]],
-                                 local_sem=T.sem.ls, pid=pid, routing_id=rid, dma_engine_mask=topo.mask(core, home))
-                if mine:
-                    g.wait_ge(T.sem.ls, 16 * len(mine))
-        return
     queues = {"V": g.vector, "S": g.scalar, "P": g.tensor, "G": g, "Y": g.sync}
     sent = 0
     for e in ("G", "Y", "S", "V", "P"):
@@ -812,13 +774,6 @@ def rank_program(g, core, T, topo):
                 g.remote_dma(out_ap=T["land%d" % t][:], in_ap=T["lout%d" % t][:], remote_sem=T.sem["arr%d" % t], local_sem=T.sem.ls,
                              pid=pid, routing_id=rid, dma_engine_mask=sum(1 << x for x in eng))
                 sent += len(eng)
-            elif "fold" in o:
-                job = o["fold"]
-                dst = helpers(core, T, topo)[job["helper"]]
-                rid, pid, _ = topo.addr(dst)
-                g.remote_dma_fused([RemoteDMATransfer(dst_ids=[DstId(rid=rid, pnc=pid)], dma_engine_mask=topo.mask(core, dst),
-                                                      remote_sem=T.sem["there_" + job["out"][0]], srcs=[_ap(T, job["a"]), _ap(T, job["b"])],
-                                                      dsts=[_ap(T, job["stage"])], alu_op=2)], local_sem=T.sem["left_" + job["out"][0]])
             elif "dma" in o:
                 o["f"](q, T).then_inc(T.sem[o["dma"]], 16)
             elif "flex" in o:
@@ -826,8 +781,6 @@ def rank_program(g, core, T, topo):
             else:
                 o["f"](q, T).then_inc(T.sem["s" + e], 1)
     g.wait_ge(T.sem.ls, sent)
-    for name, count in {job["out"][0]: job["count"] for job in jobs}.items():
-        g.wait_ge(T.sem["left_" + name], 16 * count)
     for i, o in enumerate(ops):
         if "dma" in o and o["name"].startswith("st"):
             g.sync.wait_ge(T.sem[o["dma"]], 16)

@@ -1,3 +1,4 @@
+import math
 import numpy as np
 from concourse.mybir import dt, AluOpType, AxisListType, ActivationFunctionType
 
@@ -8,36 +9,35 @@ TW = 64
 CE = 16 * TW
 FO = 592
 BANK = 512
-FREE = 4
+FREE = 3
 NB = 4
 BIG = 12582912.0
 
 _F, _B, _I, _U, _H = "float32", "bfloat16", "int32", "uint16", "float16"
 SCRATCH = {
-    "fl": ("sbuf", [128, FO + W], _B), "xm": ("sbuf", [128, 4096], _B),
+    "fl": ("sbuf", [128, 3 * W], _B), "xm": ("sbuf", [128, 4096], _B),
     "ones": ("sbuf", [128, 128], _B), "ident": ("sbuf", [128, 128], _B), "nident": ("sbuf", [128, 128], _B),
     "identf": ("sbuf", [128, 128], _F), "sgp": ("sbuf", [128, 128], _H),
     "g8": ("sbuf", [128, 8], _B), "g8b": ("sbuf", [128, 8], _B),
-    "b1": ("sbuf", [128, 144], _B), "b2": ("sbuf", [128, 144], _B), "b4096": ("sbuf", [128, 144], _B),
+    "b1": ("sbuf", [128, 144], _B), "b2": ("sbuf", [128, 144], _B),
     "b8192": ("sbuf", [128, 144], _B), "b16384": ("sbuf", [128, 144], _B),
     "ck": ("sbuf", [128, 5 * TW], _B), "cy": ("sbuf", [128, 3 * TW], _B), "cz": ("sbuf", [128, 2 * TW], _B),
-    "iot": ("sbuf", [128, 32], _F), "i16": ("sbuf", [128, TW], _F), "neg": ("sbuf", [128, TW], _F), "thb": ("sbuf", [128, 3 * TW], _F),
+    "iot": ("sbuf", [128, 32], _F), "i16": ("sbuf", [128, TW], _F), "neg": ("sbuf", [128, TW], _F), "thb": ("sbuf", [128, 6 * TW], _H), "thf": ("sbuf", [128, TW], _F),
     "ipt": ("sbuf", [128, 2], _I), "ipf": ("sbuf", [128, 2], _F), "cpos": ("sbuf", [128, TW], _F),
     "dgj": ("sbuf", [128, 512], _F), "diag": ("sbuf", [128, 512], _F), "seg": ("sbuf", [128, 512], _F),
     "thi": ("sbuf", [128, 1], _I), "epi": ("sbuf", [128, 1], _I), "epf": ("sbuf", [128, 8], _F),
     "tha": ("sbuf", [128, 8], _F), "nk": ("sbuf", [128, 32], _F), "aout": ("sbuf", [128, 4], _F),
-    "ru0": ("sbuf", [128, 256], _U), "lu": ("sbuf", [128, 32], _U),
+    "ri": ("sbuf", [128, 256], _I), "bi": ("sbuf", [128, 256], _I), "ru0": ("sbuf", [128, 256], _U), "lu": ("sbuf", [128, 32], _U),
     "lg": ("sbuf", [128, 512], _F), "ls": ("sbuf", [128, 512], _F),
     "lo": ("sbuf", [128, 64], _F), "lx": ("sbuf", [128, 64], _I),
     "yrf": ("sbuf", [128, 256], _F), "ymf": ("sbuf", [128, 256], _F),
-    "pv": ("psum", [128, 512], _F), "sc": ("psum", [128, 1024], _F),
-    "cnt": ("psum", [128, 512], _F), "sub": ("psum", [128, FREE * BANK], _F),
+    "pv": ("psum", [128, 512], _F), "sc": ("psum", [128, NB * BANK], _F), "sub": ("psum", [128, FREE * BANK], _F),
 }
 for _k in range(3):
     SCRATCH["lout%d" % _k] = ("sbuf", [128, 32], _F)
     SCRATCH["land%d" % _k] = ("sbuf", [128, 32], _F)
 for _k in range(2):
-    for _n, _c, _d in (("rn", 264, _I), ("rf", 264, _F), ("mn", 264, _I), ("mf", 264, _F), ("rp", 264, _I), ("rm", 232, _F),
+    for _n, _c, _d in (("rn", 264, _H), ("rf", 264, _F), ("mf", 264, _I), ("rp", 264, _I), ("rm", 232, _F),
                        ("rpu", 256, _U), ("r2u", 256, _U), ("mu", 256, _U), ("xr", 4112, _B), ("xp", 4096, _B)):
         SCRATCH[_n + "_%d" % _k] = ("sbuf", [128, _c], _d)
 for _k in range(NB):
@@ -48,7 +48,7 @@ for _k in range(NB):
 NDMA = 130
 SEMAPHORES = ["sV", "sS", "sP", "sG", "ls", "arr0", "arr1", "arr2"] + ["d%d" % k for k in range(NDMA)]
 
-COST = {"cy": 0.000833, "ga": 1.48, "pe": 0.00058, "v": 0.01, "s": 0.06, "wake": 0.18, "same": 0.26, "net": 5.5,
+COST = {"cy": 0.000833, "ga": 1.48, "pe": 0.00058, "v": 0.01, "s": 0.06, "wake": 0.18, "same": 0.26, "net": 4.5,
         "issue": 0.8, "hop": 1.5, "dma": 250e3, "add": 1.1}
 TILES = ((0, 64, 128, 192, 256), (0, 64, 128, 192, 256), (0, 64, 128, 192, 256))
 PLAN = {
@@ -59,19 +59,22 @@ PLAN = {
     "half": 1,
     "plain": 64,
     "tail": 1,
-    "acS": ((2, 0), (2, 1), (2, 2), (2, 3)),
+    "acS": (),
     "first": "SVV",
     "me": "S",
     "wide": (32, 32, 32, 32, 32),
+    "plus": 1,
     "haste": 30.0,
     "eng": ("S", "S", "S", "S"),
     "split": 2,
     "lag": (3, 4, 8),
-    "passes": 400,
-    "seed": 1,
+    "passes": 40,
+    "swaps": 120000, "heat": 0.14, "jump": 0.5,
+    "seed": 3,
     "shake": 0.9,
 }
-RANGE = ((0.2, 0.26, 1.47, 0.00042, 1.0), (0.15, 0.25, 1.9, 0.00042, 1.3), (0.15, 0.25, 1.3, 0.0008, 1.0), (0.15, 0.25, 1.6, 0.0007, 0.8))
+RANGE = ((0.2, 0.26, 1.47, 0.00045, 1.0, 1.0), (0.13, 0.2, 1.9, 0.0005, 0.85, 0.8), (0.13, 0.2, 1.25, 0.00075, 0.8, 0.8))
+STEP = 24
 LENT = {}
 
 
@@ -108,8 +111,11 @@ def design():
 
     def op(eng, f, rd, wr, dur, lat=WAKE, name="", **kw):
         o = {"eng": eng, "f": f, "rd": [_span(r) for r in rd], "wr": [_span(r) for r in wr], "dur": dur, "lat": lat, "name": name}
-        o.update(kw)
+        here[2][name] = here[2].get(name, 0) + 1
+        o.update(kw, kind=(here[0], name, here[2][name]), tile=here[1])
         ops.append(o)
+
+    here = ["start", 0, {}]
 
     def tt(out, a, b, alu, name="tt"):
         c = 1 if (_psum(a[0]) or _psum(b[0])) else 2
@@ -177,18 +183,19 @@ def design():
         op("P", f, [a, b, (plus, 0, 128), (minus, 0, 128)], [out], PEC * 2 * n, name=name, lend=-(-n // BANK))
         return out
 
-    def total(out, terms, const, plus, name):
+    def total(out, terms, const, plus, name, ends=(True, True), holds=None):
         n = out[2] - out[1]
-        first = ([("ones", (const[0], const[1], const[1] + n))] if const else []) + ([("identf", plus)] if plus else [])
+        full = plus and SCRATCH[plus[0]][2] == _F
+        first = ([((const + ("ones",))[2], (const[0], const[1], const[1] + n))] if const else []) + ([("identf" if full else "ident", plus)] if plus else [])
 
         def f(q, T):
             todo = [(T[m][:], _ap(T, x)) for m, x in first]
             todo += [(T[wb][:, 15 - p:143 - p], T[x[0]][:, x[1] + p:x[2]:16]) for x, wb in terms for p in range(16)]
             for j, (m, x) in enumerate(todo):
-                i = q.matmul(_ap(T, out), m, x, j == 0, j == len(todo) - 1)
+                i = q.matmul(_ap(T, out), m, x, ends[0] and j == 0, ends[1] and j == len(todo) - 1)
             return i
-        op("P", f, [x for x, _ in terms] + [(wb, 0, 144) for _, wb in terms] + [x for _, x in first] + [(m, 0, 128) for m, _ in first], [out],
-           PEC * max(64, n) * (16 * len(terms) + (1 if const else 0) + (4 if plus else 0)), name=name)
+        op("P", f, [x for x, _ in terms] + [(wb, 0, 144) for _, wb in terms] + [x for _, x in first] + [(m, 0, 128) for m, _ in first], [holds or out],
+           PEC * max(64, n) * (16 * len(terms) + (1 if const else 0) + (4 if full else 1 if plus else 0)), name=name, joint=bool(holds))
 
     nd = [0]
 
@@ -223,10 +230,10 @@ def design():
     tw = TW
     place = lambda bank, first, count, j, n: (bank, TW * (first + j % count), TW * (first + j % count) + n)
 
-    dma("S", lambda T: T.fl[:, FO:FO + W], lambda T: T.flood[:], [], [("fl", FO, FO + W)], "ld flood", 524288)
-    dma("Y", lambda T: T["rn_0"][:, 0:P], lambda T: T.riv[:], [], [("rn_0", 0, P)], "ld riv", 131072)
-    dma("Y", lambda T: T["mn_0"][:, 0:P], lambda T: T.bord[:], [], [("mn_0", 0, P)], "ld bord", 131072)
-    dma("S", lambda T: T.fl[:, 0:FO], lambda T: T.flood[:, W - FO:W], [], [("fl", 0, FO)], "ld flood2", 700000)
+    dma("S", lambda T: T.fl[:, W:2 * W], lambda T: T.flood[:], [], [("fl", W, 2 * W)], "ld flood", 524288)
+    dma("Y", lambda T: T.ri[:], lambda T: T.riv[:], [], [("ri", 0, P)], "ld riv", 131072)
+    dma("Y", lambda T: T.bi[:], lambda T: T.bord[:], [], [("bi", 0, P)], "ld bord", 131072)
+    dma("S", lambda T: T.fl[:, W - FO:W], lambda T: T.flood[:, W - FO:W], [], [("fl", W - FO, W)], "ld flood2", 700000)
     dma("Y", lambda T: T.thi[:], lambda T: T.th[:], [], [("thi", 0, 1)], "ld th")
     dma("G", lambda T: T.epi[:], lambda T: T.eps[:], [], [("epi", 0, 1)], "ld eps")
 
@@ -245,7 +252,7 @@ def design():
     scale(("identf", 0, 128), ("ident", 0, 128), 1.0)
     memset("b1", 0, 144, 0.0)
     copy(("b1", 15, 143, 16), ("g8b", 0, 8))
-    for w in (8192, 16384, 4096, 2):
+    for w in (8192, 16384, 2):
         scale(("b%d" % w, 0, 144), ("b1", 0, 144), float(w))
     iota(("ck", 0, 5 * tw), [[0, 5 * tw]], -262144, 0, (0, 64))
     iota(("ck", 0, 5 * tw), [[32, 5], [0, tw]], 0, 0, (64, 128))
@@ -254,8 +261,9 @@ def design():
     for t in range(ROUNDS):
         iota(("cy", tw * t, tw * t + tw), [[0, tw]], cons[t] // 32, 0, (64, 96))
         asel(("cy", tw * t, tw * t + tw), ("ones", 0, tw), [[0, tw]], OP.is_gt, cons[t] % 32, -1, (96, 128))
-    iota(("cz", 0, 2 * tw), [[0, 2 * tw]], -544, 0, (0, 64))
-    iota(("cz", 0, 2 * tw), [[-1024, 2], [0, tw]], 0, 0, (64, 128))
+    iota(("cz", 0, 2 * tw), [[0, 2 * tw]], -1088, 0, (0, 64))
+    iota(("cz", 0, 2 * tw), [[-4096, 2], [0, tw]], 0, 0, (64, 96))
+    memset("cz", 0, 2 * tw, FO / 32.0, 96, 128)
     ts(("ipt", 1, 2), ("ipt", 0, 1), 15, None, OP.bitwise_and)
     copy(("ipf", 0, 1), ("ipt", 1, 2))
     ts(("pv", 0, tw), ("i16", 0, tw), ("ipf", 0, 1), 1.0 / 512, OP.add, OP.mult)
@@ -271,18 +279,22 @@ def design():
         for buf, lo, hi, val in (("rf", 257, 264, FO), ("mf", 256, 264, FO), ("rp", 256, 264, 0), ("rm", 0, 1, 0), ("xr", 4096, 4112, 0)):
             iota(("%s_%d" % (buf, k), lo, hi), [[0, hi - lo]], val, 0)
 
-    FL = ("fl", FO, FO + W)
-    FC = ("fl", 0, W + 160)
+    FL = ("fl", W, 2 * W)
+    FC = ("fl", W - FO, 2 * W - FO + 160)
+    FM = ("fl", W - FO, 2 * W)
+    carry(("fl", 0, W - FO), ("fl", W, 2 * W - FO), False, "thrice")
+    carry(("fl", 2 * W, 3 * W), FL, False, "thrice")
     cuts = [0] + [b + 2 for b in TILES[0][1:-1]] + [P]
     for j, (lo, hi) in enumerate(_cut(0, cuts[1], (cuts[1] + 3) // 2) + list(zip(cuts[1:-1], cuts[2:]))):
-        copy(("ru0", lo, hi), ("rn_0", lo, hi), "R u16")
+        copy(("ru0", lo, hi), ("ri", lo, hi), "R u16")
         gather(("xr_0", 16 * lo, 16 * hi), FL, ("ru0", lo, hi), "XR0", PLAN["first"][j] if j < len(PLAN["first"]) else "S")
-    ts(("rf_0", 1, 257), ("rn_0", 0, 256), float(FO), None, OP.add)
+    ts(("rf_0", 1, 257), ("ri", 0, 256), float(FO), None, OP.add)
+    copy(("rn_0", 0, 256), ("ri", 0, 256))
     copy(("rf_0", 0, 1), ("rf_0", 1, 2))
-    ts(("mf_0", 0, 256), ("mn_0", 0, 256), float(FO), None, OP.add)
-    copy(("mu_0", 0, P), ("mn_0", 0, P), "M u16")
+    ts(("mf_0", 0, 256), ("bi", 0, 256), float(FO), None, OP.add)
+    ts(("mu_0", 0, P), ("bi", 0, P), float(FO), None, OP.add, name="M u16")
     for lo, hi in zip(TILES[0][:-1], TILES[0][1:]):
-        gather(("xm", 16 * lo, 16 * hi), FL, ("mu_0", lo, hi), "XM0", PLAN["eng"][3], -1.0)
+        gather(("xm", 16 * lo, 16 * hi), FM, ("mu_0", lo, hi), "XM0", PLAN["eng"][3], -1.0)
 
     tiles = [(t, k) for t in range(ROUNDS) for k in range(len(TILES[t]) - 1)]
     written = [np.zeros(5 * CE, bool) for _ in range(NB)]
@@ -291,11 +303,12 @@ def design():
         t, k = tiles[j]
         c0, c1 = TILES[t][k], TILES[t][k + 1]
         n = c1 - c0
+        here[:] = ["choose", j, {}]
         late = j >= len(tiles) - PLAN["tail"]
         z = t % 2
-        rn, rf, mn, mf, xr, xp = ("%s_%d" % (x, z) for x in ("rn", "rf", "mn", "mf", "xr", "xp"))
+        rn, rf, mf, xr, xp = ("%s_%d" % (x, z) for x in ("rn", "rf", "mf", "xr", "xp"))
         pr, v, u, fs, js, ou, win, now, nb, hb = ("%s_%d" % (x, j % NB) for x in ("pr", "v", "u", "fs", "js", "ou", "win", "now", "nb", "hb"))
-        s0 = (0, BANK - 2 * n, 2 * BANK - 5 * n)[j % 3]
+        s0 = BANK * (j % NB)
         S = lambda a, b=1: ("sc", s0 + a * n, s0 + (a + b) * n)
         F = lambda a, b=1: (fs, a * TW, a * TW + b * n)
         J = lambda a: (js, a * TW, a * TW + n)
@@ -307,10 +320,20 @@ def design():
         for h0, h1 in ((0, 2 * n), (2 * n, 4 * n)) if PLAN["split"] == 2 or late else ((0, 4 * n),):
             ts((v, h0, h1), (pr, h0, h1), 4, W - 1, OP.arith_shift_right, OP.bitwise_and, name="v")
             ts((u, h0, h1), (v, h0, h1), 77.0 * t, None, OP.add, name="u")
-        mode = PLAN["mode"][t][k]
+        mode = PLAN["mode"][t][k] + "T"
         nxt = (xr, 16 * (c0 + 1), 16 * (c1 + 1))
-        for a, c in _cut(c0, c1, PLAN["wide"][0]):
-            absS((now, 16 * (a - c0), 16 * (c - c0)), sub((xr, 16 * a, 16 * c), (xr, 16 * a + 16, 16 * c + 16), "now-"), "now||")
+        x = (now, 0, 16 * n)
+        if mode[5] == "T":
+            for a, c in _cut(c0, c1, PLAN["wide"][0]):
+                absS((now, 16 * (a - c0), 16 * (c - c0)), sub((xr, 16 * a, 16 * c), (xr, 16 * a + 16, 16 * c + 16), "now-"), "now||")
+        else:
+            ts(x, (xr, 16 * c0, 16 * c1), -1.0, None, OP.mult, name="now-")
+            carry(x, nxt, True, "now+")
+            if mode[5] == "e":
+                absS(x, x, "now||")
+            else:
+                ts((hb, 3 * CE, 3 * CE + 16 * n), x, -2.0, 0.0, OP.mult, OP.max, name="relu")
+                carry(x, (hb, 3 * CE, 3 * CE + 16 * n), True, "+relu")
         for m in (4, 0, 1, 2, 3):
             if mode[m] == "T":
                 for a, c in _cut(c0, c1, PLAN["wide"][1]):
@@ -363,7 +386,7 @@ def design():
         tt(k4, S(1), kc, OP.min, "kmin")
         tt(S(0), S(4), k4, OP.is_le, "m5")
         ts(kv, k4, W - 1, None, OP.bitwise_and, name="kv")
-        scale(me, (mf, c0, c1), 1.0, 4096.0 - cons[t] - FO, "me", PLAN["me"])
+        ts(me, (mf, c0, c1), 4096.0 - cons[t] - FO, None, OP.add, name="me")
         ts(ka, k4, 6144, 10, OP.bitwise_and, OP.arith_shift_right, name="ka")
         tt(S(1), S(0), ("cpos", 0, n), OP.mult, "uu")
         tt(w, ("pv", 0, n), ka, OP.add, "w")
@@ -372,12 +395,13 @@ def design():
         tt(S(2), S(0), me, OP.mult, "t5")
         tt(d, S(2), kv, OP.max, "d")
         yield
+        here[:] = ["accept", j, {}]
         whole = (win, 0, 4 * CE + 16 * n)
         for a, c in _cut(0, n, 32 if late else PLAN["cand"][4]):
             gtt((nb, 16 * a, 16 * c), whole, (ou, a, c), (now, 16 * a, 16 * c), OP.is_lt, "nearer")
-        Z = place("cnt", 4, 3, j, n)
-        total(Z, [((nb, 0, 16 * n), "b16384")], ("cy", tw * t), d if late else None, "cnt1")
-        if not late:
+        Z = S(5)
+        total(Z, [((nb, 0, 16 * n), "b16384")], ("cy", tw * t), d if late or PLAN["plus"] else None, "cnt1")
+        if not (late or PLAN["plus"]):
             tt(Z, Z, d, OP.add, "z")
         tt(rr, Z, (rn, c0, c1), OP.max, "rr")
         rp, rpu = "rp_%d" % z, "rpu_%d" % z
@@ -396,22 +420,26 @@ def design():
     def necks(j):
         t, k = tiles[j]
         lo, hi = piece(j)
+        here[:] = ["necks", j, {}]
         if k == 0:
-            ts(("thb", TW * t, TW * t + tw), ("neg", 0, tw), ("tha", t, t + 1), None, OP.mult, name="thb")
+            ts(("thb", 2 * TW * t, 2 * TW * t + tw), ("neg", 0, tw), ("tha", t, t + 1), None, OP.mult, name="thb")
+            ts(("thf", 0, tw), ("thb", 2 * TW * t, 2 * TW * t + tw), ("tha", t, t + 1), -1.0, OP.add, OP.mult, name="thb")
+            copy(("thb", 2 * TW * t + tw, 2 * TW * t + 2 * tw), ("thf", 0, tw), "thb")
         if hi <= lo:
             return
         late = j >= len(tiles) - PLAN["tail"]
         xp, rm, a2 = "xp_%d" % (t % 2), "rm_%d" % (t % 2), "a2_%d" % (j % NB)
         n = hi - lo
-        ds = place("cnt", 0, 2, j, n)
+        ds = ("sc", BANK * (j % NB) + 6 * TW, BANK * (j % NB) + 6 * TW + n)
         for a, c in _cut(lo, hi, 32 if late else PLAN["wide"][2]):
             absS((a2, 16 * (a - lo), 16 * (c - lo)), sub((xp, 16 * a, 16 * c), (xp, 16 * (a + L), 16 * (c + L)), "nk-"), "nk||")
-        total(ds, [((a2, 0, 16 * n), "b2")], None, ("thb", TW * t, TW * t + n), "dist")
+        total(ds, [((a2, 0, 16 * n), "b2")], ("thb", 2 * TW * t + tw, "ident"), ("thb", 2 * TW * t, 2 * TW * t + n), "dist")
         scan((rm, 1 + lo, 1 + hi), ds, ("neg", 0, n), (rm, lo, lo + 1), OP.min, OP.max, "rm")
 
     def loops(j):
         t, k = tiles[j]
         lo = piece(j)[0]
+        here[:] = ["loops", j, {}]
         rm, rp = "rm_%d" % (t % 2), "rp_%d" % (t % 2)
         c = lambda i: ("nk", 8 * t + i, 8 * t + i + 1)
         end = (rm, P - L, P - L + 1)
@@ -419,15 +447,15 @@ def design():
         reduce(c(0), (rm, 1, 1 + lo), OP.add, "ge")
         reduce(c(1), (rm, 1 + lo, 1 + P - L), OP.add, "ge2")
         ts(("lu", 0, 32), ("iot", 0, 32), c(0), c(1), OP.add, OP.add, name="lu")
-        ts(c(2), end, -12288.0, -8192.0, OP.mult, OP.add, name="fl")
+        ts(c(2), end, -10240.0, -8192.0, OP.mult, OP.add, name="fl")
         gtt(("lg", 0, 512), (rp, 0, 264), ("lu", 0, 32), ("diag", 0, 512), OP.mult, "loop")
         scan(("ls", 0, 512), ("seg", 0, 512), ("lg", 0, 512), 0.0, OP.mult, OP.add, "scan")
         own = ("ls", 15, 512, 16)
         ts(lout, own, c(2), None, OP.add, name="lout")
-        op("G", None, [lout], [], 1.0, name="send", send=t)
-        op("N", None, [lout], [("land%d" % t, 0, 32)], 0.0, lat=COST["net"], name="recv", recv=t)
+        op("G", None, [lout], [("sent", t, t + 1)], 1.0, lat=0.0, name="send", send=t)
+        op("N", None, [("sent", t, t + 1)], [("land%d" % t, 0, 32)], 0.0, lat=COST["net"], name="recv", recv=t)
         ts(("tha", t + 1, t + 2), end, -32.0, ("tha", t, t + 1), OP.mult, OP.add, name="A")
-        ts(c(4), end, 16384.0, 8192.0, OP.mult, OP.add, name="l0")
+        ts(c(4), end, 12288.0, 4096.0, OP.mult, OP.add, name="l0")
         ts(("lo", 32, 64), (rp, P - L, P), c(4), None, OP.add, name="l0")
         tt(("lo", 0, 32), own, ("lo", 32, 64), OP.max, "l0")
 
@@ -437,10 +465,11 @@ def design():
         n = hi - lo
         if n <= 0:
             return
+        here[:] = ["landed" if end else "last" if last else "moved", tiles.index((t, k - end)), {}]
         a3, c3, fs, js = ("%s_%d" % (x, s) for x in ("a3", "c3", "fs", "js"))
-        cn = place("cnt", 2, 2, s, n)
+        cn = ("sc", BANK * s + 7 * TW, BANK * s + 7 * TW + n)
         rp, rm, u = "rp_%d" % z, ("rm_%d" % z, lo, hi), "r2u_%d" % z
-        rn = ("yrf", lo, hi) if last and not end else ("rn_%d" % y, lo, hi)
+        rn = ("yrf", lo, hi) if last else ("rn_%d" % y, lo, hi)
         if not end:
             df, ix = place("pv", 4, 3, s, n), (fs, 7 * TW, 7 * TW + n)
             tt(ix, ("pv", 0, n), rm, OP.subtract, "ix")
@@ -451,16 +480,19 @@ def design():
             src = ("xp_%d" % z, 16 * lo, 16 * (hi + L))
         else:
             tt(("lx", 0, 32), ("land%d" % t, 0, 32), ("lo", 0, 32), OP.max, "l1")
-            ts(rn, ("lx", 0, 32), W - 1, None, OP.bitwise_and, name="l2")
-            copy((u, lo, hi), rn, "R''u")
-            src = FL
+            ts(("lx", 32, 64), ("lx", 0, 32), W - 1, None, OP.bitwise_and, name="l2")
+            copy((u, lo, hi), ("lx", 0, 32), "R''u")
+            copy(rn, ("lx", 32, 64), "R f")
+            src = ("fl", 0, 3 * W)
         if last and end:
-            copy(("yrf", lo, hi), rn, "R f")
             x3, c4, c5 = (a3, 0, 16 * n), (c3, 0, 16 * n), (c3, 16 * n, 32 * n)
             gtt(x3, src, (u, lo, hi), ("xm", 16 * lo, 16 * hi), OP.add, "cand")
             ts(c4, x3, ("epf", 0, 1), None, OP.is_le, name="c3")
             ts(c5, x3, ("epf", 1, 2), None, OP.is_ge, name="c3")
-            total(cn, [(c4, "b4096"), (c5, "b4096")], ("cz", tw), ("yrf", lo, hi), "cnt3")
+            bank = ("sc", BANK * s, BANK * s + BANK)
+            total(cn, [], ("cz", tw), rn, "cnt3", (True, False), bank)
+            total(cn, [(c4, "b8192")], None, None, "cnt3", (False, False), bank)
+            total(cn, [(c5, "b8192")], None, None, "cnt3", (False, True), bank)
         else:
             xr = "xr_%d" % y
             for a, c in _cut(lo, hi, PLAN["plain"]):
@@ -479,19 +511,19 @@ def design():
                     ts((c3,) + h, sub((xr, 16 * a, 16 * c), ("xm", 16 * a, 16 * c), "ac-", "sgp", "sgp"), BIG, BIG, OP.add, OP.is_equal, name="ac=")
             if sizes:
                 ts((c3, 0, 16 * n), (a3, 0, 16 * n), ("epf", 0, 1), None, OP.is_le, name="c3")
-            total(cn, [((c3, 0, 16 * n), "b4096")], ("cz", 0), None, "cnt3")
-            tt(cn, cn, rn, OP.add, "z3")
-        mm, mn = (js, 4 * TW, 4 * TW + n), ("mn_%d" % y, lo, hi)
-        tt(mm, cn, ("mn_%d" % z, lo, hi), OP.max, "mm")
-        ts(mn, mm, W - 1, None, OP.bitwise_and, name="M'")
+            total(cn, [((c3, 0, 16 * n), "b8192")], ("cz", 0), None if last else rn, "cnt3")
+            if last:
+                tt(cn, cn, rn, OP.add, "z3")
+        mm, mf = (js, 4 * TW, 4 * TW + n), ("mf_%d" % y, lo, hi)
+        tt(mm, cn, ("mf_%d" % z, lo, hi), OP.max, "mm")
+        ts(mf, mm, 2 * W - 1, None, OP.bitwise_and, name="M'")
         if last:
-            copy(("ymf", lo, hi), mn, "M f")
+            ts(("ymf", lo, hi), mf, -float(FO), None, OP.add, name="M f")
             return
-        ts(("mf_%d" % y, lo, hi), mn, float(FO), None, OP.add, name="mf")
         mu = "mu_%d" % y
-        copy((mu, lo, hi), mn, "M'u")
+        copy((mu, lo, hi), mf, "M'u")
         for a, c in _cut(lo, hi, PLAN["plain"]):
-            gather(("xm", 16 * a, 16 * c), FL, (mu, a, c), "XM'", PLAN["eng"][2], -1.0)
+            gather(("xm", 16 * a, 16 * c), FM, (mu, a, c), "XM'", PLAN["eng"][2], -1.0)
 
     def whole(j):
         t, k = tiles[j]
@@ -530,6 +562,7 @@ def design():
         upto(j, 1)
     for p in (2, 3, 4):
         upto(len(tiles) - 1, p)
+    here[:] = ["start", 0, {}]
     ts(("aout", 1, 2), ("tha", ROUNDS, ROUNDS + 1), ("tha", 0, 1), 1.0 / 32, OP.subtract, OP.mult)
     dma("Y", lambda T: T.ya[:], lambda T: T.aout[:, 1:2], [("aout", 1, 2)], [], "st ya")
     dma("Y", lambda T: T.yr[:, 0:224], lambda T: T.yrf[:, 0:224], [("yrf", 0, 224)], [], "st yr")
@@ -657,23 +690,194 @@ def arrange(ops):
         worth = sum(replay(ops, seq, there, deps, *x) for x in RANGE)
         if best is None or worth <= best[0]:
             best = (worth, there, seq, deps)
+    on = [best[1][i][2] for i in range(n)]
+    worth, seq, more, got = polish(ops, on, best[2])
     order = {e: [] for e in "VSPGYN"}
-    for i in best[2]:
+    for turn, i in enumerate(seq):
         o = ops[i]
-        o["t0"], o["on"], o["turn"], o["dep"] = best[1][i][0], best[1][i][2], best[1][i][3], best[3][i]
-        if o["on"] == "S" and "slow" in o:
+        o["t0"], o["on"], o["turn"], o["dep"] = best[1][i][0], on[i], turn, pred[i] | set(more[i])
+        if on[i] == "S" and "slow" in o:
             o["dur"] = o["slow"]
         if "lend" in o:
-            LENT[o["wr"][0][0]] = best[1][i][4]
-        order[o["on"]].append(i)
-    return order, best[0]
+            LENT[o["wr"][0][0]] = got[i]
+        order[on[i]].append(i)
+    return order, worth
 
 
-def replay(ops, seq, laid, deps, wake, same, ga, pe, slow):
+def polish(ops, on, seq):
+    n, rng = len(ops), np.random.default_rng(PLAN["seed"])
+    pred = [o["dep"] for o in ops]
+    succ = [set() for _ in ops]
+    above, near = [], []
+    for i in range(n):
+        far = set().union(*[above[j] for j in pred[i]])
+        near.append([j for j in pred[i] if j not in far])
+        above.append(far | pred[i])
+        for j in pred[i]:
+            succ[j].add(i)
+    ends = [i for i in range(n) if not succ[i]]
+    own = [[j for j in near[i] if on[j] == on[i] and not (ops[i].get("joint") and ops[j].get("joint"))] for i in range(n)]
+    other = [[j for j in near[i] if on[j] != on[i]] for i in range(n)]
+    banks = [sorted(o["banks"]) for o in ops]
+    lend = [o.get("lend", 0) for o in ops]
+    fill = [on[i] == "G" and bool(o["f"]) and "dma" not in o for i, o in enumerate(ops)]
+    move = ["move" in o for o in ops]
+    cases = []
+    for wake, same, ga, pe, slow, rest in RANGE:
+        dur = [(o["slow"] if on[i] == "S" and "slow" in o else o["dur"] * (pe / COST["pe"] if on[i] == "P" else slow if move[i] else 1.0))
+               + o.get("picks", 0) * COST["cy"] * (ga - COST["ga"]) for i, o in enumerate(ops)]
+        lat = [(o["lat"] - o["move"]) * slow if "move" in o else wake if o["lat"] == COST["wake"] else o["lat"] * rest for o in ops]
+        cases.append((dur, lat, [o.get("move", 0.0) * slow for o in ops], same - wake))
+
+    names = sorted({b for x in banks for b in x})
+    eng = ["VSPGYN".index(e) for e in on]
+    meets = [[(3 * names.index(b) + eng[i], [3 * names.index(b) + y for y in range(3) if y != eng[i]]) for b in banks[i]] for i in range(n)]
+    plain = [not (lend[i] or lend[i - 1] or fill[i] or move[i]) for i in range(n)]
+    at_last, at_lent, at_fill = 6, 6 + 3 * len(names), 6 + 3 * len(names) + 3 * FREE
+
+    def links(seq, a, b, old):
+        more, ahead, moved, got, kept = (x[:] for x in old)
+        st = kept[a // STEP][:]
+        for pos in range(a - a % STEP, n):
+            if not pos % STEP:
+                if pos > b and st == kept[pos // STEP]:
+                    break
+                kept[pos // STEP] = st[:]
+            i = seq[pos]
+            x = other[i]
+            for mine, theirs in meets[i]:
+                x = x + [st[at_last + y] for y in theirs if st[at_last + y] >= 0]
+                st[at_last + mine] = i
+            if not plain[i]:
+                k = lend[i]
+                if k:
+                    room = [(max(st[c + 2], st[c + 3 * k - 1]), c) for c in range(at_lent, at_fill - 3 * k + 1, 3 * k)
+                            if st[c] < 0 and st[c + 3 * k - 3] < 0]
+                    if not room:
+                        return None
+                    got[i] = c = min(room)[1]
+                    for c in range(c, c + 3 * k, 3):
+                        st[c] = i
+                        if st[c + 1] >= 0:
+                            x = x + [st[c + 1]]
+                elif lend[i - 1]:
+                    for c in range(got[i - 1], got[i - 1] + 3 * lend[i - 1], 3):
+                        st[c:c + 3] = -1, i, pos
+                elif fill[i]:
+                    if st[at_fill] >= 0:
+                        x = x + [st[at_fill]]
+                    st[at_fill] = i
+                else:
+                    moved[i] = st[at_fill + 1]
+                    st[at_fill + 1] = i
+            more[i] = x
+            e = eng[i]
+            if e < 5:
+                ahead[i] = st[e]
+                st[e] = i
+        return more, ahead, moved, got, kept
+
+    def run(seq, a, b, link, case, old):
+        more, ahead, moved, _, kept = link
+        dur, lat, bytes_, extra = case
+        was, fin, over, why, gone = old[1], old[0][:], old[1][:], old[2][:], old[3][:]
+        reach = b
+        for pos in range(a, n):
+            if pos > reach and not pos % STEP and all(over[kept[pos // STEP][c]] == was[kept[pos // STEP][c]] for c in ids) \
+                    and all(fin[x] == old[0][x] for x in kept[pos // STEP][:5]):
+                break
+            i = seq[pos]
+            w = ahead[i]
+            t = fin[w]
+            for j in more[i]:
+                if over[j] > t:
+                    t, w = over[j], j
+            for j in own[i]:
+                if over[j] + extra > t:
+                    t, w = over[j] + extra, j
+            t += dur[i]
+            fin[i] = t
+            if bytes_[i]:
+                if gone[moved[i]] > t:
+                    w = moved[i]
+                    t = gone[w]
+                gone[i] = t = t + bytes_[i]
+            why[i] = w
+            t += lat[i]
+            over[i] = t
+            if t != was[i] and last[i] > reach:
+                reach = last[i]
+        return fin, over, why, gone, max([over[i] for i in ends])
+
+    ids = [c for c in range(at_fill + 2) if c < at_lent or c >= at_fill or (c - at_lent) % 3 == 1]
+    where, users = [0] * n, [[] for _ in ops]
+    for i in range(n):
+        where[seq[i]] = i
+        for j in near[i]:
+            users[j].append(i)
+    last = [max([where[j] for j in x], default=0) for x in users]
+    link = links(seq, 0, n, (other, [-1] * n, [-1] * n, [-1] * n, [[-1] * (at_fill + 2)] * (n // STEP + 1)))
+    now = [run(seq, 0, n, link, c, ([0.0] * (n + 1), [0.0] * (n + 1), [-1] * n, [0.0] * (n + 1))) for c in cases]
+    worth = sum(r[4] for r in now)
+    best, paths = (worth, seq, link[0], link[3]), {}
+    for turn in range(PLAN["swaps"]):
+        k = int(rng.integers(len(cases)))
+        if k not in paths:
+            i, paths[k] = max(ends, key=lambda x: now[k][1][x]), []
+            while now[k][2][i] >= 0:
+                u = now[k][2][i]
+                if i not in succ[u]:
+                    paths[k].append((u, i))
+                i = u
+        u, v = paths[k][int(rng.integers(len(paths[k])))]
+        forward = rng.random() < 0.5
+        while rng.random() < PLAN["jump"]:
+            if forward:
+                u = link[1][u] if link[1][u] >= 0 else u
+            else:
+                at = where[v]
+                v = next((y for y in seq[at + 1:at + 40] if link[1][y] == v), v)
+        a, b = where[u], where[v]
+        mid = seq[a:b + 1]
+        if forward:
+            go = {v}
+            for x in mid[-2::-1]:
+                if not succ[x].isdisjoint(go):
+                    go.add(x)
+        else:
+            go = {u}
+            for x in mid[1:]:
+                if not pred[x].isdisjoint(go):
+                    go.add(x)
+        if u in go and v in go:
+            continue
+        trial = seq[:]
+        trial[a:b + 1] = [x for x in mid if (x in go) == forward] + [x for x in mid if (x in go) != forward]
+        new = links(trial, a, b, link)
+        if new is None:
+            continue
+        allow = -PLAN["heat"] * (1.0 - turn / PLAN["swaps"]) * len(cases) * math.log(1.0 - rng.random())
+        first = run(trial, a, b, new, cases[k], now[k])
+        if first[4] - now[k][4] > allow + 0.3:
+            continue
+        then = [first if j == k else run(trial, a, b, new, cases[j], now[j]) for j in range(len(cases))]
+        if sum(r[4] for r in then) <= worth + allow:
+            worth, seq, now, link, paths = sum(r[4] for r in then), trial, then, new, {}
+            for i in range(a, b + 1):
+                where[seq[i]] = i
+            for j in {j for i in mid for j in near[i]}:
+                last[j] = max([where[x] for x in users[j]])
+            if worth < best[0]:
+                best = (worth, seq, link[0], link[3])
+    return best[:3] + ([(c - at_lent) // 3 for c in best[3]],)
+
+
+def replay(ops, seq, laid, deps, wake, same, ga, pe, slow, rest):
     free, over = {}, {}
     for i in seq:
         o, e = ops[i], laid[i][2]
-        t = max([free.get(e, 0.0)] + [over[j] + (same - wake if laid[j][2] == e else 0.0) for j in deps[i]])
+        t = max([free.get(e, 0.0)] + [over[j] + (same - wake if laid[j][2] == e else 0.0) for j in deps[i]
+                                      if not (o.get("joint") and ops[j].get("joint"))])
         t += (o["slow"] if e == "S" and "slow" in o else o["dur"] * pe / COST["pe"] if e == "P" else o["dur"]) + o.get("picks", 0) * COST["cy"] * (ga - COST["ga"])
         if "move" in o:
             free[e] = t + o["dur"] * (slow - 1.0)
@@ -682,7 +886,7 @@ def replay(ops, seq, laid, deps, wake, same, ga, pe, slow):
             continue
         if e != "N":
             free[e] = t
-        over[i] = t + (wake if o["lat"] == COST["wake"] else o["lat"])
+        over[i] = t + (wake if o["lat"] == COST["wake"] else o["lat"] * rest)
     return max(over.values())
 
 
@@ -719,6 +923,8 @@ def made():
                     need = {}
                     for j in o["dep"]:
                         key, val = _key(j, ops, num)
+                        if o.get("joint") and ops[j].get("joint"):
+                            continue
                         if key is not None and st.get(key, 0) < val and need.get(key, (0, 0))[0] < val:
                             need[key] = (val, j)
                     out = []

import math
import numpy as np
from concourse.mybir import dt, AluOpType, AxisListType, ActivationFunctionType

OP = AluOpType
ACT = ActivationFunctionType
N, W, P, L, ROUNDS = 8, 2048, 256, 32, 3
TW = 64
CE = 16 * TW
FO = 592
BANK = 512
FREE = 3
NB = 4
BIG = 12582912.0

_F, _B, _I, _U, _H = "float32", "bfloat16", "int32", "uint16", "float16"
SCRATCH = {
    "fl": ("sbuf", [128, 3 * W], _B), "xm": ("sbuf", [128, 4096], _B),
    "ones": ("sbuf", [128, 128], _B), "ident": ("sbuf", [128, 128], _B), "nident": ("sbuf", [128, 128], _B),
    "identf": ("sbuf", [128, 128], _F), "sgp": ("sbuf", [128, 128], _H),
    "g8": ("sbuf", [128, 8], _B), "g8b": ("sbuf", [128, 8], _B),
    "b1": ("sbuf", [128, 144], _B), "b2": ("sbuf", [128, 144], _B),
    "b8192": ("sbuf", [128, 144], _B), "b16384": ("sbuf", [128, 144], _B),
    "ck": ("sbuf", [128, 5 * TW], _B), "cy": ("sbuf", [128, 3 * TW], _B), "cz": ("sbuf", [128, 2 * TW], _B),
    "iot": ("sbuf", [128, 32], _F), "i16": ("sbuf", [128, TW], _F), "neg": ("sbuf", [128, TW], _F), "thb": ("sbuf", [128, 6 * TW], _H), "thf": ("sbuf", [128, TW], _F),
    "ipt": ("sbuf", [128, 2], _I), "ipf": ("sbuf", [128, 2], _F), "cpos": ("sbuf", [128, TW], _F),
    "dgj": ("sbuf", [128, 512], _F), "diag": ("sbuf", [128, 512], _F), "seg": ("sbuf", [128, 512], _F),
    "thi": ("sbuf", [128, 1], _I), "epi": ("sbuf", [128, 1], _I), "epf": ("sbuf", [128, 8], _F),
    "tha": ("sbuf", [128, 8], _F), "nk": ("sbuf", [128, 32], _F), "aout": ("sbuf", [128, 4], _F),
    "ri": ("sbuf", [128, 256], _I), "bi": ("sbuf", [128, 256], _I), "ru0": ("sbuf", [128, 256], _U), "lu": ("sbuf", [128, 32], _U),
    "lg": ("sbuf", [128, 512], _F), "ls": ("sbuf", [128, 512], _F),
    "lo": ("sbuf", [128, 64], _F), "lx": ("sbuf", [128, 64], _I),
    "yrf": ("sbuf", [128, 256], _F), "ymf": ("sbuf", [128, 256], _F),
    "pv": ("psum", [128, 512], _F), "sc": ("psum", [128, NB * BANK], _F), "sub": ("psum", [128, FREE * BANK], _F),
}
for _k in range(3):
    SCRATCH["lout%d" % _k] = ("sbuf", [128, 32], _F)
    SCRATCH["land%d" % _k] = ("sbuf", [128, 32], _F)
for _k in range(2):
    for _n, _c, _d in (("rn", 264, _H), ("rf", 264, _F), ("mf", 264, _I), ("rp", 264, _I), ("rm", 232, _F),
                       ("rpu", 256, _U), ("r2u", 256, _U), ("mu", 256, _U), ("xr", 4112, _B), ("xp", 4096, _B)):
        SCRATCH[_n + "_%d" % _k] = ("sbuf", [128, _c], _d)
for _k in range(NB):
    for _n, _c, _d in (("pr", 4 * TW, _I), ("v", 4 * TW, _I), ("u", 4 * TW, _U), ("fs", 8 * TW, _F), ("js", 5 * TW, _I), ("ou", TW, _U),
                       ("win", 5 * CE, _B), ("now", CE, _B), ("nb", CE, _B), ("a2", CE, _B), ("a3", CE, _B), ("c3", CE, _B),
                       ("hb", 4 * CE, _B)):
        SCRATCH[_n + "_%d" % _k] = ("sbuf", [128, _c], _d)
NDMA = 130
SEMAPHORES = ["sV", "sS", "sP", "sG", "ls", "arr0", "arr1", "arr2"] + ["d%d" % k for k in range(NDMA)]

COST = {"cy": 0.000833, "ga": 1.48, "pe": 0.00058, "v": 0.01, "s": 0.06, "wake": 0.18, "same": 0.26, "net": 4.5,
        "issue": 0.8, "hop": 1.5, "dma": 250e3, "add": 1.1}
TILES = ((0, 64, 128, 192, 256), (0, 64, 128, 192, 256), (0, 64, 128, 192, 256))
PLAN = {
    "cand": (32, 32, 32, 32, 32),
    "mode": (("aaaaT", "hhgae", "hhgae", "hhgae"), ("hhgae", "hhgae", "hhgae", "hhgae"), ("hhgae", "hhgae", "hhgae", "aaaaT")),
    "pair": 0,
    "join": 0,
    "half": 1,
    "plain": 64,
    "tail": 1,
    "acS": (),
    "first": "SVV",
    "me": "S",
    "wide": (32, 32, 32, 32, 32),
    "plus": 1,
    "haste": 30.0,
    "eng": ("S", "S", "S", "S"),
    "split": 2,
    "lag": (3, 4, 8),
    "passes": 40,
    "swaps": 120000, "heat": 0.14, "jump": 0.5,
    "seed": 3,
    "shake": 0.9,
}
RANGE = ((0.2, 0.26, 1.47, 0.00045, 1.0, 1.0), (0.13, 0.2, 1.9, 0.0005, 0.85, 0.8), (0.13, 0.2, 1.25, 0.00075, 0.8, 0.8))
STEP = 24
LENT = {}


def _span(r):
    return r[0], r[1], r[2]


def _ap(T, r):
    if r[0][0] == "#":
        at = BANK * LENT.get(r[0], 0)
        return T.sub[:, at + r[1]:at + r[2]]
    if len(r) == 4:
        return T[r[0]][:, r[1]:r[2]:r[3]]
    return T[r[0]][:, r[1]:r[2]]


def _count(r):
    return (r[2] - r[1] + (r[3] - 1 if len(r) == 4 else 0)) // (r[3] if len(r) == 4 else 1)


def _psum(name):
    return SCRATCH[name][0] == "psum" if name in SCRATCH else name[0] == "#"


def _cut(lo, hi, w):
    k = -(-(hi - lo) // w)
    b = [lo + 2 * ((hi - lo) * j // (2 * k)) for j in range(k)] + [hi]
    return list(zip(b[:-1], b[1:]))


def design():
    ops = []
    CY, GA, PEC, VF, SF, WAKE = (COST[k] for k in ("cy", "ga", "pe", "v", "s", "wake"))

    def op(eng, f, rd, wr, dur, lat=WAKE, name="", **kw):
        o = {"eng": eng, "f": f, "rd": [_span(r) for r in rd], "wr": [_span(r) for r in wr], "dur": dur, "lat": lat, "name": name}
        here[2][name] = here[2].get(name, 0) + 1
        o.update(kw, kind=(here[0], name, here[2][name]), tile=here[1])
        ops.append(o)

    here = ["start", 0, {}]

    def tt(out, a, b, alu, name="tt"):
        c = 1 if (_psum(a[0]) or _psum(b[0])) else 2
        op("V", lambda q, T: q.tensor_tensor(_ap(T, out), _ap(T, a), _ap(T, b), alu), [a, b], [out],
           VF + CY * max(64, c * _count(out)), name=name)

    def ts(out, a, s1, s2, op0, op1=None, name="ts"):
        aps = [s for s in (s1, s2) if isinstance(s, tuple)]
        two = all(not _psum(r[0]) and SCRATCH[r[0]][2] in (_B, _U, _H) for r in (out, a))

        def f(q, T):
            x1 = _ap(T, s1) if isinstance(s1, tuple) else s1
            x2 = _ap(T, s2) if isinstance(s2, tuple) else s2
            if op1 is None:
                return q.tensor_scalar(_ap(T, out), _ap(T, a), x1, None, op0)
            return q.tensor_scalar(_ap(T, out), _ap(T, a), x1, x2, op0, op1)
        op("V", f, [a] + aps, [out], VF + CY * max(64, (0.5 if two else 1) * _count(out)), name=name)

    def copy(out, a, name="copy"):
        op("V", lambda q, T: q.tensor_copy(_ap(T, out), _ap(T, a)), [a], [out], VF + CY * max(64, _count(out)), name=name)

    def memset(buf, lo, hi, val, p0=0, p1=128):
        op("V", lambda q, T: q.memset(T[buf][p0:p1, lo:hi], val), [], [(buf, lo, hi)], VF + CY * max(64, 0.5 * (hi - lo)), name="memset")

    def reduce(out, a, alu, name):
        op("V", lambda q, T: q.tensor_reduce(_ap(T, out), _ap(T, a), AxisListType.X, alu), [a], [out], VF + CY * max(64, _count(a)), name=name)

    def scan(out, a, b, first, op0, op1, name):
        aps = [first] if isinstance(first, tuple) else []
        op("V", lambda q, T: q.tensor_tensor_scan(_ap(T, out), _ap(T, a), _ap(T, b), _ap(T, first) if aps else first, op0, op1),
           [a, b] + aps, [out], VF + CY * max(64, _count(out)), name=name)

    def gtt(out, win, off, b, alu, name):
        op("V", lambda q, T: q.tensor_tensor(_ap(T, out), _ap(T, win).indirect(_ap(T, off)), _ap(T, b), alu), [win, off, b], [out],
           VF + 0.03 + CY * GA * _count(out), name=name, picks=_count(out))

    def gather(out, win, off, name, eng="S", sign=1.0):
        def f(q, T, e):
            x = _ap(T, win).indirect(_ap(T, off))
            if e == "S":
                return q.activation(_ap(T, out), x, ACT.Copy, scale=sign)
            return q.tensor_copy(_ap(T, out), x) if sign == 1.0 else q.tensor_scalar(_ap(T, out), x, sign, None, OP.mult)
        op(eng, f, [win, off], [out], 0.06 + CY * GA * _count(out), name=name, flex=True, picks=_count(out))

    def absS(out, a, name):
        op("S", lambda q, T: q.activation(_ap(T, out), _ap(T, a), ACT.Abs), [a], [out], SF + CY * _count(out), name=name)

    def scale(out, a, x, y=0.0, name="scale", eng="VS"):
        def f(q, T, e):
            if e == "V":
                return q.tensor_scalar(_ap(T, out), _ap(T, a), x, y, OP.mult, OP.add)
            return q.activation(_ap(T, out), _ap(T, a), ACT.Identity, bias=y, scale=x)
        op(eng, f, [a], [out], VF + CY * max(64, _count(out)), name=name, flex=True, slow=SF + CY * _count(out))

    def sub(a, b, name, plus="ident", minus="nident"):
        n = _count(a)
        out = ("#%d" % len(ops), 0, n)

        def f(q, T):
            for s in range(0, n, BANK):
                e = min(n, s + BANK)
                q.matmul(_ap(T, (out[0], s, e)), T[plus][:], T[a[0]][:, a[1] + s:a[1] + e], True, False)
                i = q.matmul(_ap(T, (out[0], s, e)), T[minus][:], T[b[0]][:, b[1] + s:b[1] + e], False, True)
            return i
        op("P", f, [a, b, (plus, 0, 128), (minus, 0, 128)], [out], PEC * 2 * n, name=name, lend=-(-n // BANK))
        return out

    def total(out, terms, const, plus, name, ends=(True, True), holds=None):
        n = out[2] - out[1]
        full = plus and SCRATCH[plus[0]][2] == _F
        first = ([((const + ("ones",))[2], (const[0], const[1], const[1] + n))] if const else []) + ([("identf" if full else "ident", plus)] if plus else [])

        def f(q, T):
            todo = [(T[m][:], _ap(T, x)) for m, x in first]
            todo += [(T[wb][:, 15 - p:143 - p], T[x[0]][:, x[1] + p:x[2]:16]) for x, wb in terms for p in range(16)]
            for j, (m, x) in enumerate(todo):
                i = q.matmul(_ap(T, out), m, x, ends[0] and j == 0, ends[1] and j == len(todo) - 1)
            return i
        op("P", f, [x for x, _ in terms] + [(wb, 0, 144) for _, wb in terms] + [x for _, x in first] + [(m, 0, 128) for m, _ in first], [holds or out],
           PEC * max(64, n) * (16 * len(terms) + (1 if const else 0) + (4 if full else 1 if plus else 0)), name=name, joint=bool(holds))

    nd = [0]

    def dma(q, fo, fi, rd, wr, name, nbytes=0):
        k = nd[0]
        nd[0] += 1
        op(q, lambda e, T: e.dma_start(fo(T), fi(T)), rd, wr, COST["issue"] if q == "G" else 0.06, lat=2.0 + nbytes / 200e3, name=name, dma="d%d" % k)

    def carry(out, a, add, name):
        k = nd[0]
        nd[0] += 1
        move = 256 * _count(out) / COST["dma"] * (COST["add"] if add else 1.0)
        if add:
            op("G", lambda e, T: e.dma_start(_ap(T, out), _ap(T, a), accum_op=OP.add), [a, out], [out], COST["issue"], lat=COST["hop"] + move,
               name=name, dma="d%d" % k, move=move)
        else:
            op("Y", lambda e, T: e.dma_start(_ap(T, out), _ap(T, a)), [a], [out], 0.06, lat=COST["hop"] + move, name=name, dma="d%d" % k, move=move)

    def iota(out, pat, base, cm, rows=(0, 128)):
        def f(q, T):
            o = T[out[0]][rows[0]:rows[1], out[1]:out[2]]
            if SCRATCH[out[0]][2] == _I:
                return q.iota(o, pat, base, cm)
            return q.iota(o, pat, base, cm, allow_small_or_imprecise_dtypes=True)
        op("G", f, [], [out], 0.13 + WAKE + 2 * CY * _count(out), name="iota")

    def asel(out, a, pat, cmp, base, cm, rows=(0, 128)):
        part = lambda T, r: T[r[0]][rows[0]:rows[1], r[1]:r[2]]
        op("G", lambda q, T: q.affine_select(part(T, out), part(T, a), pat, cmp, 0.0, base, cm), [a], [out],
           0.17 + WAKE + 2 * CY * _count(out), name="asel")

    tw = TW
    place = lambda bank, first, count, j, n: (bank, TW * (first + j % count), TW * (first + j % count) + n)

    dma("S", lambda T: T.fl[:, W:2 * W], lambda T: T.flood[:], [], [("fl", W, 2 * W)], "ld flood", 524288)
    dma("Y", lambda T: T.ri[:], lambda T: T.riv[:], [], [("ri", 0, P)], "ld riv", 131072)
    dma("Y", lambda T: T.bi[:], lambda T: T.bord[:], [], [("bi", 0, P)], "ld bord", 131072)
    dma("S", lambda T: T.fl[:, W - FO:W], lambda T: T.flood[:, W - FO:W], [], [("fl", W - FO, W)], "ld flood2", 700000)
    dma("Y", lambda T: T.thi[:], lambda T: T.th[:], [], [("thi", 0, 1)], "ld th")
    dma("G", lambda T: T.epi[:], lambda T: T.eps[:], [], [("epi", 0, 1)], "ld eps")

    memset("ones", 0, 128, 1.0)
    iota(("ipt", 0, 2), [[0, 2]], 0, 1)
    iota(("i16", 0, tw), [[16, tw]], 0, 0)
    asel(("ident", 0, 128), ("ones", 0, 128), [[-1, 128]], OP.is_equal, 0, 1)
    asel(("g8", 0, 8), ("ones", 0, 8), [[-16, 8]], OP.is_ge, 0, 1)
    asel(("g8b", 0, 8), ("g8", 0, 8), [[16, 8]], OP.is_ge, 15, -1)
    iota(("iot", 0, 32), [[1, 32]], P - L + 1, 0)
    memset("neg", 0, tw, -1.0)
    iota(("dgj", 0, 512), [[0, 32], [1, 16]], 0, 0)
    iota(("diag", 0, 512), [[0, 512]], 1, 0)
    asel(("seg", 0, 512), ("diag", 0, 512), [[0, 32], [1, 16]], OP.is_gt, 0, 0)
    scale(("nident", 0, 128), ("ident", 0, 128), -1.0)
    scale(("identf", 0, 128), ("ident", 0, 128), 1.0)
    memset("b1", 0, 144, 0.0)
    copy(("b1", 15, 143, 16), ("g8b", 0, 8))
    for w in (8192, 16384, 2):
        scale(("b%d" % w, 0, 144), ("b1", 0, 144), float(w))
    iota(("ck", 0, 5 * tw), [[0, 5 * tw]], -262144, 0, (0, 64))
    iota(("ck", 0, 5 * tw), [[32, 5], [0, tw]], 0, 0, (64, 128))
    cons = [(77 * t - FO) % W for t in range(ROUNDS)]
    iota(("cy", 0, 3 * tw), [[0, 3 * tw]], -2176, 0, (0, 64))
    for t in range(ROUNDS):
        iota(("cy", tw * t, tw * t + tw), [[0, tw]], cons[t] // 32, 0, (64, 96))
        asel(("cy", tw * t, tw * t + tw), ("ones", 0, tw), [[0, tw]], OP.is_gt, cons[t] % 32, -1, (96, 128))
    iota(("cz", 0, 2 * tw), [[0, 2 * tw]], -1088, 0, (0, 64))
    iota(("cz", 0, 2 * tw), [[-4096, 2], [0, tw]], 0, 0, (64, 96))
    memset("cz", 0, 2 * tw, FO / 32.0, 96, 128)
    ts(("ipt", 1, 2), ("ipt", 0, 1), 15, None, OP.bitwise_and)
    copy(("ipf", 0, 1), ("ipt", 1, 2))
    ts(("pv", 0, tw), ("i16", 0, tw), ("ipf", 0, 1), 1.0 / 512, OP.add, OP.mult)
    ts(("cpos", 0, tw), ("pv", 0, tw), 8.0, None, OP.add)
    ts(("diag", 0, 512), ("dgj", 0, 512), ("ipf", 0, 1), None, OP.is_equal)
    ts(("tha", 0, 1), ("thi", 0, 1), 2.0, -1.0, OP.mult, OP.add)
    copy(("epf", 0, 1), ("epi", 0, 1))
    ts(("epf", 1, 2), ("epi", 0, 1), -1.0, None, OP.mult)
    ts(("epf", 2, 3), ("epi", 0, 1), 2.0, 1.0, OP.mult, OP.add)
    op("V", lambda q, T: q.reciprocal(T.epf[:, 3:4], T.epf[:, 2:3]), [("epf", 2, 3)], [("epf", 3, 4)], 0.25, name="recip")
    ts(("sgp", 0, 128), ("ident", 0, 128), ("epf", 3, 4), None, OP.mult)
    for k in range(2):
        for buf, lo, hi, val in (("rf", 257, 264, FO), ("mf", 256, 264, FO), ("rp", 256, 264, 0), ("rm", 0, 1, 0), ("xr", 4096, 4112, 0)):
            iota(("%s_%d" % (buf, k), lo, hi), [[0, hi - lo]], val, 0)

    FL = ("fl", W, 2 * W)
    FC = ("fl", W - FO, 2 * W - FO + 160)
    FM = ("fl", W - FO, 2 * W)
    carry(("fl", 0, W - FO), ("fl", W, 2 * W - FO), False, "thrice")
    carry(("fl", 2 * W, 3 * W), FL, False, "thrice")
    cuts = [0] + [b + 2 for b in TILES[0][1:-1]] + [P]
    for j, (lo, hi) in enumerate(_cut(0, cuts[1], (cuts[1] + 3) // 2) + list(zip(cuts[1:-1], cuts[2:]))):
        copy(("ru0", lo, hi), ("ri", lo, hi), "R u16")
        gather(("xr_0", 16 * lo, 16 * hi), FL, ("ru0", lo, hi), "XR0", PLAN["first"][j] if j < len(PLAN["first"]) else "S")
    ts(("rf_0", 1, 257), ("ri", 0, 256), float(FO), None, OP.add)
    copy(("rn_0", 0, 256), ("ri", 0, 256))
    copy(("rf_0", 0, 1), ("rf_0", 1, 2))
    ts(("mf_0", 0, 256), ("bi", 0, 256), float(FO), None, OP.add)
    ts(("mu_0", 0, P), ("bi", 0, P), float(FO), None, OP.add, name="M u16")
    for lo, hi in zip(TILES[0][:-1], TILES[0][1:]):
        gather(("xm", 16 * lo, 16 * hi), FM, ("mu_0", lo, hi), "XM0", PLAN["eng"][3], -1.0)

    tiles = [(t, k) for t in range(ROUNDS) for k in range(len(TILES[t]) - 1)]
    written = [np.zeros(5 * CE, bool) for _ in range(NB)]

    def step1(j):
        t, k = tiles[j]
        c0, c1 = TILES[t][k], TILES[t][k + 1]
        n = c1 - c0
        here[:] = ["choose", j, {}]
        late = j >= len(tiles) - PLAN["tail"]
        z = t % 2
        rn, rf, mf, xr, xp = ("%s_%d" % (x, z) for x in ("rn", "rf", "mf", "xr", "xp"))
        pr, v, u, fs, js, ou, win, now, nb, hb = ("%s_%d" % (x, j % NB) for x in ("pr", "v", "u", "fs", "js", "ou", "win", "now", "nb", "hb"))
        s0 = BANK * (j % NB)
        S = lambda a, b=1: ("sc", s0 + a * n, s0 + (a + b) * n)
        F = lambda a, b=1: (fs, a * TW, a * TW + b * n)
        J = lambda a: (js, a * TW, a * TW + n)
        X = lambda m, b=1: (win, CE * m, CE * (m + b - 1) + 16 * n)
        R16 = place("pv", 1, 3, j, n)
        ts(R16, (rn, c0, c1), 16.0, None, OP.add, name="R16")
        for m, (bf, o) in enumerate(((rf, c0), (rf, c0 + 2), (mf, c0), (mf, c0 + 1))):
            tt((pr, n * m, n * m + n), R16, (bf, o, o + n), OP.mult, name="prod")
        for h0, h1 in ((0, 2 * n), (2 * n, 4 * n)) if PLAN["split"] == 2 or late else ((0, 4 * n),):
            ts((v, h0, h1), (pr, h0, h1), 4, W - 1, OP.arith_shift_right, OP.bitwise_and, name="v")
            ts((u, h0, h1), (v, h0, h1), 77.0 * t, None, OP.add, name="u")
        mode = PLAN["mode"][t][k] + "T"
        nxt = (xr, 16 * (c0 + 1), 16 * (c1 + 1))
        x = (now, 0, 16 * n)
        if mode[5] == "T":
            for a, c in _cut(c0, c1, PLAN["wide"][0]):
                absS((now, 16 * (a - c0), 16 * (c - c0)), sub((xr, 16 * a, 16 * c), (xr, 16 * a + 16, 16 * c + 16), "now-"), "now||")
        else:
            ts(x, (xr, 16 * c0, 16 * c1), -1.0, None, OP.mult, name="now-")
            carry(x, nxt, True, "now+")
            if mode[5] == "e":
                absS(x, x, "now||")
            else:
                ts((hb, 3 * CE, 3 * CE + 16 * n), x, -2.0, 0.0, OP.mult, OP.max, name="relu")
                carry(x, (hb, 3 * CE, 3 * CE + 16 * n), True, "+relu")
        for m in (4, 0, 1, 2, 3):
            if mode[m] == "T":
                for a, c in _cut(c0, c1, PLAN["wide"][1]):
                    x = sub(("xm", 16 * a, 16 * c), (xr, 16 * a + 16, 16 * c + 16), "c5-", "ident", "ident")
                    absS((win, CE * m + 16 * (a - c0), CE * m + 16 * (c - c0)), x, "c5||")
            elif m == 4:
                carry(X(m), nxt, False, "c5=")
                carry(X(m), ("xm", 16 * c0, 16 * c1), True, "c5+")
            elif mode[m] in "eh":
                gather(X(m), FC, (u, n * m, n * m + n), "candS", "S", -1.0)
                carry(X(m), nxt, True, "+next")
            else:
                for a, c in _cut(0, n, PLAN["cand"][m]):
                    gtt((win, CE * m + 16 * a, CE * m + 16 * c), FC, (u, n * m + a, n * m + c),
                        (xr, 16 * (c0 + a + 1), 16 * (c0 + c + 1)), OP.subtract, "cand")
        m, at = 0, 0
        while m < 5:
            far = mode[m] in "gh"
            b = 1 + (m < 4 and n == TW and mode[m] != "T" and mode[m + 1] != "T" and far == (mode[m + 1] in "gh")
                     and PLAN["join" if far else "pair"] and not late)
            if far:
                h = (hb, at, at + _count(X(m, b)))
                at = h[2]
                if PLAN["half"]:
                    for i in range(b):
                        ts((hb, h[1] + i * CE, h[1] + i * CE + 16 * n), X(m + i), -2.0, 0.0, OP.mult, OP.max, name="relu")
                else:
                    ts(h, X(m, b), -2.0, 0.0, OP.mult, OP.max, name="relu")
                carry(X(m, b), h, True, "+relu")
            elif mode[m] != "T":
                absS(X(m, b), X(m, b), "cand||")
            m += b
        seen = written[j % NB]
        for m in range(5):
            seen[CE * m:CE * m + 16 * n] = True
        for m in range(4):
            gap = np.flatnonzero(~seen[CE * m:CE * (m + 1)])
            if len(gap):
                a, c = CE * m + int(gap[0]), CE * m + int(gap[-1]) + 1
                iota((win, a, c), [[0, c - a]], 0, 0)
                seen[a:c] = True
        for m in (4, 0, 1, 2, 3):
            total(S(m), [(X(m), "b8192")], ("ck", tw * m), None, "score")
        kb, kc, w, o, me, d = F(0, 2), F(2), F(3), F(4), F(5), F(6)
        k4, ka, kv, rr = J(0), J(1), J(2), J(3)
        tt(S(0, 2), S(0, 2), (v, 0, 2 * n), OP.add, "key")
        tt(kb, S(2, 2), (v, 2 * n, 4 * n), OP.add, "key")
        tt(kc, S(0), (fs, 0, n), OP.min, "kmin")
        tt(S(1), S(1), (fs, n, 2 * n), OP.min, "kmin")
        tt(k4, S(1), kc, OP.min, "kmin")
        tt(S(0), S(4), k4, OP.is_le, "m5")
        ts(kv, k4, W - 1, None, OP.bitwise_and, name="kv")
        ts(me, (mf, c0, c1), 4096.0 - cons[t] - FO, None, OP.add, name="me")
        ts(ka, k4, 6144, 10, OP.bitwise_and, OP.arith_shift_right, name="ka")
        tt(S(1), S(0), ("cpos", 0, n), OP.mult, "uu")
        tt(w, ("pv", 0, n), ka, OP.add, "w")
        tt(o, S(1), w, OP.max, "o")
        ts((ou, 0, n), o, 512.0, None, OP.mult, name="ou")
        tt(S(2), S(0), me, OP.mult, "t5")
        tt(d, S(2), kv, OP.max, "d")
        yield
        here[:] = ["accept", j, {}]
        whole = (win, 0, 4 * CE + 16 * n)
        for a, c in _cut(0, n, 32 if late else PLAN["cand"][4]):
            gtt((nb, 16 * a, 16 * c), whole, (ou, a, c), (now, 16 * a, 16 * c), OP.is_lt, "nearer")
        Z = S(5)
        total(Z, [((nb, 0, 16 * n), "b16384")], ("cy", tw * t), d if late or PLAN["plus"] else None, "cnt1")
        if not (late or PLAN["plus"]):
            tt(Z, Z, d, OP.add, "z")
        tt(rr, Z, (rn, c0, c1), OP.max, "rr")
        rp, rpu = "rp_%d" % z, "rpu_%d" % z
        e = n - (c1 == P)
        ts((rp, c0, c0 + e), (js, 3 * TW, 3 * TW + e), W - 1, None, OP.bitwise_and, name="R'")
        if c1 == P:
            copy((rp, 255, 256), (rn, 255, 256), "R'255")
        copy((rpu, c0, c1), (rp, c0, c1), "R'u")
        for a, c in _cut(c0, c1, 32 if late else PLAN["plain"]):
            gather((xp, 16 * a, 16 * c), FL, (rpu, a, c), "XR'", "VS" if late else PLAN["eng"][0])

    def piece(j):
        t, k = tiles[j]
        return max(0, TILES[t][k] - L), TILES[t][k + 1] - L

    def necks(j):
        t, k = tiles[j]
        lo, hi = piece(j)
        here[:] = ["necks", j, {}]
        if k == 0:
            ts(("thb", 2 * TW * t, 2 * TW * t + tw), ("neg", 0, tw), ("tha", t, t + 1), None, OP.mult, name="thb")
            ts(("thf", 0, tw), ("thb", 2 * TW * t, 2 * TW * t + tw), ("tha", t, t + 1), -1.0, OP.add, OP.mult, name="thb")
            copy(("thb", 2 * TW * t + tw, 2 * TW * t + 2 * tw), ("thf", 0, tw), "thb")
        if hi <= lo:
            return
        late = j >= len(tiles) - PLAN["tail"]
        xp, rm, a2 = "xp_%d" % (t % 2), "rm_%d" % (t % 2), "a2_%d" % (j % NB)
        n = hi - lo
        ds = ("sc", BANK * (j % NB) + 6 * TW, BANK * (j % NB) + 6 * TW + n)
        for a, c in _cut(lo, hi, 32 if late else PLAN["wide"][2]):
            absS((a2, 16 * (a - lo), 16 * (c - lo)), sub((xp, 16 * a, 16 * c), (xp, 16 * (a + L), 16 * (c + L)), "nk-"), "nk||")
        total(ds, [((a2, 0, 16 * n), "b2")], ("thb", 2 * TW * t + tw, "ident"), ("thb", 2 * TW * t, 2 * TW * t + n), "dist")
        scan((rm, 1 + lo, 1 + hi), ds, ("neg", 0, n), (rm, lo, lo + 1), OP.min, OP.max, "rm")

    def loops(j):
        t, k = tiles[j]
        lo = piece(j)[0]
        here[:] = ["loops", j, {}]
        rm, rp = "rm_%d" % (t % 2), "rp_%d" % (t % 2)
        c = lambda i: ("nk", 8 * t + i, 8 * t + i + 1)
        end = (rm, P - L, P - L + 1)
        lout = ("lout%d" % t, 0, 32)
        reduce(c(0), (rm, 1, 1 + lo), OP.add, "ge")
        reduce(c(1), (rm, 1 + lo, 1 + P - L), OP.add, "ge2")
        ts(("lu", 0, 32), ("iot", 0, 32), c(0), c(1), OP.add, OP.add, name="lu")
        ts(c(2), end, -10240.0, -8192.0, OP.mult, OP.add, name="fl")
        gtt(("lg", 0, 512), (rp, 0, 264), ("lu", 0, 32), ("diag", 0, 512), OP.mult, "loop")
        scan(("ls", 0, 512), ("seg", 0, 512), ("lg", 0, 512), 0.0, OP.mult, OP.add, "scan")
        own = ("ls", 15, 512, 16)
        ts(lout, own, c(2), None, OP.add, name="lout")
        op("G", None, [lout], [("sent", t, t + 1)], 1.0, lat=0.0, name="send", send=t)
        op("N", None, [("sent", t, t + 1)], [("land%d" % t, 0, 32)], 0.0, lat=COST["net"], name="recv", recv=t)
        ts(("tha", t + 1, t + 2), end, -32.0, ("tha", t, t + 1), OP.mult, OP.add, name="A")
        ts(c(4), end, 12288.0, 4096.0, OP.mult, OP.add, name="l0")
        ts(("lo", 32, 64), (rp, P - L, P), c(4), None, OP.add, name="l0")
        tt(("lo", 0, 32), own, ("lo", 32, 64), OP.max, "l0")

    def moved(t, k, lo, hi, s):
        z, y = t % 2, (t + 1) % 2
        last, end = t == ROUNDS - 1, hi == P
        n = hi - lo
        if n <= 0:
            return
        here[:] = ["landed" if end else "last" if last else "moved", tiles.index((t, k - end)), {}]
        a3, c3, fs, js = ("%s_%d" % (x, s) for x in ("a3", "c3", "fs", "js"))
        cn = ("sc", BANK * s + 7 * TW, BANK * s + 7 * TW + n)
        rp, rm, u = "rp_%d" % z, ("rm_%d" % z, lo, hi), "r2u_%d" % z
        rn = ("yrf", lo, hi) if last else ("rn_%d" % y, lo, hi)
        if not end:
            df, ix = place("pv", 4, 3, s, n), (fs, 7 * TW, 7 * TW + n)
            tt(ix, ("pv", 0, n), rm, OP.subtract, "ix")
            ts((u, lo, hi), ix, 512.0, None, OP.mult, name="R''u")
            tt(df, (rp, lo, hi), (rp, lo + L, hi + L), OP.subtract, "df")
            tt(df, df, rm, OP.mult, "dm")
            tt(rn, df, (rp, lo, hi), OP.add, "R''")
            src = ("xp_%d" % z, 16 * lo, 16 * (hi + L))
        else:
            tt(("lx", 0, 32), ("land%d" % t, 0, 32), ("lo", 0, 32), OP.max, "l1")
            ts(("lx", 32, 64), ("lx", 0, 32), W - 1, None, OP.bitwise_and, name="l2")
            copy((u, lo, hi), ("lx", 0, 32), "R''u")
            copy(rn, ("lx", 32, 64), "R f")
            src = ("fl", 0, 3 * W)
        if last and end:
            x3, c4, c5 = (a3, 0, 16 * n), (c3, 0, 16 * n), (c3, 16 * n, 32 * n)
            gtt(x3, src, (u, lo, hi), ("xm", 16 * lo, 16 * hi), OP.add, "cand")
            ts(c4, x3, ("epf", 0, 1), None, OP.is_le, name="c3")
            ts(c5, x3, ("epf", 1, 2), None, OP.is_ge, name="c3")
            bank = ("sc", BANK * s, BANK * s + BANK)
            total(cn, [], ("cz", tw), rn, "cnt3", (True, False), bank)
            total(cn, [(c4, "b8192")], None, None, "cnt3", (False, False), bank)
            total(cn, [(c5, "b8192")], None, None, "cnt3", (False, True), bank)
        else:
            xr = "xr_%d" % y
            for a, c in _cut(lo, hi, PLAN["plain"]):
                gather((xr, 16 * a, 16 * c), src, (u, a, c), "XR''", PLAN["eng"][1])
            if not last:
                rf = "rf_%d" % y
                ts((rf, lo + 1, hi + 1), rn, float(FO), None, OP.add, name="rf")
                if lo == 0:
                    copy((rf, 0, 1), (rf, 1, 2), "rf0")
            sizes = (t, k) in PLAN["acS"]
            for a, c in _cut(lo, hi, PLAN["wide"][4 if sizes else 3]):
                h = (16 * (a - lo), 16 * (c - lo))
                if sizes:
                    absS((a3,) + h, sub((xr, 16 * a, 16 * c), ("xm", 16 * a, 16 * c), "ac-", "ident", "ident"), "ac||")
                else:
                    ts((c3,) + h, sub((xr, 16 * a, 16 * c), ("xm", 16 * a, 16 * c), "ac-", "sgp", "sgp"), BIG, BIG, OP.add, OP.is_equal, name="ac=")
            if sizes:
                ts((c3, 0, 16 * n), (a3, 0, 16 * n), ("epf", 0, 1), None, OP.is_le, name="c3")
            total(cn, [((c3, 0, 16 * n), "b8192")], ("cz", 0), None if last else rn, "cnt3")
            if last:
                tt(cn, cn, rn, OP.add, "z3")
        mm, mf = (js, 4 * TW, 4 * TW + n), ("mf_%d" % y, lo, hi)
        tt(mm, cn, ("mf_%d" % z, lo, hi), OP.max, "mm")
        ts(mf, mm, 2 * W - 1, None, OP.bitwise_and, name="M'")
        if last:
            ts(("ymf", lo, hi), mf, -float(FO), None, OP.add, name="M f")
            return
        mu = "mu_%d" % y
        copy((mu, lo, hi), mf, "M'u")
        for a, c in _cut(lo, hi, PLAN["plain"]):
            gather(("xm", 16 * a, 16 * c), FM, (mu, a, c), "XM'", PLAN["eng"][2], -1.0)

    def whole(j):
        t, k = tiles[j]
        final = TILES[t][k + 1] == P
        yield from step1(j)
        yield
        necks(j)
        if final:
            loops(j)
        yield
        if t < ROUNDS - 1:
            moved(t, k, *piece(j), j % NB)
        elif final:
            for i in range(k + 1):
                moved(t, i, *piece(j - k + i), (j + i + 1) % NB)
            moved(t, k + 1, P - L, P, (j + k + 2) % NB)
        yield

    runs = [whole(j) for j in range(len(tiles))]
    part = [0] * len(tiles)

    def upto(j, p):
        for i in range(max(0, j + 1)):
            while part[i] < p:
                next(runs[i])
                part[i] += 1

    ended = 0
    for j, (t, k) in enumerate(tiles):
        for p in (4, 3, 2):
            upto(j - PLAN["lag"][p - 2], p)
        upto(max([i for i in range(j) if tiles[i][0] < t and piece(i)[0] <= TILES[t][k + 1]], default=-1), 4)
        if ended < t and TILES[t][k + 1] >= P - L:
            moved(ended, len(TILES[ended]) - 1, P - L, P, (j + 1) % NB)
            ended += 1
        upto(j, 1)
    for p in (2, 3, 4):
        upto(len(tiles) - 1, p)
    here[:] = ["start", 0, {}]
    ts(("aout", 1, 2), ("tha", ROUNDS, ROUNDS + 1), ("tha", 0, 1), 1.0 / 32, OP.subtract, OP.mult)
    dma("Y", lambda T: T.ya[:], lambda T: T.aout[:, 1:2], [("aout", 1, 2)], [], "st ya")
    dma("Y", lambda T: T.yr[:, 0:224], lambda T: T.yrf[:, 0:224], [("yrf", 0, 224)], [], "st yr")
    dma("Y", lambda T: T.ym[:, 0:224], lambda T: T.ymf[:, 0:224], [("ymf", 0, 224)], [], "st ym")
    dma("Y", lambda T: T.yr[:, 224:256], lambda T: T.yrf[:, 224:256], [("yrf", 224, 256)], [], "st yr")
    dma("Y", lambda T: T.ym[:, 224:256], lambda T: T.ymf[:, 224:256], [("ymf", 224, 256)], [], "st ym")
    return ops


def depend(ops):
    acc = {}
    for i, o in enumerate(ops):
        dep = set()
        touches = [(r, False) for r in o["rd"]] + [(r, True) for r in o["wr"]]
        for (buf, lo, hi), wr in touches:
            for (j, l2, h2, w2) in acc.setdefault(buf, []):
                if j != i and lo < h2 and l2 < hi and (wr or w2):
                    dep.add(j)
        for (buf, lo, hi), wr in touches:
            lst = acc[buf]
            if wr:
                lst[:] = [a for a in lst if not (lo <= a[1] and a[2] <= hi)]
            lst.append((i, lo, hi, wr))
        o["dep"] = dep
        o["banks"] = {(buf, b) for (buf, lo, hi), _ in touches if buf in SCRATCH and _psum(buf) for b in range(lo // BANK, (hi - 1) // BANK + 1)}


def lay(ops, rank, before, behind, back):
    n = len(ops)
    left = [len(x) for x in before]
    at = [ops[i]["lat"] if back else 0.0 for i in range(n)]
    free = {e: 0.0 for e in "VSPGYND"}
    ready = {e: [] for e in "VSPGYN"}
    held, out = {}, {}
    lent = [0.0] * FREE
    takes = {i + back: o["lend"] for i, o in enumerate(ops) if "lend" in o}
    for i in range(n):
        if not left[i]:
            for e in ops[i]["eng"]:
                ready[e].append(i)

    def room(k):
        return min((max(lent[b:b + k]), b) for b in range(0, FREE - k + 1, k))

    def when(i, e):
        t = at[i]
        for b in ops[i]["banks"]:
            for x, f in held.get(b, {}).items():
                if x != e and f > t:
                    t = f
        return max(t, room(takes[i])[0]) if i in takes else t
    while len(out) < n:
        t, e = min((max(free[e], min(when(i, e) for i in ready[e])), e) for e in ready if ready[e])
        i = max(ready[e], key=lambda j: (rank[j] - PLAN["haste"] * max(0.0, when(j, e) - t), j if back else -j))
        t = max(t, when(i, e))
        o = ops[i]
        for x in o["eng"]:
            ready[x].remove(i)
        dur = o["slow"] if e == "S" and "slow" in o else o["dur"]
        if e != "N":
            free[e] = t + dur
        end = t + dur + (0.0 if back else o["lat"])
        if "move" in o and not back:
            free["D"] = max(t + dur, free["D"]) + o["move"]
            end = free["D"] + o["lat"] - o["move"]
        b = None
        if i in takes:
            b = room(takes[i])[1]
            lent[b:b + takes[i]] = [1e9] * takes[i]
        mate = i + 1 if back else i - 1
        if mate in takes:
            b = out[mate][4]
            lent[b:b + takes[mate]] = [t + dur + COST["wake"]] * takes[mate]
        out[i] = (t, end, e, len(out), b)
        for x in o["banks"]:
            held.setdefault(x, {})[e] = t + dur + COST["wake"]
        for j in behind[i]:
            at[j] = max(at[j], end + (ops[j]["lat"] if back else 0.0) + (COST["same"] - COST["wake"] if ops[j]["eng"] == e else 0.0))
            left[j] -= 1
            if not left[j]:
                for x in ops[j]["eng"]:
                    ready[x].append(j)
    return out


def arrange(ops):
    n = len(ops)
    pred = [o["dep"] for o in ops]
    ways = []
    for back in (0, 1):
        before = [set() if back else set(x) for x in pred]
        for i in range(n) if back else ():
            for j in pred[i]:
                before[j].add(i)
        for i, o in enumerate(ops):
            if "lend" in o:
                before[i + back] |= before[i + 1 - back] - {i + back}
        behind = [[] for _ in ops]
        for i in range(n):
            for j in before[i]:
                behind[j].append(i)
        ways.append((before, behind))
    rank = [0.0] * n
    for i in range(n - 1, -1, -1):
        rank[i] = ops[i]["dur"] + ops[i]["lat"] + max([rank[j] for j in ways[0][1][i]], default=0.0)
    best, rng = None, np.random.default_rng(PLAN["seed"])
    for turn in range(PLAN["passes"]):
        if best:
            home = lay(ops, [best[1][i][1] + x for i, x in enumerate(rng.normal(0.0, PLAN["shake"], n))], *ways[1], True)
            rank = [home[i][1] for i in range(n)]
        there = lay(ops, rank, *ways[0], False)
        seq = sorted(range(n), key=lambda i: there[i][3])
        deps, last, fill = {}, {}, set()
        for i in seq:
            e, d = there[i][2], set(pred[i])
            if e == "G" and ops[i]["f"] and "dma" not in ops[i]:
                d, fill = d | fill, {i}
            banks = set(ops[i]["banks"])
            if there[i][4] is not None:
                banks |= {("sub", there[i][4] + b) for b in range(ops[i if "lend" in ops[i] else i - 1]["lend"])}
            for b in banks:
                d |= {j for x, j in last.setdefault(b, {}).items() if x != e}
                last[b][e] = i
            deps[i] = d
        worth = sum(replay(ops, seq, there, deps, *x) for x in RANGE)
        if best is None or worth <= best[0]:
            best = (worth, there, seq, deps)
    on = [best[1][i][2] for i in range(n)]
    worth, seq, more, got = polish(ops, on, best[2])
    order = {e: [] for e in "VSPGYN"}
    for turn, i in enumerate(seq):
        o = ops[i]
        o["t0"], o["on"], o["turn"], o["dep"] = best[1][i][0], on[i], turn, pred[i] | set(more[i])
        if on[i] == "S" and "slow" in o:
            o["dur"] = o["slow"]
        if "lend" in o:
            LENT[o["wr"][0][0]] = got[i]
        order[on[i]].append(i)
    return order, worth


def polish(ops, on, seq):
    n, rng = len(ops), np.random.default_rng(PLAN["seed"])
    pred = [o["dep"] for o in ops]
    succ = [set() for _ in ops]
    above, near = [], []
    for i in range(n):
        far = set().union(*[above[j] for j in pred[i]])
        near.append([j for j in pred[i] if j not in far])
        above.append(far | pred[i])
        for j in pred[i]:
            succ[j].add(i)
    ends = [i for i in range(n) if not succ[i]]
    own = [[j for j in near[i] if on[j] == on[i] and not (ops[i].get("joint") and ops[j].get("joint"))] for i in range(n)]
    other = [[j for j in near[i] if on[j] != on[i]] for i in range(n)]
    banks = [sorted(o["banks"]) for o in ops]
    lend = [o.get("lend", 0) for o in ops]
    fill = [on[i] == "G" and bool(o["f"]) and "dma" not in o for i, o in enumerate(ops)]
    move = ["move" in o for o in ops]
    cases = []
    for wake, same, ga, pe, slow, rest in RANGE:
        dur = [(o["slow"] if on[i] == "S" and "slow" in o else o["dur"] * (pe / COST["pe"] if on[i] == "P" else slow if move[i] else 1.0))
               + o.get("picks", 0) * COST["cy"] * (ga - COST["ga"]) for i, o in enumerate(ops)]
        lat = [(o["lat"] - o["move"]) * slow if "move" in o else wake if o["lat"] == COST["wake"] else o["lat"] * rest for o in ops]
        cases.append((dur, lat, [o.get("move", 0.0) * slow for o in ops], same - wake))

    names = sorted({b for x in banks for b in x})
    eng = ["VSPGYN".index(e) for e in on]
    meets = [[(3 * names.index(b) + eng[i], [3 * names.index(b) + y for y in range(3) if y != eng[i]]) for b in banks[i]] for i in range(n)]
    plain = [not (lend[i] or lend[i - 1] or fill[i] or move[i]) for i in range(n)]
    at_last, at_lent, at_fill = 6, 6 + 3 * len(names), 6 + 3 * len(names) + 3 * FREE

    def links(seq, a, b, old):
        more, ahead, moved, got, kept = (x[:] for x in old)
        st = kept[a // STEP][:]
        for pos in range(a - a % STEP, n):
            if not pos % STEP:
                if pos > b and st == kept[pos // STEP]:
                    break
                kept[pos // STEP] = st[:]
            i = seq[pos]
            x = other[i]
            for mine, theirs in meets[i]:
                x = x + [st[at_last + y] for y in theirs if st[at_last + y] >= 0]
                st[at_last + mine] = i
            if not plain[i]:
                k = lend[i]
                if k:
                    room = [(max(st[c + 2], st[c + 3 * k - 1]), c) for c in range(at_lent, at_fill - 3 * k + 1, 3 * k)
                            if st[c] < 0 and st[c + 3 * k - 3] < 0]
                    if not room:
                        return None
                    got[i] = c = min(room)[1]
                    for c in range(c, c + 3 * k, 3):
                        st[c] = i
                        if st[c + 1] >= 0:
                            x = x + [st[c + 1]]
                elif lend[i - 1]:
                    for c in range(got[i - 1], got[i - 1] + 3 * lend[i - 1], 3):
                        st[c:c + 3] = -1, i, pos
                elif fill[i]:
                    if st[at_fill] >= 0:
                        x = x + [st[at_fill]]
                    st[at_fill] = i
                else:
                    moved[i] = st[at_fill + 1]
                    st[at_fill + 1] = i
            more[i] = x
            e = eng[i]
            if e < 5:
                ahead[i] = st[e]
                st[e] = i
        return more, ahead, moved, got, kept

    def run(seq, a, b, link, case, old):
        more, ahead, moved, _, kept = link
        dur, lat, bytes_, extra = case
        was, fin, over, why, gone = old[1], old[0][:], old[1][:], old[2][:], old[3][:]
        reach = b
        for pos in range(a, n):
            if pos > reach and not pos % STEP and all(over[kept[pos // STEP][c]] == was[kept[pos // STEP][c]] for c in ids) \
                    and all(fin[x] == old[0][x] for x in kept[pos // STEP][:5]):
                break
            i = seq[pos]
            w = ahead[i]
            t = fin[w]
            for j in more[i]:
                if over[j] > t:
                    t, w = over[j], j
            for j in own[i]:
                if over[j] + extra > t:
                    t, w = over[j] + extra, j
            t += dur[i]
            fin[i] = t
            if bytes_[i]:
                if gone[moved[i]] > t:
                    w = moved[i]
                    t = gone[w]
                gone[i] = t = t + bytes_[i]
            why[i] = w
            t += lat[i]
            over[i] = t
            if t != was[i] and last[i] > reach:
                reach = last[i]
        return fin, over, why, gone, max([over[i] for i in ends])

    ids = [c for c in range(at_fill + 2) if c < at_lent or c >= at_fill or (c - at_lent) % 3 == 1]
    where, users = [0] * n, [[] for _ in ops]
    for i in range(n):
        where[seq[i]] = i
        for j in near[i]:
            users[j].append(i)
    last = [max([where[j] for j in x], default=0) for x in users]
    link = links(seq, 0, n, (other, [-1] * n, [-1] * n, [-1] * n, [[-1] * (at_fill + 2)] * (n // STEP + 1)))
    now = [run(seq, 0, n, link, c, ([0.0] * (n + 1), [0.0] * (n + 1), [-1] * n, [0.0] * (n + 1))) for c in cases]
    worth = sum(r[4] for r in now)
    best, paths = (worth, seq, link[0], link[3]), {}
    for turn in range(PLAN["swaps"]):
        k = int(rng.integers(len(cases)))
        if k not in paths:
            i, paths[k] = max(ends, key=lambda x: now[k][1][x]), []
            while now[k][2][i] >= 0:
                u = now[k][2][i]
                if i not in succ[u]:
                    paths[k].append((u, i))
                i = u
        u, v = paths[k][int(rng.integers(len(paths[k])))]
        forward = rng.random() < 0.5
        while rng.random() < PLAN["jump"]:
            if forward:
                u = link[1][u] if link[1][u] >= 0 else u
            else:
                at = where[v]
                v = next((y for y in seq[at + 1:at + 40] if link[1][y] == v), v)
        a, b = where[u], where[v]
        mid = seq[a:b + 1]
        if forward:
            go = {v}
            for x in mid[-2::-1]:
                if not succ[x].isdisjoint(go):
                    go.add(x)
        else:
            go = {u}
            for x in mid[1:]:
                if not pred[x].isdisjoint(go):
                    go.add(x)
        if u in go and v in go:
            continue
        trial = seq[:]
        trial[a:b + 1] = [x for x in mid if (x in go) == forward] + [x for x in mid if (x in go) != forward]
        new = links(trial, a, b, link)
        if new is None:
            continue
        allow = -PLAN["heat"] * (1.0 - turn / PLAN["swaps"]) * len(cases) * math.log(1.0 - rng.random())
        first = run(trial, a, b, new, cases[k], now[k])
        if first[4] - now[k][4] > allow + 0.3:
            continue
        then = [first if j == k else run(trial, a, b, new, cases[j], now[j]) for j in range(len(cases))]
        if sum(r[4] for r in then) <= worth + allow:
            worth, seq, now, link, paths = sum(r[4] for r in then), trial, then, new, {}
            for i in range(a, b + 1):
                where[seq[i]] = i
            for j in {j for i in mid for j in near[i]}:
                last[j] = max([where[x] for x in users[j]])
            if worth < best[0]:
                best = (worth, seq, link[0], link[3])
    return best[:3] + ([(c - at_lent) // 3 for c in best[3]],)


def replay(ops, seq, laid, deps, wake, same, ga, pe, slow, rest):
    free, over = {}, {}
    for i in seq:
        o, e = ops[i], laid[i][2]
        t = max([free.get(e, 0.0)] + [over[j] + (same - wake if laid[j][2] == e else 0.0) for j in deps[i]
                                      if not (o.get("joint") and ops[j].get("joint"))])
        t += (o["slow"] if e == "S" and "slow" in o else o["dur"] * pe / COST["pe"] if e == "P" else o["dur"]) + o.get("picks", 0) * COST["cy"] * (ga - COST["ga"])
        if "move" in o:
            free[e] = t + o["dur"] * (slow - 1.0)
            free["D"] = max(free[e], free.get("D", 0.0)) + o["move"] * slow
            over[i] = free["D"] + (o["lat"] - o["move"]) * slow
            continue
        if e != "N":
            free[e] = t
        over[i] = t + (wake if o["lat"] == COST["wake"] else o["lat"] * rest)
    return max(over.values())


_made = {}


def made():
    if not _made:
        ops = design()
        depend(ops)
        order, end = arrange(ops)
        _made["ops"], _made["order"], _made["end"] = ops, order, end
        num = {}
        for e in "VSPG":
            c = 0
            for i in order[e]:
                if "dma" in ops[i] or "send" in ops[i]:
                    continue
                c += 1
                num[i] = c
        _made["num"] = num
        pos = {i: n for e in order for n, i in enumerate(order[e])}
        state = {e: {} for e in order}
        after = {}
        waits = {}
        todo = {e: 0 for e in order}
        ndone = 0
        while ndone < len(ops):
            for e in order:
                while todo[e] < len(order[e]) and all(j in after for j in ops[order[e][todo[e]]]["dep"]):
                    i = order[e][todo[e]]
                    o = ops[i]
                    st = state[e] if e != "N" else {}
                    need = {}
                    for j in o["dep"]:
                        key, val = _key(j, ops, num)
                        if o.get("joint") and ops[j].get("joint"):
                            continue
                        if key is not None and st.get(key, 0) < val and need.get(key, (0, 0))[0] < val:
                            need[key] = (val, j)
                    out = []
                    for key, (val, j) in sorted(need.items(), key=lambda kv: -pos[kv[1][1]]):
                        if st.get(key, 0) >= val:
                            continue
                        out.append((key, val))
                        for a, c in after[j].items():
                            st[a] = max(st.get(a, 0), c)
                        st[key] = max(st.get(key, 0), val)
                    waits[i] = out
                    me = dict(st) if e != "N" else {}
                    key, val = _key(i, ops, num)
                    if key is not None:
                        me[key] = val
                    after[i] = me
                    todo[e] += 1
                    ndone += 1
        _made["waits"] = waits
    return _made


def _key(i, ops, num):
    o = ops[i]
    if "dma" in o:
        return o["dma"], 16
    if "send" in o:
        return None, 0
    if "recv" in o:
        return "arr%d" % o["recv"], 8
    return "s" + o["on"], num[i]


def rank_program(g, core, T, topo):
    rank = T.rank_of(core)
    if rank is None:
        return
    m = made()
    ops, order, waits = m["ops"], m["order"], m["waits"]
    queues = {"V": g.vector, "S": g.scalar, "P": g.tensor, "G": g, "Y": g.sync}
    sent = 0
    for e in ("G", "Y", "S", "V", "P"):
        q = queues[e]
        for i in order[e]:
            o = ops[i]
            for key, val in waits[i]:
                q.wait_ge(T.sem[key], val)
            if "send" in o:
                t = o["send"]
                dst = T.cores[(rank + 1 + t % (N - 1)) % N]
                rid, pid, _ = topo.addr(dst)
                eng = topo.engines(core, dst)[:8]
                g.remote_dma(out_ap=T["land%d" % t][:], in_ap=T["lout%d" % t][:], remote_sem=T.sem["arr%d" % t], local_sem=T.sem.ls,
                             pid=pid, routing_id=rid, dma_engine_mask=sum(1 << x for x in eng))
                sent += len(eng)
            elif "dma" in o:
                o["f"](q, T).then_inc(T.sem[o["dma"]], 16)
            elif "flex" in o:
                o["f"](q, T, e).then_inc(T.sem["s" + e], 1)
            else:
                o["f"](q, T).then_inc(T.sem["s" + e], 1)
    g.wait_ge(T.sem.ls, sent)
    for i, o in enumerate(ops):
        if "dma" in o and o["name"].startswith("st"):
            g.sync.wait_ge(T.sem[o["dma"]], 16)
    for e in "VSPG":
        g.sync.wait_ge(T.sem["s" + e], max(c for i, c in m["num"].items() if ops[i]["on"] == e))
